import numpy as np, ml_dtypes
CORES = [16,17,18,19,32,33,34,35]
N = 8
import mx_ref
BF = ml_dtypes.bfloat16
def gentries(a):
    return np.ascontiguousarray(a.reshape(8, 16, -1).transpose(0, 2, 1)).reshape(8, -1)
def gtable(e):
    e = np.asarray(e); return np.ascontiguousarray(e.reshape(8, -1, 16).transpose(0, 2, 1)).reshape(128, -1).astype(np.int32)
def gcols(t, e):
    v = np.concatenate([t.reshape(8, 16, -1, 4), np.zeros((8, 16, 1, 4), BF)], axis=2)
    return np.ascontiguousarray(np.stack([v[g][:, e[g]] for g in range(8)])).reshape(128, -1)
def tile(rs):
    return np.stack(rs, axis=2).reshape(128, -1).astype(BF)
def cut(t, i, w=512):
    return t[:, w * i:w * i + w]
def pick(q, e):
    c = np.concatenate([q[0].reshape(128, -1, 4), np.zeros((128, 1, 4), np.uint8)], axis=1); s = np.concatenate([q[1], np.ones((16, 1), np.uint8)], axis=1)
    return (np.ascontiguousarray(c[:, e].reshape(128, -1)), np.ascontiguousarray(s[:, e]))
def join(*qs):
    return (np.concatenate([q[0] for q in qs], axis=1), np.concatenate([q[1] for q in qs], axis=1))
def put(q, e, v):
    c, s = q[0].reshape(128, -1, 4).copy(), q[1].copy(); c[:, e] = v[0].reshape(128, -1, 4); s[:, e] = v[1]
    return (c.reshape(128, -1), s)
def pk(c, s):
    return (np.ascontiguousarray(c), mx_ref.live(s))
def emit(q):
    return q[0], q[1]
def packed(v, rng):
    q = [mx_ref.quantize(np.ascontiguousarray(v[r])) for r in range(N)]
    return np.stack([a for a, b in q]), np.stack([mx_ref.plane(b, rng) for a, b in q])
def values_of_codes():
    e, c = np.zeros((128, 128, 4), np.float32), np.zeros((128, 2, 4), np.uint8)
    e[np.arange(128), np.arange(128), 0] = 1
    c[:127, :, 0] = np.arange(256).reshape(2, 128).T[:127]
    return mx_ref.matmul(mx_ref.quantize(e.reshape(128, 512).astype(BF)), (c.reshape(128, 8), np.full((16, 2), 127, np.uint8))).T.reshape(-1).astype(np.float64)
CODE_VALUE, SCALE_VALUE = values_of_codes(), 2.0 ** (np.arange(256) - 127.0)
def decode(q):
    return (CODE_VALUE[q[0]].reshape(16, 8, -1, 4) * SCALE_VALUE[q[1]][:, None, :, None] + 0.0).reshape(128, -1).astype(np.float32)
def f(rng, *shape):
    return mx_ref.flush((rng.standard_normal(shape, dtype=np.float32) * np.exp2(rng.integers(-2, 3, shape[:-1] + (1,)))).astype(BF))
def wide(rng, *shape, cols=0):
    v = rng.standard_normal(shape, dtype=np.float32) * np.exp2(rng.integers(-12, 13, shape)).astype(np.float32)
    if cols: v *= np.repeat(np.exp2(rng.integers(-cols, cols + 1, shape[:-2] + (1, shape[-1] // 4))) * (rng.random(shape[:-2] + (1, shape[-1] // 4)) > 0.0625), 4, axis=-1).astype(np.float32)
    return mx_ref.flush(v.astype(BF))
C, K, R = 512, 256, 3
def living(z):
    return np.sort(np.argsort(-(z[::16] + np.float32(0.0)), axis=1, kind="stable")[:, :K], axis=1)
def ancestors(p, e, alive):
    to = np.where(alive, np.arange(C), p)
    for k in range(9): to = np.take_along_axis(to, to, axis=1)
    a = np.take_along_axis(to, np.take_along_axis(p, e, axis=1), axis=1)
    return np.where(np.take_along_axis(alive, a, axis=1), a, e)
def cleared(v):
    v = v.astype(np.float32)
    v[np.abs(v) < np.float32(2.0 ** -16)] = 0
    return v.astype(BF)
def pointers(rng):
    w = 2 ** rng.integers(1, 10, (N, 8, 1))
    back = rng.integers(1, w + 1, (N, 8, C))
    back[rng.random((N, 8, C)) < 0.03125] = 0
    e = np.maximum(np.arange(C) - back, 0)
    return np.stack([gtable(e[r]) for r in range(N)])
def numbers_of(rng):
    return {"x": cleared(f(rng, N, 128, 4 * C)), "ptr": pointers(rng), "u": np.array(f(rng, N, 128, 512))}
def weights(rng, w):
    c, p = packed(w, rng)
    return {"wc": c, "ws": p}
def still(rng, gs=(), hs=()):
    w = np.zeros((N, 128, 4, 128, 4), np.float32)
    i = np.arange(128)
    for b in range(4): w[:, i, b, i, b] = 32
    for g in gs:
        w[:, 16 * g, 0, 16 * g, 0] = 128
        w[:, 16 * g + 2, 0, 16 * g + 2, 0] = 0
    for g in hs: w[:, 16 * g + 4, 0, 16 * g + 4, 0] = 36
    return weights(rng, w.reshape(N, 128, 2048).astype(BF))
def signs(rng):
    return np.stack([rng.permutation(8) % 2 * 2.0 - 1.0 for r in range(N)]).astype(np.float32)
def setup_inputs(rng):
    return {**numbers_of(rng), **weights(rng, f(rng, N, 128, 2048))}
def setup_inputs_ties(rng):
    d = numbers_of(rng)
    n = rng.permutation(N)
    x = d["x"].reshape(N, 8, 16, C, 4)
    for r in range(N):
        for g in range(8):
            k = np.zeros(C, int) if r == n[0] else rng.permutation(C) % 3
            a = x[r, g, :8, :3].copy()
            a[:, 2] = 0
            x[r, g, :8] = a[:, k]
    x[n[1]] = 0
    u = d["u"].reshape(N, 8, 16, 8, 16, 4)
    b = np.zeros((N, 8, 16, 8, 4), BF)
    for g in range(8): b[:, g, :8, g] = u[:, g, :8, g, 0]
    u[:, :, :, :, 0] = b
    w = f(rng, N, 128, 2048).astype(np.float32).reshape(N, 8, 16, 4, 8, 16, 4)
    w[:, :, 8:, :, :, :8] = 0
    for g in range(8):
        for h in range(8):
            if g != h: w[:, g, :, :, h, :8] = 0
    w[:, :, :, :, :, :8] *= 4
    return {"x": x.reshape(N, 128, 4 * C), "ptr": d["ptr"], "u": u.reshape(N, 128, 512), **weights(rng, w.reshape(N, 128, 2048).astype(BF))}
def setup_inputs_near(rng):
    d = numbers_of(rng)
    x = d["x"].astype(np.float32).reshape(N, 8, 16, C, 4)
    s = (np.arange(C) // 2 + rng.integers(0, C // 4, (N, 8, 1))) % (C // 2)
    g = ((s[..., None] >> np.arange(8)) & 1) * np.exp2(np.arange(8) - 23.0)
    v = np.stack([rng.permutation(8) for r in range(N)])
    k = (v % 2 * 2.0 - 1.0).astype(np.float32)
    size = np.where(v < 4, 1.0, 2.0 ** -30).astype(np.float32)
    x[:, :, 0] = 0
    x[:, :, 0, :, 0] = 1
    for r in rng.permutation(N)[:N // 2]:
        for h in range(8):
            x[r, h, 0, rng.choice(np.flatnonzero(s[r, h] == C // 2 - 1)), 0] = k[r, h] * 2.0 ** 30
            x[r, h, 0, rng.choice(np.flatnonzero(s[r, h] == 0)), 0] = k[r, h] * -2.0 ** 30
    x[:, :, 8] = g[..., :4]
    x[:, :, 9] = g[..., 4:]
    x[:, :, 10:] = rng.integers(4, 8, (N, 8, 6, C, 4)) * rng.choice([-1.0, 1.0], (N, 8, 6, C, 4)) * 2.0 ** -20
    u = d["u"].reshape(N, 128, 128, 4)
    u[:, :, ::16] = 0
    for h in range(0, 128, 16):
        c = size[:, h // 16]
        u[:, h, h, 0] = (k[:, h // 16] * c).astype(BF)
        u[:, h + 8:h + 10, h] = c[:, None, None].astype(BF)
    return {"x": x.reshape(N, 128, 4 * C).astype(BF), "ptr": d["ptr"], "u": u.reshape(N, 128, 512), **still(rng)}
def setup_inputs_huge(rng):
    d = numbers_of(rng)
    x = 2.0 ** 30 * (0.6 + 0.4 * rng.random((N, 128, C, 4)))
    c = np.ones((N, C))
    for r in rng.permutation(N)[:N // 4]: c[r, rng.permutation(C) % 3 == 0] = -1
    x *= c[:, None, :, None]
    u = d["u"].reshape(N, 128, 128, 4)
    a = 2.0 ** 30 * (1 - 0.25 * rng.random((N, 128, 8, 4))) * signs(rng)[:, None, :, None]
    u[:, :, ::16] = a.astype(np.float32).astype(BF)
    return {"x": x.astype(np.float32).reshape(N, 128, 4 * C).astype(BF), "ptr": d["ptr"], "u": u.reshape(N, 128, 512), **still(rng)}
def setup_inputs_deep(rng):
    d = numbers_of(rng)
    x = d["x"].reshape(N, 8, 16, C, 4)
    u = d["u"].reshape(N, 8, 16, 8, 16, 4)
    u[:, :, :, :, 0] = 0
    kind = rng.permutation([0, 0, 1, 1, 2, 3, 3, 4])
    e = np.stack([gentries(d["ptr"][r]) for r in range(N)])
    e[:, kind != 2] = np.maximum(np.arange(C) - 1, 0)
    e[:, kind == 4] = np.arange(C)
    step = SCALE_VALUE[mx_ref.quantize(np.full((128, 16), 28.0, np.float32).astype(BF))[1][0, 0]] * 2.0 ** -9
    small = (np.where(np.arange(C) < K + K // 2, 3, 5) * step).astype(np.float32).astype(BF)
    for g in range(8):
        alive = np.arange(C) > K if kind[g] == 0 else np.arange(C) >= K
        a = np.where(alive, 4.0, -4.0).astype(np.float32)
        if kind[g] == 0: a[0] = 8
        if kind[g] == 4: a[K:K + K // 2] = 12
        o = 8 if kind[g] == 4 else 0
        for r in range(N):
            b = np.where(alive, (16.0, 8.0, 0.0, 8.0 - 8.0 * (r % 2), 8.0)[kind[g]], 0.0).astype(np.float32)
            x[r, g, o + r % 2, :, 0] = a.astype(BF)
            x[r, g, o + 1 - r % 2, :, 0] = b.astype(BF)
            u[r, g, o + r % 2, g, 0, 0] = 1
            if kind[g] == 3:
                x[r, g, 2, :, 0] = 0
                if r % 2 == 0:
                    x[r, g, 0, K, 0] = 3
                    x[r, g, 2, K, 0] = 64
                    u[r, g, 2, g, 0, 0] = 1
            if kind[g] == 4:
                x[r, g, :8] = 0
                x[r, g, 3, :, 0] = small
                x[r, g, 4, :, 0] = 28
                u[r, g, 3, g, 0, 0] = 1
    return {"x": x.reshape(N, 128, 4 * C), "ptr": np.stack([gtable(e[r]) for r in range(N)]), "u": u.reshape(N, 128, 512), **still(rng, np.flatnonzero(kind == 3), np.flatnonzero(kind == 4))}
def setup_inputs_spread(rng):
    d = setup_inputs(rng)
    d["x"] = cleared(wide(rng, N, 128, 4 * C, cols=6))
    return d
def check_inputs(d):
    b = []
    for k in ("x", "u"):
        a = np.abs(d[k].astype(np.float32))
        if not (np.isfinite(a).all() and ((a == 0) | (a >= 2.0 ** -30) & (a <= 2.0 ** 30)).all()): b.append("a value of " + k)
    for p in d["ptr"]:
        e = gentries(p)
        if ((e < 0) | (e > np.arange(C))).any():
            b.append("an entry of ptr")
            break
    return b
def reference(x, ptr, u, wc, ws):
    qu = [mx_ref.quantize(u[r]) for r in range(N)]
    lay = [pk(wc[r], ws[r]) for r in range(N)]
    now = [x[r] for r in range(N)]
    point = [gentries(ptr[r]) for r in range(N)]
    for t in range(R):
        blend, sent = [], []
        for r in range(N):
            e = living(mx_ref.matmul(qu[r], mx_ref.quantize(now[r])))
            number = np.full((8, C), -1)
            np.put_along_axis(number, e, np.arange(K)[None, :], axis=1)
            a = ancestors(point[r], e, number >= 0)
            s = ((gcols(now[r], e).astype(np.float32) + gcols(now[r], a).astype(np.float32)) * np.float32(0.5)).astype(BF)
            q = mx_ref.quantize(s)
            h = tile([np.maximum(mx_ref.matmul(pick(lay[r], np.arange(128 * b, 128 * b + 128)), q), np.float32(0.0)) * np.float32(0.03125) for b in range(4)])
            blend.append(s)
            sent.append(mx_ref.quantize(h))
            point[r] = np.concatenate([np.take_along_axis(number, a, axis=1), np.tile(np.arange(K), (8, 1))], axis=1)
        came = decode(join(*sent)).astype(BF)
        for r in range(N): now[r] = np.concatenate([blend[r], cut(came, (r - 1) % N, 4 * K)], axis=1)
    y, pl = np.zeros((N, 128, C), np.float32), np.zeros((N, 8, C), np.float32)
    oc, osc = np.zeros((N, 128, 4 * C), np.uint8), np.zeros((N, 16, C), np.uint8)
    for r in range(N):
        q = mx_ref.quantize(now[r])
        y[r] = mx_ref.matmul(qu[r], q)
        pl[r] = point[r]
        oc[r], osc[r] = emit(q)
    return {"y": y, "pl": pl, "oc": oc, "osc": osc}

@@ -1,0 +1,482 @@
+from concourse.mybir import dt, AluOpType, AxisListType, ActivationFunctionType
+
+C, K, R = 512, 256, 3
+HALF = K // 2
+WIN = K + 16
+A = AluOpType
+AF = ActivationFunctionType
+BIG = 1048576.0
+HOLD = 4096.0
+NSEM, NDSEM = 90, 40
+SKIP = [0, 0, 0, 0, 0, 32, 64, 128]
+F0 = ({1: "g3", 2: "c3 g4", 3: "c4 g5", 4: "c5 g6", 5: "c6", 6: "g7", 7: "c7"}, 6)
+F1 = ({1: "c3 g4", 2: "c4", 3: "g5", 4: "c5 g6", 5: "c6", 6: "g7", 7: "c7"}, 6)
+PLAN0 = ("v0 c5 v1 D0 D1 c1 a0 a1 c0 c2 c3 c7 K0 c6 c4 e0 c10 D3 l8 k1 l6 a3 d2 c8 c9 l4 g6 p0 D5 a4 d6 a5 d7 q0 a6 a7 c11 c14 D8 D9 a8 a9 "
+         "c15 c12 r0 d10 l0 a10 d11 a11 c13 e1 d12 d13 g4 a12 a13 l9 d14 a14 d15 a15 p1 d16 d17 l2 a16 a17 q1 l5 g2 r1 l3 l1 g0 u2 b0 b1 "
+         "s0 l7 u4 m0 u0 g7 s1 n0 u6 m1 g1 x2 x0 g3 u3 x6 x4 u1 u7 n1 g5 w0 u5 x3 x1 x7 x5 w1")
+PLAN1 = ("c0 v0 c3 v1 D1 K0 a1 D0 c1 c6 D3 a2 a3 c7 D4 D5 a4 c4 c5 a5 c2 D6 c12 e0 D7 c8 a6 a7 D8 l4 D9 a8 a9 D10 c9 l8 l0 D11 c14 a10 a11 "
+         "c11 c15 p0 D12 q0 D13 c10 c13 g4 a12 a13 e1 l2 d14 r0 D15 g0 l9 a14 a15 l7 p1 g2 q1 l6 l5 b0 l3 u0 r1 s0 l1 b1 m0 g6 U2 u4 n0 "
+         "u6 g7 s1 x0 x2 m1 x4 x6 g5 u7 n1 w0 u5 x7 g3 x5 g1 u3 u1 x3 x1 w1")
+
+SCRATCH = {}
+
+
+def _sb(name, n, dtype):
+    SCRATCH[name] = ("sbuf", [128, n], dtype)
+
+
+for _t in range(R + 1):
+    _sb("X%d" % _t, 4 * C, "bfloat16")
+    _sb("Q%d" % _t, C, "float8_e4m3fn_x4")
+    _sb("S%d" % _t, C, "uint8")
+for _t in range(R):
+    _sb("LQ%d" % _t, K, "float8_e4m3fn_x4")
+    _sb("LS%d" % _t, K, "uint8")
+for _n, _w in (("U", 512), ("E", 2048), ("H", 1024), ("V", 1024), ("V2", 1024), ("K2", C), ("zer", C), ("junk", C), ("gtb", C + 2),
+               ("geb", C), ("bnd", C), ("cnt", C + 2), ("one", C), ("z", C), ("jk", 16 * WIN), ("val", C), ("Aa", C), ("Au", C)):
+    _sb(_n, _w, "bfloat16")
+for _n, _s, _w in (("QU", "SU", 128), ("QR", "SR", 128), ("WL", "WSL", 512), ("WQ", "WS", 512), ("QE", "SE", 512), ("QH", "SH", K)):
+    _sb(_n, _w, "float8_e4m3fn_x4")
+    _sb(_s, _w, "uint8")
+for _n, _w in (("iot", C), ("t16", C), ("K1", C), ("D", C), ("scJ", C), ("scP", K), ("scB", K), ("va", C),
+               ("rowA", C), ("rowB", C), ("prow0", C), ("prow", C), ("pe", K), ("Br", K),
+               ("ysb", C), ("sm", 32), ("F", 64), ("Tt", 66), ("Tb", 34), ("o", 10 * 34), ("Dt", 4 * 34), ("G2t", 34), ("G3t", 34),
+               ("Tat", 34), ("Sgt", 34), ("nC1", 64), ("nC", 32), ("Msk", 32), ("nl", 16), ("l1", 32), ("l2", 16),
+               ("l4", 16), ("tmp", 64), ("f", 8), ("Kc", 8), ("ec", 16), ("e2", 16), ("nb", 16), ("et", 16)):
+    _sb(_n, _w, "float32")
+for _n, _w in (("L0", 32), ("LJ", 7 * 32), ("Lna", 3 * 16), ("el", 5 * 16), ("pel", 16), ("offU", 8)):
+    _sb(_n, _w, "uint16")
+for _n, _w in (("pt", 32), ("pi", 4), ("oi", 8)):
+    _sb(_n, _w, "int32")
+for _b in range(8):
+    SCRATCH["P%d" % _b] = ("psum", [128, 512], "float32")
+
+SEMAPHORES = (["c%d" % i for i in range(NSEM)] + ["d%d" % i for i in range(NDSEM)] + ["sent", "warr"]
+              + ["arr%d%d" % (t, h) for t in range(R) for h in range(2)])
+
+
+def _clash(a, b):
+    return a == b or a.startswith(b + ".") or b.startswith(a + ".")
+
+
+def _emit(g, T, ops):
+    queues = {"v": g.vector, "s": g.scalar, "t": g.tensor, "y": g.sync, "g": g}
+    known, seen, waits, needed = [], {q: set() for q in queues}, [], set()
+    for i, (q, fn, rd, wr, ext, dma) in enumerate(ops):
+        deps = []
+        for j in range(i - 1, -1, -1):
+            if j in seen[q] or ops[j][1] is None or ops[j][5] == "remote":
+                continue
+            qj, rj, wj = ops[j][0], ops[j][2], ops[j][3]
+            hit = any(_clash(a, b) for a in rd + wr for b in wj) or any(_clash(a, b) for a in wr for b in rj)
+            if not hit and qj != q:
+                hit = any(a == b and a.startswith("P") for a in rd for b in rj)
+            if hit:
+                deps.append(j)
+                seen[q] |= known[j] | {j}
+        known.append(set(seen[q]))
+        waits.append(deps)
+        needed.update(deps)
+    last, count, mark = {}, {}, {}
+    for i, (q, fn, rd, wr, ext, dma) in enumerate(ops):
+        for j in waits[i]:
+            queues[q].wait_ge(T.sem[mark[j][0]], mark[j][1])
+        if ext is not None:
+            queues[q].wait_ge(T.sem[ext[0]], ext[1])
+        if fn is None:
+            continue
+        ins = fn()
+        if i in needed:
+            pool = ["d%d" % k for k in range(NDSEM)] if dma else ["c%d" % k for k in range(NSEM)]
+            name = [s for s in pool if s not in last or last[s] in known[i]][0]
+            step = 16 if dma else 1
+            last[name] = i
+            count[name] = count.get(name, 0) + step
+            mark[i] = (name, count[name])
+            ins.then_inc(T.sem[name], step)
+
+
+def rank_program(g, core, T, topo):
+    rank = T.rank_of(core)
+    if rank is None:
+        return
+    n = len(T.cores)
+    nxt, prv = T.cores[(rank + 1) % n], T.cores[(rank - 1) % n]
+    assert topo.may_write(core, nxt)
+    rid, pid = topo.addr(nxt)[0], topo.addr(nxt)[1]
+    mask, n_out, n_in = topo.mask(core, nxt), len(topo.engines(core, nxt)), len(topo.engines(prv, core))
+    ops, sent = [], [0]
+    V, S = g.vector, g.scalar
+    u8, u32 = dt.uint8, dt.uint32
+
+    def op(q, fn, rd, wr, ext=None, dma=False):
+        ops.append((q, fn, list(rd), list(wr), ext, dma))
+
+    def ts(out, in0, s1, op0, rd, wr, s2=None, op1=None):
+        if op1 is None:
+            op("v", lambda: V.tensor_scalar(out, in0, s1, None, op0), rd, wr)
+        else:
+            op("v", lambda: V.tensor_scalar(out, in0, s1, s2, op0, op1), rd, wr)
+
+    def tt(out, a, b, o, rd, wr):
+        op("v", lambda: V.tensor_tensor(out, a, b, o), rd, wr)
+
+    def scan(out, d0, d1, init, op0, op1, rd, wr):
+        op("v", lambda: V.tensor_tensor_scan(out, d0, d1, init, op0, op1), rd, wr)
+
+    def cp(out, in_, rd, wr):
+        op("v", lambda: V.tensor_copy(out, in_), rd, wr)
+
+    def fill(ap, c, wr):
+        op("v", lambda: V.memset(ap, c), [], wr)
+
+    def act(out, in_, func, rd, wr, **kw):
+        op("s", lambda: S.activation(out, in_, func, **kw), rd, wr)
+
+    def gather(out, win, lst, rd, wr, func=AF.Copy, **kw):
+        act(out, win.indirect(lst), func, rd, wr, **kw)
+
+    def quant(q, s, x, rd, wr):
+        op("v", lambda: V.quantize_mx(q, s, x), rd, wr)
+
+    def mm(bank, w, ws, x, xs, cols, rd, ext=None):
+        op("t", lambda: g.tensor.matmul_mx(T[bank][:, 0:cols], w, ws, x, xs, True, True), rd, [bank], ext)
+
+    def dma(q, out, in_, rd, wr):
+        eng = g.sync if q == "y" else g.scalar
+        op(q, lambda: eng.dma_start(out, in_), rd, wr, None, True)
+
+    def iota(out, pattern, base, cm, wr, flt=True):
+        if flt:
+            op("g", lambda: g.iota(out, pattern, base, cm, allow_small_or_imprecise_dtypes=True), [], wr)
+        else:
+            op("g", lambda: g.iota(out, pattern, base, cm), [], wr)
+
+    def send(dst, src, sem, rd):
+        op("g", lambda: g.remote_dma(dst, src, T.sem[sem], T.sem.sent, pid, rid, mask), rd, [], None, "remote")
+        sent[0] += n_out
+
+    def col(name, j):
+        return T[name][:, j:j + 1]
+
+    r_, r8, hf, off = col("sm", 0), col("sm", 1), col("sm", 2), col("sm", 3)
+    tau1, c1, m1 = col("sm", 4), col("sm", 5), col("tmp", 39)
+
+    def jumps(w, row0, key0, lst0, lkey0):
+        rows = [(row0, key0)] + [((T.rowA, "rowA"), (T.rowB, "rowB"))[k % 2] for k in range(7)]
+        lists = [(lambda a, b: lst0[0][:, lst0[1] + a // 16:lst0[1] + b // 16], lkey0)]
+        lists += [(lambda a, b, k=k: T.LJ[:, 32 * k + a // 16:32 * k + b // 16], "LJ.%d" % k) for k in range(7)]
+
+        def jg(k):
+            a = SKIP[k] if k == 7 else 0
+            gather(rows[k][0][:, a:w], rows[k - 1][0][:, 0:w], lists[k - 1][0](a, w), [rows[k - 1][1], lists[k - 1][1]], [rows[k][1]])
+
+        def jc(k):
+            a = SKIP[k] if k >= 6 else 0
+            scan(T.scJ[:, a:w], T.K1[:, a:w], rows[k][0][:, a:w], 0.0, A.add, A.min, ["K1", rows[k][1]], ["scJ"])
+            ts(lists[k][0](a, w), T.scJ[:, a + 15:w:16], off, A.add, ["scJ", "sm.off"], [lists[k][1]])
+        return jg, jc, lists
+
+    dma("y", T.pt[:], T.ptr[:], [], ["pt"])
+    dma("s", T.U[:], T.u[:], [], ["U"])
+    dma("y", T.X0[:, 0:1024], T.x[:, 0:1024], [], ["X0.lo"])
+    dma("s", T.X0[:, 1024:2048], T.x[:, 1024:2048], [], ["X0.hi"])
+    dma("y", T.WL[:].bitcast(u8), T.wc[:], [], ["WL"])
+    dma("y", T.WSL[:], T.ws[:], [], ["WSL"])
+
+    iota(T.pi[:, 0:1], [[1, 1]], 0, 1, ["pi.0"], False)
+    iota(T.t16[:], [[0, C // 16], [1, 16]], 0, 0, ["t16"])
+    iota(T.iot[:], [[1, C]], 0, 0, ["iot"])
+    iota(T.oi[:], [[16, 8]], 0, 0, ["oi"], False)
+    fill(T.one[:], 1.0, ["one"])
+    ts(T.pi[:, 1:2], T.pi[:, 0:1], 15, A.bitwise_and, ["pi.0"], ["pi.1"])
+    ts(T.pi[:, 2:3], T.pi[:, 0:1], 7, A.bitwise_and, ["pi.0"], ["pi.2"])
+    ts(T.pi[:, 3:4], T.pi[:, 0:1], 16, A.bitwise_and, ["pi.0"], ["pi.3"])
+    fill(T.zer[:], 0.0, ["zer"])
+    cp(T.sm[:, 0:3], T.pi[:, 1:4], ["pi"], ["sm.r"])
+    for nm in ("G2t", "G3t", "Tat", "Sgt"):
+        fill(T[nm][:], 1.0, [nm])
+    fill(T.Tt[:], 0.0, ["Tt"])
+    fill(T.Tb[:], 0.0, ["Tb"])
+    ts(T.K2[:], T.t16[:], r_, A.is_equal, ["t16", "sm.r"], ["K2"], BIG, A.mult)
+    act(T.K1[:], T.K2[:], AF.Identity, ["K2"], ["K1"], bias=-HOLD)
+    ts(off, r_, -HOLD, A.mult, ["sm.r"], ["sm.off"], 15 * HOLD, A.add)
+    fill(T.Dt[:], 0.0, ["Dt"])
+    fill(T.gtb[:, C:C + 2], 0.0, ["gtb.pad"])
+    fill(T.cnt[:, 0:1], 0.0, ["cnt.pad"])
+    fill(col("Tat", 32), -1.5, ["Tat"])
+    cp(T.L0[:], T.pt[:], ["pt"], ["L0"])
+    gather(T.prow0[:], T.iot[:], T.L0[:], ["iot", "L0"], ["prow0"])
+    jg, jc, lists = jumps(C, T.prow0, "prow0", (T.L0, 0), "L0")
+    jg(1)
+    ts(col("sm", 6), r_, 7.5, A.is_gt, ["sm.r"], ["sm.6"], 2.0, A.mult)
+    ts(col("sm", 7), r_, 0.25, A.mult, ["sm.r"], ["sm.7"], 0.25, A.add)
+    ts(col("sm", 8), r_, 0.125, A.mult, ["sm.r"], ["sm.8"], 1.125, A.add)
+    ts(col("sm", 9), r_, 8.0, A.not_equal, ["sm.r"], ["sm.9"], -BIG, A.mult)
+    ts(col("sm", 10), r_, 6.5, A.is_gt, ["sm.r"], ["sm.10"], 0.125, A.mult)
+    fill(col("sm", 13), 0.125, ["sm.13"])
+    unit = 2.0 ** -20
+    for j, step in enumerate((4624, 272, 16)):
+        ts(col("Kc", j), r_, 1.0, A.add, ["sm.r"], ["Kc.%d" % j], step * unit, A.mult)
+    ts(col("Kc", 3), r_, 0.5, A.add, ["sm.r"], ["Kc.3"], unit, A.mult)
+    ts(col("Kc", 4), r_, 1.0, A.add, ["sm.r"], ["Kc.4"], 78608 * unit, A.mult)
+    ts(col("Kc", 5), r_, 1.0, A.add, ["sm.r"], ["Kc.5"], unit, A.mult)
+    ts(tau1, col("sm", 6), -1.0, A.add, ["sm.6"], ["sm.tau1"])
+    ts(c1, col("sm", 6), -1.5, A.mult, ["sm.6"], ["sm.c1"], 1.5, A.add)
+    ts(col("G3t", 32), col("sm", 8), col("sm", 7), A.max, ["sm.7", "sm.8"], ["G3t"])
+    ts(col("sm", 12), col("sm", 10), 0.125, A.add, ["sm.10"], ["sm.12"])
+    ts(T.tmp[:, 0:16], T.iot[:, 0:16], r_, A.is_le, ["iot", "sm.r"], ["tmp.a"], 4.0, A.mult)
+    ts(T.tmp[:, 16:24], T.iot[:, 0:8], r8, A.is_le, ["iot", "sm.r"], ["tmp.b"], 2.0 ** 25, A.mult)
+    ts(T.l1[:], T.iot[:, 0:32], 15.5, A.is_gt, ["iot"], ["l1"], 16.0, A.mult)
+    ts(T.l2[:], T.iot[:, 0:16], 16.0, A.mult, ["iot", "sm.r"], ["l2"], r_, A.add)
+    cp(T.offU[:], T.oi[:], ["oi"], ["offU"])
+    ts(T.tmp[:, 0:16], T.tmp[:, 0:16], 1.0, A.max, ["tmp.a"], ["tmp.a"])
+    ts(T.tmp[:, 16:24], T.tmp[:, 16:24], 1.0, A.max, ["tmp.b"], ["tmp.b"])
+    ts(T.Msk[:], T.l1[:], hf, A.not_equal, ["l1", "sm.r"], ["Msk"], -BIG, A.mult)
+    quant(T.QU[:], T.SU[:], T.U[:], ["U"], ["QU"])
+    op("v", lambda: V.tensor_reduce(col("G2t", 32), T.tmp[:, 0:16], AxisListType.X, A.mult), ["tmp.a"], ["G2t"])
+    scan(T.tmp[:, 32:40], T.tmp[:, 16:24], T.zer[:, 0:8], 2.0 ** -125, A.mult, A.add, ["tmp.b", "zer"], ["tmp.m"])
+    ts(T.nC1[:, 0:32], T.Msk[:], c1, A.add, ["Msk", "sm.c1"], ["nC1.a"])
+    ts(T.nC1[:, 32:64], T.Msk[:], c1, A.add, ["Msk", "sm.c1", "sm.9"], ["nC1.b"], col("sm", 9), A.add)
+    cp(T.QR[:].bitcast(u32), T.QU[:].bitcast(u32).indirect(T.offU[:]), ["QU", "offU"], ["QR.c"])
+    jc(1)
+    jg(2)
+    cp(T.SR[:], T.SU[:].indirect(T.offU[:]), ["QU", "offU"], ["QR.s"])
+    quant(T.Q0[:, 0:K], T.S0[:, 0:K], T.X0[:, 0:1024], ["X0.lo"], ["Q0.lo"])
+    quant(T.Q0[:, K:C], T.S0[:, K:C], T.X0[:, 1024:2048], ["X0.hi"], ["Q0.hi"])
+    jc(2)
+    ts(T.nl[:], T.l2[:], off, A.subtract, ["l2", "sm.off"], ["nl"])
+    ts(T.nb[:], T.l2[:], 1024.0, A.mult, ["l2"], ["nb"], 512.0, A.add)
+    ts(T.et[:], T.iot[:, 0:16], 32.0, A.mult, ["iot"], ["et"], float(WIN), A.add)
+    for b in range(4):
+        op("g", lambda b=b: g.affine_select(T.E[:, C * b:C * b + C], T.one[:], [[1, C]], A.is_equal, 0.0, -b, -4), ["one"], ["E.%d" % b])
+    send(T.WQ[:].bitcast(u8), T.WL[:].bitcast(u8), "warr", ["WL"])
+    send(T.WS[:], T.WSL[:], "warr", ["WSL"])
+
+    def oc(s, j):
+        return col("o", 34 * s + j)
+
+    def select(t, fills, dstep):
+        Q, Sx, qk = T["Q%d" % t], T["S%d" % t], "Q%d" % t
+        mm("P0", T.QR[:], T.SR[:], Q[:], Sx[:], C, ["QR", qk])
+        mm("P1", T.QR[:], T.SR[:], Q[:], Sx[:], C, ["QR", qk])
+        tau, w = oc(0, 31), oc(9, 31)
+
+        def count(s, bias, bk, scale, sk):
+            fk = "f.%d" % s
+            if s < 8:
+                act(T.junk[:], T.P0[:], AF.Sign, ["P0"] + bk + sk, ["junk", fk], bias=bias, scale=scale, accum_out=col("f", s - 1))
+            else:
+                act(T.junk[:], T.D[:], AF.Sign, ["D"] + bk, ["junk", fk], bias=bias, accum_out=col("f", s - 1))
+            for fn in fills.get(s, []):
+                fn()
+
+        def flag(s, blk, cap, ck, m, mk):
+            ts(T.F[:, 32 * blk:32 * blk + 32], cap, col("f", s - 1), A.is_ge, ck + ["f.%d" % s] + mk, ["F.%d" % blk], m, A.mult)
+
+        def turn(two):
+            if two:
+                op("v", lambda: V.transpose(T.Tt[:, 0:64], T.F[:]), ["F"], ["Tt"])
+            else:
+                op("v", lambda: V.transpose(T.Tb[:, 0:32], T.F[:, 0:32]), ["F.0"], ["Tb"])
+
+        def osl(s, k):
+            return T.o[:, 34 * s:34 * s + k]
+
+        count(1, m1, ["tmp.m"], tau1, ["sm.tau1"])
+        flag(1, 0, T.nC1[:, 0:32], ["nC1.a"], m1, ["tmp.m"])
+        flag(1, 1, T.nC1[:, 32:64], ["nC1.b"], 2.0, [])
+        turn(True)
+        scan(osl(1, 33), T.Tt[:, 0:33], T.G2t[:, 0:33], 0.0, A.max, A.mult, ["Tt", "G2t"], ["o.1"])
+        scan(osl(0, 33), T.Tt[:, 32:65], T.Tat[:, 0:33], -1.0, A.add, A.mult, ["Tt", "Tat"], ["o.0"])
+        ts(T.nC[:], T.Msk[:], oc(0, 32), A.add, ["Msk", "o.0"], ["nC"])
+        ts(col("Sgt", 32), tau, -1.0, A.mult, ["o.0"], ["Sgt"])
+        count(2, oc(1, 32), ["o.1"], tau, ["o.0"])
+        flag(2, 0, T.nC[:], ["nC"], oc(1, 32), ["o.1"])
+        turn(False)
+        scan(osl(2, 33), T.Tb[:, 0:33], T.G3t[:, 0:33], oc(1, 31), A.max, A.mult, ["Tb", "G3t", "o.1"], ["o.2"])
+        ts(T.sm[:, 14:16], T.sm[:, 12:14], oc(2, 31), A.mult, ["sm.12", "sm.13", "o.2"], ["sm.w"])
+        count(3, oc(2, 32), ["o.2"], tau, ["o.0"])
+        flag(3, 0, T.nC[:], ["nC"], oc(2, 32), ["o.2"])
+        flag(3, 1, T.nC[:], ["nC"], col("sm", 14), ["sm.w"])
+        turn(True)
+        scan(osl(3, 32), T.Tt[:, 0:32], T.G2t[:, 0:32], oc(2, 31), A.max, A.mult, ["Tt", "G2t", "o.2"], ["o.3.a"])
+        scan(osl(9, 32), T.Tt[:, 32:64], T.G2t[:, 0:32], col("sm", 15), A.max, A.mult, ["Tt", "G2t", "sm.w"], ["o.9"])
+        ts(oc(3, 33), col("Kc", 4), w, A.mult, ["Kc.4", "o.9", "o.3.a"], ["o.3.m"], oc(3, 31), A.add)
+        ts(col("sm", 16), col("Kc", 5), w, A.mult, ["Kc.5", "o.9"], ["sm.cand"])
+        ts(T.Dt[:, 33:136:34], T.Kc[:, 0:4], w, A.mult, ["Kc", "o.9"], ["Dt.a"])
+        ts(col("Dt", 3 * 34 + 32), oc(3, 31), -1.0, A.mult, ["o.3.a"], ["Dt.b"])
+        for s in range(4, 8):
+            pk = "o.%d" % (s - 1)
+            if s == dstep:
+                ts(T.D[:], T.P1[:], tau, A.mult, ["P1", "o.0", "o.3.a"], ["D"], oc(3, 31), A.add)
+            count(s, oc(s - 1, 33), [pk], tau, ["o.0"])
+            flag(s, 0, T.nC[:], ["nC"], oc(s - 1, 33), [pk])
+            turn(False)
+            scan(osl(s, 34), T.Tb[:], T.Dt[:, 34 * (s - 4):34 * (s - 3)], oc(s - 1, 31), A.max, A.add, ["Tb", "Dt", pk], ["o.%d" % s])
+        ts(col("sm", 17), oc(7, 31), tau, A.mult, ["o.7", "o.0"], ["sm.tl"])
+        ts(T.z[:], T.P1[:], col("sm", 17), A.add, ["P1", "sm.tl"], ["z"])
+        count(8, oc(7, 33), ["o.7"], None, [])
+        flag(8, 0, T.nC[:], ["nC"], col("sm", 16), ["sm.cand"])
+        turn(False)
+        scan(osl(8, 33), T.Tb[:, 0:33], T.Sgt[:, 0:33], 0.0, A.max, A.mult, ["Tb", "Sgt"], ["o.8"])
+
+    hs = [(h, HALF * h, HALF * h + HALF, 8 * h, 8 * h + 8) for h in range(2)]
+    for t in range(R):
+        X, Xn, xk, nk = T["X%d" % t], T["X%d" % (t + 1)], "X%d" % t, "X%d" % (t + 1)
+        Qn, Sn, qn = T["Q%d" % (t + 1)], T["S%d" % (t + 1)], "Q%d" % (t + 1)
+        fills, dstep = F0 if t == 0 else F1
+        select(t, {s: [lambda x=x, jg=jg, jc=jc: (jg if x[0] == "g" else jc)(int(x[1])) for x in v.split()] for s, v in fills.items()}, dstep)
+        thr = oc(8, 32)
+        ts(T.gtb[:, 0:C], T.z[:], thr, A.is_gt, ["z", "o.8"], ["gtb.a"], -1024.0, A.mult)
+        ts(T.geb[:], T.z[:], thr, A.is_ge, ["z", "o.8"], ["geb"], 1024.0, A.mult)
+        scan(T.bnd[:, ::-1], T.gtb[:, C:0:-1], T.zer[:], 1024.0 * K, A.add, A.add, ["gtb", "zer"], ["bnd"])
+        scan(T.cnt[:, 1:C + 1], T.geb[:], T.bnd[:], 0.0, A.add, A.min, ["geb", "bnd"], ["cnt.a"])
+        w = C if t == 0 else K
+        order = [(7, 128)] + ([(7, K)] if t == 0 else []) + [(k, SKIP[k]) for k in range(6, -1, -1)]
+        bufs = [((T.val, "val"), (T.Aa, "Aa"))[k % 2] for k in range(len(order) + 1)]
+        pw, pk = (T.prow0[:], "prow0") if t == 0 else (T.prow[:], "prow")
+        LQ, LS, lk = T["LQ%d" % t], T["LS%d" % t], "Lna.%d" % t
+
+        def work(name):
+            kind, i = name[0].lower(), int(name[1:])
+            h, e = i % 2, i // 2
+            a, b, c, d = hs[h][1:]
+            lna = T.Lna[:, 16 * t + c:16 * t + d]
+
+            def copy(out, in_, rd, wr):
+                if name[0] == kind:
+                    act(out, in_, AF.Copy, rd, wr)
+                else:
+                    cp(out, in_, rd, wr)
+            if kind == "v":
+                if i == 0:
+                    ts(T.va[:, 0:w], T.cnt[:, 1:w + 1], 1025.0 / 1024, A.mult, ["cnt"], ["va"], -1025.0, A.add)
+                else:
+                    tt(T.val[:, 0:w], T.va[:, 0:w], T.cnt[:, 0:w], A.subtract, ["va", "cnt"], ["val"])
+            elif kind == "k":
+                if i == 0:
+                    copy(T.Aa[:, 0:128], T.val[:, 0:128], ["val.0"], ["Aa.0.k"])
+                else:
+                    copy(T.val[:, 128:K], T.Aa[:, 128:K], ["Aa.0.a"], ["val.0"])
+            elif kind == "a":
+                k, lo = order[e]
+                lo, hi = max(lo, h * w // 2), (h + 1) * w // 2
+                src, dst = bufs[e], bufs[e + 1]
+                tt(dst[0][:, lo:hi], src[0][:, 0:hi].indirect(lists[k][0](lo, hi)), T.Au[:, lo:hi], A.max,
+                   [src[1] if h else src[1] + ".0", lists[k][1], "Au.%d" % h], [dst[1] + ".%d" % h + (".a" if e == 0 else "")])
+            elif kind == "d":
+                lo = order[e - 1][1] if e else 0
+                lo, hi = max(lo, h * w // 2), (h + 1) * w // 2
+                copy(T.Au[:, lo:hi], bufs[e][0][:, lo:hi], [bufs[e][1] + ".%d" % h + (".a" if e == 1 else "")], ["Au.%d" % h])
+            elif kind == "c":
+                act(T.jk[:, WIN * i:WIN * i + WIN], T.cnt[:, 1 + 16 * i:1 + 16 * i + WIN], AF.Sign, ["cnt", "nb"],
+                    ["jk.%d" % i, "ec.%d.%d" % (i // 8, i)], bias=col("nb", i), scale=-1.0, accum_out=col("ec", i))
+            elif kind == "e":
+                tt(T.e2[:, c:d], T.ec[:, c:d], T.et[:, c:d], A.add, ["ec.%d" % h, "et"], ["e2.%d" % h])
+            elif kind == "l":
+                if e == 4:
+                    ts(T.el[:, 64 + c:64 + d], T.e2[:, c:d], 0.5, A.mult, ["e2.%d" % h], ["el.4.%d" % h])
+                else:
+                    ts(T.el[:, 16 * e + c:16 * e + d], T.e2[:, c:d], 2.0, A.mult, ["e2.%d" % h], ["el.%d.%d" % (e, h)], float(e), A.add)
+            elif kind == "p":
+                gather(T.pe[:, a:b], pw, T.el[:, 64 + c:64 + d], [pk, "el.4.%d" % h], ["pe.%d" % h])
+            elif kind == "q":
+                scan(T.scP[:, a:b], T.K1[:, a:b], T.pe[:, a:b], 0.0, A.add, A.min, ["K1", "pe.%d" % h], ["scP.%d" % h])
+            elif kind == "r":
+                ts(T.pel[:, c:d], T.scP[:, a + 15:b:16], off, A.add, ["scP.%d" % h, "sm.off"], ["pel.%d" % h])
+            elif kind == "g":
+                gather(T.V[:, K * e + a:K * e + b], X[:], T.el[:, 16 * e + c:16 * e + d], [xk, "el.%d.%d" % (e, h)], ["V.%d.%d" % (e, h)], scale=0.5)
+            elif kind == "u":
+                copy(T.V2[:, K * e + a:K * e + b], T.V[:, K * e + a:K * e + b], ["V.%d.%d" % (e, h)], ["V2.%d.%d" % (e, h)])
+            elif kind == "b":
+                gather(T.Br[:, a:b], bufs[-1][0][:, 0:w], T.pel[:, c:d], [bufs[-1][1], "pel.%d" % h], ["Br.%d" % h], func=AF.Abs)
+            elif kind == "s":
+                scan(T.scB[:, a:b], T.K1[:, a:b], T.Br[:, a:b], 0.0, A.add, A.min, ["K1", "Br.%d" % h], ["scB.%d" % h])
+            elif kind == "m":
+                tt(T.l4[:, c:d], T.scB[:, a + 15:b:16], T.nl[:, c:d], A.min, ["scB.%d" % h, "nl"], ["l4.%d" % h])
+            elif kind == "n":
+                ts(lna, T.l4[:, c:d], off, A.add, ["l4.%d" % h, "sm.off"], [lk + ".%d" % h])
+            elif kind == "x":
+                tt(Xn[:, 4 * a + e:4 * b:4], T.V[:, K * e:K * e + b].indirect(lna), T.V2[:, K * e + a:K * e + b], A.add,
+                   ["V.%d.%d" % (e, j) for j in range(h + 1)] + ["V2.%d.%d" % (e, h), lk + ".%d" % h], [nk + ".lo.%d.%d" % (h, e)])
+            elif kind == "w":
+                qk = qn + ".lo.%d" % h
+                quant(Qn[:, a:b], Sn[:, a:b], Xn[:, 4 * a:4 * b], [nk + ".lo.%d" % h], [qk])
+                send(LQ[:, a:b].bitcast(u8), Qn[:, a:b].bitcast(u8), "arr%d%d" % (t, h), [qk])
+                send(LS[:, a:b], Sn[:, a:b], "arr%d%d" % (t, h), [qk])
+
+        for name in (PLAN0 if t == 0 else PLAN1).split():
+            work(name)
+        gather(T.prow[:, 0:K], T.iot[:, 0:K], T.Lna[:, 16 * t:16 * t + 16], ["iot", lk], ["prow.lo"])
+        if t == 0:
+            act(T.prow[:, K:C], T.iot[:, 0:K], AF.Copy, ["iot"], ["prow.hi"])
+            quant(T.QE[:], T.SE[:], T.E[:], ["E"], ["QE"])
+        if t < R - 1:
+            jg, jc, lists = jumps(K, T.prow, "prow.lo", (T.Lna, 16 * t), lk)
+            jg(1)
+            jc(1)
+            jg(2)
+            jc(2)
+            jg(3)
+        else:
+            dma("y", T.oc[:, 0:1024], Qn[:, 0:K].bitcast(u8), [qn + ".lo"], ["out.0"])
+            for k in range(4):
+                dma("y", T.osc[4 * k:4 * k + 4, 0:K], Sn[32 * k:32 * k + 4, 0:K], [qn + ".lo"], ["out.1%d" % k])
+            mm("P0", T.QU[:], T.SU[:], Qn[:, 0:K], Sn[:, 0:K], K, ["QU", qn + ".lo"])
+            cp(T.ysb[:, 0:K], T.P0[:, 0:K], ["P0"], ["ysb.lo"])
+            dma("y", T.pl[:], T.prow[0:128:16, :], ["prow"], ["out.2"])
+            dma("y", T.y[:, 0:K], T.ysb[:, 0:K], ["ysb.lo"], ["out.3"])
+        if t == 0:
+            op("t", None, [], [], ("warr", 2 * n_in))
+        banks = ("P6", "P7", "P0", "P1")
+
+        def layer(h):
+            a, b = hs[h][1:3]
+            for e in range(4):
+                mm("P%d" % (2 + e), T.WQ[:, 128 * e:128 * e + 128], T.WS[:, 128 * e:128 * e + 128], LQ[:, a:b], LS[:, a:b], HALF, [],
+                   ("arr%d%d" % (t, h), 2 * n_in) if e == 0 else None)
+
+        def scores(h):
+            a, b = K + hs[h][1], K + hs[h][2]
+            qk = qn + ".hi.%d" % h
+            mm("P6", T.QU[:], T.SU[:], Qn[:, a:b], Sn[:, a:b], HALF, ["QU", qk])
+            dma("y", T.oc[:, 4 * a:4 * b], Qn[:, a:b].bitcast(u8), [qk], ["out.4%d" % h])
+            if h == 1:
+                for k in range(4):
+                    dma("s" if k < 2 else "y", T.osc[4 * k:4 * k + 4, K:C], Sn[32 * k:32 * k + 4, K:C], [qn + ".hi"], ["out.5%d" % k])
+
+        def store(h):
+            a, b = K + hs[h][1], K + hs[h][2]
+            cp(T.ysb[:, a:b], T.P6[:, 0:HALF], ["P6"], ["ysb.hi%d" % h])
+            dma("s" if h else "y", T.y[:, a:b], T.ysb[:, a:b], ["ysb.hi%d" % h], ["out.6%d" % h])
+
+        layer(0)
+        for h, a, b, c, d in hs:
+            for e in range(4):
+                bank = "P%d" % (2 + e)
+                if e % 2:
+                    act(T.H[:, 4 * a + e:4 * b:4], T[bank][:, 0:HALF], AF.Relu, [bank], ["H.%d.%d" % (h, e)], scale=0.03125)
+                else:
+                    ts(T.H[:, 4 * a + e:4 * b:4], T[bank][:, 0:HALF], 0.0, A.max, [bank], ["H.%d.%d" % (h, e)], 0.03125, A.mult)
+            quant(T.QH[:, a:b], T.SH[:, a:b], T.H[:, 4 * a:4 * b], ["H.%d" % h], ["QH.%d" % h])
+            if t == R - 1 and h == 1:
+                store(0)
+            for e in range(4):
+                mm(banks[e], T.QE[:, 128 * e:128 * e + 128], T.SE[:, 128 * e:128 * e + 128], T.QH[:, a:b], T.SH[:, a:b], HALF, ["QE", "QH.%d" % h])
+            if h == 0:
+                layer(1)
+            for e in range(4):
+                dst, key = Xn[:, 4 * (K + a) + e:4 * (K + b):4], nk + ".hi.%d.%d" % (h, e)
+                if e % 2:
+                    act(dst, T[banks[e]][:, 0:HALF], AF.Copy, [banks[e]], [key])
+                else:
+                    cp(dst, T[banks[e]][:, 0:HALF], [banks[e]], [key])
+            quant(Qn[:, K + a:K + b], Sn[:, K + a:K + b], Xn[:, 4 * (K + a):4 * (K + b)], [nk + ".hi.%d" % h], [qn + ".hi.%d" % h])
+            if t == R - 1:
+                scores(h)
+        if t == R - 1:
+            store(1)
+
+    op("g", None, ["out"], [], ("sent", sent[0]))
+    _emit(g, T, ops)

@@ -10,13 +10,14 @@ HOLD = 4096.0
 NSEM, NDSEM = 90, 40
 SKIP = [0, 0, 0, 0, 0, 32, 64, 128]
 F0 = ({1: "g3", 2: "c3 g4", 3: "c4 g5", 4: "c5 g6", 5: "c6", 6: "g7", 7: "c7"}, 6)
-F1 = ({1: "c3 g4", 2: "c4", 3: "g5", 4: "c5 g6", 5: "c6", 6: "g7", 7: "c7"}, 6)
-PLAN0 = ("v0 c5 v1 D0 D1 c1 a0 a1 c0 c2 c3 c7 K0 c6 c4 e0 c10 D3 l8 k1 l6 a3 d2 c8 c9 l4 g6 p0 D5 a4 d6 a5 d7 q0 a6 a7 c11 c14 D8 D9 a8 a9 "
-         "c15 c12 r0 d10 l0 a10 d11 a11 c13 e1 d12 d13 g4 a12 a13 l9 d14 a14 d15 a15 p1 d16 d17 l2 a16 a17 q1 l5 g2 r1 l3 l1 g0 u2 b0 b1 "
-         "s0 l7 u4 m0 u0 g7 s1 n0 u6 m1 g1 x2 x0 g3 u3 x6 x4 u1 u7 n1 g5 w0 u5 x3 x1 x7 x5 w1")
+F1 = ({1: "g3", 2: "c3 g4", 3: "c4", 4: "g5", 5: "c5 g6", 6: "c6 g7", 7: "c7"}, 4)
+PLAN0 = ("v0 c12 c5 c6 c1 v1 c0 c7 c2 c3 D1 D0 c4 K0 a1 c9 a0 c11 D3 e0 K1 a3 l8 D2 D5 a4 a5 c14 c13 p0 d6 d7 l0 l6 c10 a6 a7 d8 q0 d9 a8 "
+         "c15 a9 d10 l4 l2 a10 d11 a11 c8 e1 d12 d13 r0 a12 g6 a13 d14 l9 d15 p1 l1 a14 a15 d16 d17 g1 q1 a16 a17 l5 r1 g2 g4 l7 b0 s0 U2 "
+         "l3 b1 u4 u6 m0 s1 g0 n0 m1 g3 u1 u0 x6 x4 g5 x2 x0 n1 w0 u3 u5 g7 x1 x3 u7 x5 x7 w1")
 PLAN1 = ("c0 v0 c3 v1 D1 K0 a1 D0 c1 c6 D3 a2 a3 c7 D4 D5 a4 c4 c5 a5 c2 D6 c12 e0 D7 c8 a6 a7 D8 l4 D9 a8 a9 D10 c9 l8 l0 D11 c14 a10 a11 "
          "c11 c15 p0 D12 q0 D13 c10 c13 g4 a12 a13 e1 l2 d14 r0 D15 g0 l9 a14 a15 l7 p1 g2 q1 l6 l5 b0 l3 u0 r1 s0 l1 b1 m0 g6 U2 u4 n0 "
          "u6 g7 s1 x0 x2 m1 x4 x6 g5 u7 n1 w0 u5 x7 g3 x5 g1 u3 u1 x3 x1 w1")
+STAGES = "L0 R0 H0 L1 D0 R1 C0 H1 D1 X0 Y0 C1 Z0 X1 Y1 Z1"
 
 SCRATCH = {}
 
@@ -41,8 +42,8 @@ for _n, _s, _w in (("QU", "SU", 128), ("QR", "SR", 128), ("WL", "WSL", 512), ("W
 for _n, _w in (("iot", C), ("t16", C), ("K1", C), ("D", C), ("scJ", C), ("scP", K), ("scB", K), ("va", C),
                ("rowA", C), ("rowB", C), ("prow0", C), ("prow", C), ("pe", K), ("Br", K),
                ("ysb", C), ("sm", 32), ("F", 64), ("Tt", 66), ("Tb", 34), ("o", 10 * 34), ("Dt", 4 * 34), ("G2t", 34), ("G3t", 34),
-               ("Tat", 34), ("Sgt", 34), ("nC1", 64), ("nC", 32), ("Msk", 32), ("nl", 16), ("l1", 32), ("l2", 16),
-               ("l4", 16), ("tmp", 64), ("f", 8), ("Kc", 8), ("ec", 16), ("e2", 16), ("nb", 16), ("et", 16)):
+               ("Tat", 34), ("Sgt", 34), ("nC1", 64), ("nE", 64), ("nC", 32), ("Msk", 32), ("nl", 16), ("l1", 32), ("l2", 16),
+               ("l4", 16), ("tmp", 64), ("f", 10), ("Kc", 8), ("ec", 16), ("e2", 16), ("nb", 16), ("et", 16)):
     _sb(_n, _w, "float32")
 for _n, _w in (("L0", 32), ("LJ", 7 * 32), ("Lna", 3 * 16), ("el", 5 * 16), ("pel", 16), ("offU", 8)):
     _sb(_n, _w, "uint16")
@@ -177,11 +178,18 @@ def rank_program(g, core, T, topo):
             ts(lists[k][0](a, w), T.scJ[:, a + 15:w:16], off, A.add, ["scJ", "sm.off"], [lists[k][1]])
         return jg, jc, lists
 
+    def early(t):
+        mm("P7", T.QR[:], T.SR[:], T["Q%d" % t][:, 0:K], T["S%d" % t][:, 0:K], K, ["QR", "Q%d.lo" % t])
+        act(T.junk[:, 0:K], T.P7[:, 0:K], AF.Sign, ["P7", "tmp.m", "sm.tau1"], ["junk", "f.9"], bias=m1, scale=tau1, accum_out=col("f", 8))
+
+    def early2():
+        ts(T.nE[:], T.nC1[:], col("f", 8), A.subtract, ["nC1", "f.9"], ["nE"])
+
     dma("y", T.pt[:], T.ptr[:], [], ["pt"])
     dma("s", T.U[:], T.u[:], [], ["U"])
     dma("y", T.X0[:, 0:1024], T.x[:, 0:1024], [], ["X0.lo"])
     dma("s", T.X0[:, 1024:2048], T.x[:, 1024:2048], [], ["X0.hi"])
-    dma("y", T.WL[:].bitcast(u8), T.wc[:], [], ["WL"])
+    dma("y", T.WL[:].bitcast(u8), T.wc[:], ["X0"], ["WL"])
     dma("y", T.WSL[:], T.ws[:], [], ["WSL"])
 
     iota(T.pi[:, 0:1], [[1, 1]], 0, 1, ["pi.0"], False)
@@ -243,7 +251,9 @@ def rank_program(g, core, T, topo):
     jg(2)
     cp(T.SR[:], T.SU[:].indirect(T.offU[:]), ["QU", "offU"], ["QR.s"])
     quant(T.Q0[:, 0:K], T.S0[:, 0:K], T.X0[:, 0:1024], ["X0.lo"], ["Q0.lo"])
+    early(0)
     quant(T.Q0[:, K:C], T.S0[:, K:C], T.X0[:, 1024:2048], ["X0.hi"], ["Q0.hi"])
+    early2()
     jc(2)
     ts(T.nl[:], T.l2[:], off, A.subtract, ["l2", "sm.off"], ["nl"])
     ts(T.nb[:], T.l2[:], 1024.0, A.mult, ["l2"], ["nb"], 512.0, A.add)
@@ -258,13 +268,16 @@ def rank_program(g, core, T, topo):
 
     def select(t, fills, dstep):
         Q, Sx, qk = T["Q%d" % t], T["S%d" % t], "Q%d" % t
+        mm("P3", T.QR[:], T.SR[:], Q[:, K:C], Sx[:, K:C], K, ["QR", qk + ".hi"])
         mm("P0", T.QR[:], T.SR[:], Q[:], Sx[:], C, ["QR", qk])
         mm("P1", T.QR[:], T.SR[:], Q[:], Sx[:], C, ["QR", qk])
         tau, w = oc(0, 31), oc(9, 31)
 
         def count(s, bias, bk, scale, sk):
             fk = "f.%d" % s
-            if s < 8:
+            if s == 1:
+                act(T.junk[:, 0:K], T.P3[:, 0:K], AF.Sign, ["P3"] + bk + sk, ["junk", fk], bias=bias, scale=scale, accum_out=col("f", s - 1))
+            elif s < 8:
                 act(T.junk[:], T.P0[:], AF.Sign, ["P0"] + bk + sk, ["junk", fk], bias=bias, scale=scale, accum_out=col("f", s - 1))
             else:
                 act(T.junk[:], T.D[:], AF.Sign, ["D"] + bk, ["junk", fk], bias=bias, accum_out=col("f", s - 1))
@@ -284,8 +297,8 @@ def rank_program(g, core, T, topo):
             return T.o[:, 34 * s:34 * s + k]
 
         count(1, m1, ["tmp.m"], tau1, ["sm.tau1"])
-        flag(1, 0, T.nC1[:, 0:32], ["nC1.a"], m1, ["tmp.m"])
-        flag(1, 1, T.nC1[:, 32:64], ["nC1.b"], 2.0, [])
+        flag(1, 0, T.nE[:, 0:32], ["nE"], m1, ["tmp.m"])
+        flag(1, 1, T.nE[:, 32:64], ["nE"], 2.0, [])
         turn(True)
         scan(osl(1, 33), T.Tt[:, 0:33], T.G2t[:, 0:33], 0.0, A.max, A.mult, ["Tt", "G2t"], ["o.1"])
         scan(osl(0, 33), T.Tt[:, 32:65], T.Tat[:, 0:33], -1.0, A.add, A.mult, ["Tt", "Tat"], ["o.0"])
@@ -415,10 +428,11 @@ def rank_program(g, core, T, topo):
         if t < R - 1:
             jg, jc, lists = jumps(K, T.prow, "prow.lo", (T.Lna, 16 * t), lk)
             jg(1)
+            early(t + 1)
             jc(1)
             jg(2)
+            early2()
             jc(2)
-            jg(3)
         else:
             dma("y", T.oc[:, 0:1024], Qn[:, 0:K].bitcast(u8), [qn + ".lo"], ["out.0"])
             for k in range(4):
@@ -431,52 +445,47 @@ def rank_program(g, core, T, topo):
             op("t", None, [], [], ("warr", 2 * n_in))
         banks = ("P6", "P7", "P0", "P1")
 
-        def layer(h):
+        def stage(name):
+            kind, h = name[0], int(name[1])
             a, b = hs[h][1:3]
-            for e in range(4):
-                mm("P%d" % (2 + e), T.WQ[:, 128 * e:128 * e + 128], T.WS[:, 128 * e:128 * e + 128], LQ[:, a:b], LS[:, a:b], HALF, [],
-                   ("arr%d%d" % (t, h), 2 * n_in) if e == 0 else None)
-
-        def scores(h):
-            a, b = K + hs[h][1], K + hs[h][2]
             qk = qn + ".hi.%d" % h
-            mm("P6", T.QU[:], T.SU[:], Qn[:, a:b], Sn[:, a:b], HALF, ["QU", qk])
-            dma("y", T.oc[:, 4 * a:4 * b], Qn[:, a:b].bitcast(u8), [qk], ["out.4%d" % h])
-            if h == 1:
-                for k in range(4):
-                    dma("s" if k < 2 else "y", T.osc[4 * k:4 * k + 4, K:C], Sn[32 * k:32 * k + 4, K:C], [qn + ".hi"], ["out.5%d" % k])
+            if kind == "L":
+                for e in range(4):
+                    mm("P%d" % (2 + e), T.WQ[:, 128 * e:128 * e + 128], T.WS[:, 128 * e:128 * e + 128], LQ[:, a:b], LS[:, a:b], HALF, [],
+                       ("arr%d%d" % (t, h), 2 * n_in) if e == 0 else None)
+            elif kind == "R":
+                for e in range(4):
+                    bank = "P%d" % (2 + e)
+                    if e % 2:
+                        act(T.H[:, 4 * a + e:4 * b:4], T[bank][:, 0:HALF], AF.Relu, [bank], ["H.%d.%d" % (h, e)], scale=0.03125)
+                    else:
+                        ts(T.H[:, 4 * a + e:4 * b:4], T[bank][:, 0:HALF], 0.0, A.max, [bank], ["H.%d.%d" % (h, e)], 0.03125, A.mult)
+            elif kind == "H":
+                quant(T.QH[:, a:b], T.SH[:, a:b], T.H[:, 4 * a:4 * b], ["H.%d" % h], ["QH.%d" % h])
+            elif kind == "D":
+                for e in range(4):
+                    mm(banks[e], T.QE[:, 128 * e:128 * e + 128], T.SE[:, 128 * e:128 * e + 128], T.QH[:, a:b], T.SH[:, a:b], HALF, ["QE", "QH.%d" % h])
+            elif kind == "C":
+                for e in range(4):
+                    dst, key = Xn[:, 4 * (K + a) + e:4 * (K + b):4], nk + ".hi.%d.%d" % (h, e)
+                    if e % 2:
+                        act(dst, T[banks[e]][:, 0:HALF], AF.Copy, [banks[e]], [key])
+                    else:
+                        cp(dst, T[banks[e]][:, 0:HALF], [banks[e]], [key])
+            elif kind == "X":
+                quant(Qn[:, K + a:K + b], Sn[:, K + a:K + b], Xn[:, 4 * (K + a):4 * (K + b)], [nk + ".hi.%d" % h], [qk])
+            elif t == R - 1 and kind == "Y":
+                mm("P2", T.QU[:], T.SU[:], Qn[:, K + a:K + b], Sn[:, K + a:K + b], HALF, ["QU", qk])
+                dma("y", T.oc[:, 4 * (K + a):4 * (K + b)], Qn[:, K + a:K + b].bitcast(u8), [qk], ["out.4%d" % h])
+                if h == 1:
+                    for k in range(4):
+                        dma("s" if k < 2 else "y", T.osc[4 * k:4 * k + 4, K:C], Sn[32 * k:32 * k + 4, K:C], [qn + ".hi"], ["out.5%d" % k])
+            elif t == R - 1:
+                cp(T.ysb[:, K + a:K + b], T.P2[:, 0:HALF], ["P2"], ["ysb.hi%d" % h])
+                dma("s" if h else "y", T.y[:, K + a:K + b], T.ysb[:, K + a:K + b], ["ysb.hi%d" % h], ["out.6%d" % h])
 
-        def store(h):
-            a, b = K + hs[h][1], K + hs[h][2]
-            cp(T.ysb[:, a:b], T.P6[:, 0:HALF], ["P6"], ["ysb.hi%d" % h])
-            dma("s" if h else "y", T.y[:, a:b], T.ysb[:, a:b], ["ysb.hi%d" % h], ["out.6%d" % h])
-
-        layer(0)
-        for h, a, b, c, d in hs:
-            for e in range(4):
-                bank = "P%d" % (2 + e)
-                if e % 2:
-                    act(T.H[:, 4 * a + e:4 * b:4], T[bank][:, 0:HALF], AF.Relu, [bank], ["H.%d.%d" % (h, e)], scale=0.03125)
-                else:
-                    ts(T.H[:, 4 * a + e:4 * b:4], T[bank][:, 0:HALF], 0.0, A.max, [bank], ["H.%d.%d" % (h, e)], 0.03125, A.mult)
-            quant(T.QH[:, a:b], T.SH[:, a:b], T.H[:, 4 * a:4 * b], ["H.%d" % h], ["QH.%d" % h])
-            if t == R - 1 and h == 1:
-                store(0)
-            for e in range(4):
-                mm(banks[e], T.QE[:, 128 * e:128 * e + 128], T.SE[:, 128 * e:128 * e + 128], T.QH[:, a:b], T.SH[:, a:b], HALF, ["QE", "QH.%d" % h])
-            if h == 0:
-                layer(1)
-            for e in range(4):
-                dst, key = Xn[:, 4 * (K + a) + e:4 * (K + b):4], nk + ".hi.%d.%d" % (h, e)
-                if e % 2:
-                    act(dst, T[banks[e]][:, 0:HALF], AF.Copy, [banks[e]], [key])
-                else:
-                    cp(dst, T[banks[e]][:, 0:HALF], [banks[e]], [key])
-            quant(Qn[:, K + a:K + b], Sn[:, K + a:K + b], Xn[:, 4 * (K + a):4 * (K + b)], [nk + ".hi.%d" % h], [qn + ".hi.%d" % h])
-            if t == R - 1:
-                scores(h)
-        if t == R - 1:
-            store(1)
+        for name in STAGES.split():
+            stage(name)
 
     op("g", None, ["out"], [], ("sent", sent[0]))
     _emit(g, T, ops)

@@ -2,24 +2,29 @@ from concourse.mybir import dt, AluOpType, AxisListType, ActivationFunctionType
 
 C, K, R = 512, 256, 3
 HALF = K // 2
-WIN = K + 16
+WIN = HALF + 8
+PAD = 16
+ROW = C + PAD
+KB = 6
+LONG_FIRST = True
 A = AluOpType
 AF = ActivationFunctionType
 BIG = 1048576.0
+HUGE = 1e29
 HOLD = 4096.0
-NSEM, NDSEM = 90, 40
-SKIP = [0, 0, 0, 0, 0, 32, 64, 128]
-F0 = ({1: "g3", 2: "c3 g4", 3: "c4 g5", 4: "c5 g6", 5: "c6", 6: "g7", 7: "c7"}, 6)
-F1 = ({1: "g3", 2: "c3 g4", 3: "c4", 4: "g5", 5: "c5 g6", 6: "c6 g7", 7: "c7"}, 4)
-PLAN0 = ("v0 c12 c5 c6 c1 v1 c0 c7 c2 c3 D1 D0 c4 K0 a1 c9 a0 c11 D3 e0 K1 a3 l8 D2 D5 a4 a5 c14 c13 p0 d6 d7 l0 l6 c10 a6 a7 d8 q0 d9 a8 "
-         "c15 a9 d10 l4 l2 a10 d11 a11 c8 e1 d12 d13 r0 a12 g6 a13 d14 l9 d15 p1 l1 a14 a15 d16 d17 g1 q1 a16 a17 l5 r1 g2 g4 l7 b0 s0 U2 "
-         "l3 b1 u4 u6 m0 s1 g0 n0 m1 g3 u1 u0 x6 x4 g5 x2 x0 n1 w0 u3 u5 g7 x1 x3 u7 x5 x7 w1")
-PLAN1 = ("c0 v0 c3 v1 D1 K0 a1 D0 c1 c6 D3 a2 a3 c7 D4 D5 a4 c4 c5 a5 c2 D6 c12 e0 D7 c8 a6 a7 D8 l4 D9 a8 a9 D10 c9 l8 l0 D11 c14 a10 a11 "
-         "c11 c15 p0 D12 q0 D13 c10 c13 g4 a12 a13 e1 l2 d14 r0 D15 g0 l9 a14 a15 l7 p1 g2 q1 l6 l5 b0 l3 u0 r1 s0 l1 b1 m0 g6 U2 u4 n0 "
-         "u6 g7 s1 x0 x2 m1 x4 x6 g5 u7 n1 w0 u5 x7 g3 x5 g1 u3 u1 x3 x1 w1")
-STAGES = "L0 R0 H0 L1 D0 R1 C0 H1 D1 X0 Y0 C1 Z0 X1 Y1 Z1"
+UNIT = 1024.0
+NSEM, NDSEM = 112, 30
+ORDER = """
+k39 i1 k0 k1 k37 k43 k14 k6 k3 k7 k13 k69 k5 k12 k15 k60 k50 k16 k34 k68 k66 k2 k28 k8 i0 k17 k33 k31 k67 k63 k23:g i2 k9 i3 k38:g k57 k32 k35:g k42:g k22 k18 k30:g k70 u1 k61 k4 u0 k71 k27:g k20 k36 u3:s k49 p0 i5 k62 k51 k58 i4 k40:g k75 p1 p2 w3 w0 k77 k10 k76 u4 p3 u2 k73 0y0 0h0 k19 k52 k81 k59 k72 u5 k78 k25 k74 k65 0s0 k56 k48 k54 p4 0y1 k24:g k53 0s3 k64 k55 k79 k21 0j0 k80 0y2 0s5 0s4 0s6 k41:g 0s7 w4 0s8 0s11 0s9 0l0 0s10 0s1 0s13 0s14 k82 0l1 k11:g 0s15 0s16 0s21 0j1:v 0s18 0s22 0s17 0s19 0s23 0s24 0h2:s 0h7:s 0l2 0s27 0h6 0l3 0j2 k44:g k29 0s28 0s29 0h3 0s30 0s2 0s26 0s31 0l4 0s32 k26 0s20 0s33 0l5 0s34 0j3:v 0s35 0s36 0s37 0s25 w1 0s38 0l6 0l7 0h4:s 0s12 k47 0s39 0s40 0h1:s k45 0s41 0j4 0s42 0s44 w2 w6 0s43 0s45 0l8 0s46 0s47 0l9 0j5 w5
+0n0 0n1 0n2 0n3 0l10 0v0 0v2 0l11 0v1 0c0 0c8 0c12 0c3 0c2 0c9 0c11 0c1 0c10 0c15 0b0 0v3 0b1 0b2 0h5 0c6 0b3 0b4 0b5 0b6 k46:g 0d0:g 0a0 0c5 0c4 0c14 0d1:s 0a1 0c7 0e0 0d2:s 0a2 0c13 0d3:s 0a3 0d4:s 0c16 0a4 0e2 0d5:s 0e1 0a5 0d6:s 0p0 0d7:s 0a6 0d8:s 0a7 0e3 0a8 0p1 0g1 0d9:s 0a9 0g3 0d10:s 0a10 0g0 0p2 0d11:s 0p3 0a11 0p4 0p5 0q0 0q1 0q2 0q4 0q5 0q3 0q6 0r0 0x3 0g2 0x0 0q7 0g4 0g5 0g6 0x2 0r1 0x1 0x4 0g7 0w0 0x6 1h0:s 0w2 0x5 1h1:s 1h2:s 0x7 0w3 1y0 0w1 1y1 0r2 0r3 0L0 1j0 1l0 1l1 0L3 1h3:s 0L2 0L1 0R1 0w5 0R0:s 0w4 0L4 0L5 0R3 0L7 0R2 0H0 0L6 0R4 1j1 0D0 1y2 0R5:s 0D1 0R6 0D2 0R7:s 0C0 0C1:s 0C2:s 0H1 0D3 0C3:s 0D4 1l2 0X0 0D5 0D7 0D6 1l3 0C4 1y3 0C5:s 0C6 0C7:s 1h4 0X1
+1h5 1j2 1l4 1y4 1y5 1s0 1s3 1s4 1s5 1l5 1s6 1s2 1s7 1h6:s 1s8 1s9 1j3 1s12 1l6 1s1 1s11 1s13 1s14 1s15 1s16 1s21 1s17 1l7 1j4 1s18 1s19 1s10 1s22 1s23 1s24 1l8 1s25 1l9 1s27 1s28 1s29 1s30 1s31 1j5:v 1h7 1s32 1s33 1s34 1s35 1l10 1s36 1l11 1s37 1s38 1s39 1s20 1s26 1s40 1s41 1s42 1s44 1s43 1s45 1s46 1s47
+1n0 1n1 1n2 1n3 1v0 1c0 1v2 1v1 1c9 1v3 1b0 1b1 1d0 1b2 1a0 1d1 1c14 1c4 1d2 1c10 1a1 1c2 1c8 1c3 1c5 1a2 1c1 1c6 1c7 1d3 1c11 1e0 1d4 1a3 1c13 1a4 1c16 1d5 1c15 1c12 1e1 1d6 1a5 1p0 1a6 1g0 1d7 1e2 1g1 1p1 1g2 1d8 1a7 1a8 1g3 1d9 1p2 1e3 1p3 1d10 1a9 1a10 1g4 1d11 1g5 1p4 1g6 1a11 1q0 1p5 1g7:v 1q1 1q4 1q5 1q2 1q6 1q3 1r0 1q7 1r1 1x0 1x1 1x2 1x3 1x4 2h0:s 1w0 1w1 1w2 1L1 1x6 1R1:s 1x5 1x7 1r2 1w3 2y0 1r3 2j0:v 2l0 2h2 2l1 2y1 1w4 1L2 1L0 2j1:v 1R0:s 1R2 1L3 1R3 1w5 1L5 1R5:s 1L6 2l2 1L7 1L4 1H0 1D3 1D0 1D1 1D2 1R6 1R4 1R7:s 2y2 1C3:s 2l3 1C1:s 1H1 1D5 1C2:s 1D6 1D7 1C0 1X0 1D4 2j2 1C6:s 1C5 1C4 1C7:s 1X1
+2y3 2y4 2y5 2s0 2l4 2h7 2s1 2l5 2s3 2s5 2j3 2s4 2s6 2s8 2s7 2l6 2s11 2s9 2s13 2l7 2s14 2s12 2s15 2s16 2s18 2s21 2s17 2s19 2h1:s 2h5:s 2s2 2s10 2j4 2s22 2s23 2s24 2s25 2l8 2h4 2s27 2s28 2s29 2s30 2s31 2s32 2s20 2s33 2s34 2s35 2l9 2j5 2s36 2s37 2h6:s 2s38 2s39 2s26 2s40 2l10 2s41 2s42 2l11 2s44 2s43 2s45 2s46 2s47
+2n0 2n1 2n2 2n3 2v0 2c0 2c3 2c4 2c10 2c5 2c16 2c2 2v2 2c8 2v1 2v3 2b0 2b1 2d0 2b2 2c6 2a0 2d1 2c7 2d2 2a1 2a2 2c12 2c1 2d3 2c14 2e0 2h3:s 2d4 2a3 2c9 2a4 2d5 2c13 2e1 2d6 2a5 2a6 2d7 2c15 2c11 2e2 2p0 2p1 2d8 2a7 2g1 2g2 2a8 2g3 2d9 2g0 2e3 2p3 2p2 2d10 2a9 2a10 2d11 2p4 2a11 2q0 2p5 2q4 2g7:v 2g6:v 2q1 2q5 2q2 2q6 2q3 2q7 2x2 2x0 2x1 2x3 2g5 2x5 2w0 2w2 2x7 2g4 2w1 2x4 2x6 2w3 2r0 2w5 2w4 o4 o1 o5 o2 2L1 2R1 2L0 2L3 2L2 o0 2R0 2L4 o6:s 2L5 2r1 o7:s 2R2:s 2R3 2L7 2R7:s o8 2L6 2H0 2D1 2R4 2R5 2C1:s 2D2 2R6 2D0 2C0:s 2C2 2D3 2H1 2D4 2C3:s 2X0 2D7 2D5 2C7 2Y1:s 2C4 2C5:s 2D6 2C6:s o3 2Y0 2Y2 2Y3:s 2X1 2Y7 2Y5 2Y4 2Y10:s 2Y8 2Y9 2Y6 2Y11:s z0
+"""
 
 SCRATCH = {}
+_NEEDS = []
 
 
 def _sb(name, n, dtype):
@@ -33,19 +38,21 @@ for _t in range(R + 1):
 for _t in range(R):
     _sb("LQ%d" % _t, K, "float8_e4m3fn_x4")
     _sb("LS%d" % _t, K, "uint8")
-for _n, _w in (("U", 512), ("E", 2048), ("H", 1024), ("V", 1024), ("V2", 1024), ("K2", C), ("zer", C), ("junk", C), ("gtb", C + 2),
-               ("geb", C), ("bnd", C), ("cnt", C + 2), ("one", C), ("z", C), ("jk", 16 * WIN), ("val", C), ("Aa", C), ("Au", C)):
+for _n, _w in (("U", 512), ("E", 2048), ("H", 1024), ("Xh", 4 * C), ("V", 1024), ("zer", C), ("junk", 10 * C), ("gtb", C + 2),
+               ("geb", C), ("bnd", C), ("cnt", 2 * C + 16), ("one", C), ("z", C), ("jk", 16 * WIN), ("al", C), ("M", (KB + 1) * ROW),
+               ("Md", KB * C)):
     _sb(_n, _w, "bfloat16")
 for _n, _s, _w in (("QU", "SU", 128), ("QR", "SR", 128), ("WL", "WSL", 512), ("WQ", "WS", 512), ("QE", "SE", 512), ("QH", "SH", K)):
     _sb(_n, _w, "float8_e4m3fn_x4")
     _sb(_s, _w, "uint8")
-for _n, _w in (("iot", C), ("t16", C), ("K1", C), ("D", C), ("scJ", C), ("scP", K), ("scB", K), ("va", C),
-               ("rowA", C), ("rowB", C), ("prow0", C), ("prow", C), ("pe", K), ("Br", K),
-               ("ysb", C), ("sm", 32), ("F", 64), ("Tt", 66), ("Tb", 34), ("o", 10 * 34), ("Dt", 4 * 34), ("G2t", 34), ("G3t", 34),
-               ("Tat", 34), ("Sgt", 34), ("nC1", 64), ("nE", 64), ("nC", 32), ("Msk", 32), ("nl", 16), ("l1", 32), ("l2", 16),
-               ("l4", 16), ("tmp", 64), ("f", 10), ("Kc", 8), ("ec", 16), ("e2", 16), ("nb", 16), ("et", 16)):
+for _n, _w in (("iot", ROW), ("t16", 48), ("yy", K), ("K1", C), ("Pl", C), ("D", C), ("scJ", (KB + 1) * C), ("scP", K), ("scB", K),
+               ("rows", (KB + 1) * ROW),
+               ("prow", ROW), ("pout", C), ("pe", K), ("Br", K), ("ysb", C), ("sm", 32), ("F", 9 * 32), ("Tt", 66), ("Tb", 8 * 34),
+               ("o", 12 * 34), ("Dt", 5 * 34), ("G2t", 34), ("Tat", 34), ("Sgt", 34), ("nC1", 64), ("nE", 64), ("nF", 64), ("nC", 64),
+               ("Msk", 32), ("l1", 32), ("l2", 32), ("l3", 3 * 32), ("l4", 16), ("tmp", 8 * 34), ("TB", 3 * 33), ("TM", 3 * 33), ("f", 10),
+               ("Kc", 8), ("ec", 16), ("e2", 16), ("nb", 16), ("et", 16)):
     _sb(_n, _w, "float32")
-for _n, _w in (("L0", 32), ("LJ", 7 * 32), ("Lna", 3 * 16), ("el", 5 * 16), ("pel", 16), ("offU", 8)):
+for _n, _w in (("LJ", (KB + 1) * 32), ("Lb", 16), ("La", 16), ("el", 16), ("pel", 16), ("offU", 8), ("Lr", 32)):
     _sb(_n, _w, "uint16")
 for _n, _w in (("pt", 32), ("pi", 4), ("oi", 8)):
     _sb(_n, _w, "int32")
@@ -56,38 +63,66 @@ SEMAPHORES = (["c%d" % i for i in range(NSEM)] + ["d%d" % i for i in range(NDSEM
               + ["arr%d%d" % (t, h) for t in range(R) for h in range(2)])
 
 
-def _clash(a, b):
-    return a == b or a.startswith(b + ".") or b.startswith(a + ".")
+def v(name, a=0, b=None, s=1):
+    return (name, a, SCRATCH[name][1][1] if b is None else b, s)
+
+
+def col(name, j):
+    return (name, j, j + 1, 1)
+
+
+def ind(win, off):
+    return ("*", win, off)
+
+
+def _touched(xs):
+    out = []
+    for x in xs:
+        if isinstance(x, tuple):
+            if x[0] == "*":
+                out += _touched(x[1:])
+            else:
+                out.append((x[0], -1 if x[0][0] == "P" and len(x[0]) == 2 and x[0] != "Pl" else sum(1 << c for c in range(*x[1:]))))
+    return out
+
+
+def _needs(ops):
+    out = []
+    for i, o in enumerate(ops):
+        out.append([j for j in range(i)
+                    if any(a == b and m & n for a, m in o[3] + o[4] for b, n in ops[j][4])
+                    or any(a == b and m & n and (w or m == -1) for w, xs in ((0, o[3]), (1, o[4])) for a, m in xs for b, n in ops[j][3])])
+    return out
 
 
 def _emit(g, T, ops):
     queues = {"v": g.vector, "s": g.scalar, "t": g.tensor, "y": g.sync, "g": g}
-    known, seen, waits, needed = [], {q: set() for q in queues}, [], set()
-    for i, (q, fn, rd, wr, ext, dma) in enumerate(ops):
-        deps = []
-        for j in range(i - 1, -1, -1):
-            if j in seen[q] or ops[j][1] is None or ops[j][5] == "remote":
-                continue
-            qj, rj, wj = ops[j][0], ops[j][2], ops[j][3]
-            hit = any(_clash(a, b) for a in rd + wr for b in wj) or any(_clash(a, b) for a in wr for b in rj)
-            if not hit and qj != q:
-                hit = any(a == b and a.startswith("P") for a in rd for b in rj)
-            if hit:
-                deps.append(j)
+    if not _NEEDS:
+        _NEEDS.extend(_needs(ops))
+    needs, at = _NEEDS, {o[0]: i for i, o in enumerate(ops)}
+    plan = [(at[w.split(":")[0]], w.split(":")[-1]) for w in ORDER.split()] or [(i, "") for i in range(len(ops))]
+    plan = [(i, q if q in queues else ops[i][1][0]) for i, q in plan]
+    assert sorted(i for i, q in plan) == list(range(len(ops)))
+    pos = {i: k for k, (i, q) in enumerate(plan)}
+    known, seen, waits, needed = {}, {q: set() for q in queues}, {}, set()
+    for i, q in plan:
+        waits[i] = []
+        for j in sorted(needs[i], key=lambda j: -pos[j]):
+            assert pos[j] < pos[i]
+            if j not in seen[q] and ops[j][6] != "remote":
+                waits[i].append(j)
                 seen[q] |= known[j] | {j}
-        known.append(set(seen[q]))
-        waits.append(deps)
-        needed.update(deps)
+        known[i] = set(seen[q])
+        needed.update(waits[i])
     last, count, mark = {}, {}, {}
-    for i, (q, fn, rd, wr, ext, dma) in enumerate(ops):
+    for i, q in plan:
         for j in waits[i]:
             queues[q].wait_ge(T.sem[mark[j][0]], mark[j][1])
-        if ext is not None:
-            queues[q].wait_ge(T.sem[ext[0]], ext[1])
-        if fn is None:
-            continue
-        ins = fn()
+        for name, n in ops[i][5]:
+            queues[q].wait_ge(T.sem[name], n)
+        ins = ops[i][2](q)
         if i in needed:
+            dma = ops[i][6]
             pool = ["d%d" % k for k in range(NDSEM)] if dma else ["c%d" % k for k in range(NSEM)]
             name = [s for s in pool if s not in last or last[s] in known[i]][0]
             step = 16 if dma else 1
@@ -97,395 +132,413 @@ def _emit(g, T, ops):
             ins.then_inc(T.sem[name], step)
 
 
-def rank_program(g, core, T, topo):
-    rank = T.rank_of(core)
-    if rank is None:
-        return
-    n = len(T.cores)
+def program(g, core, T, topo):
+    rank, n = T.rank_of(core), len(T.cores)
     nxt, prv = T.cores[(rank + 1) % n], T.cores[(rank - 1) % n]
     assert topo.may_write(core, nxt)
     rid, pid = topo.addr(nxt)[0], topo.addr(nxt)[1]
     mask, n_out, n_in = topo.mask(core, nxt), len(topo.engines(core, nxt)), len(topo.engines(prv, core))
-    ops, sent = [], [0]
+    ops, sent, pre = [], [0], ["k", {}]
     V, S = g.vector, g.scalar
     u8, u32 = dt.uint8, dt.uint32
 
-    def op(q, fn, rd, wr, ext=None, dma=False):
-        ops.append((q, fn, list(rd), list(wr), ext, dma))
+    def ap(x):
+        if not isinstance(x, tuple):
+            return x
+        if x[0] == "*":
+            return ap(x[1]).indirect(ap(x[2]))
+        return T[x[0]][:, x[1]:(None if x[2] < 0 else x[2]):x[3]]
 
-    def ts(out, in0, s1, op0, rd, wr, s2=None, op1=None):
-        if op1 is None:
-            op("v", lambda: V.tensor_scalar(out, in0, s1, None, op0), rd, wr)
-        else:
-            op("v", lambda: V.tensor_scalar(out, in0, s1, s2, op0, op1), rd, wr)
+    def named(s):
+        pre[0] = s
 
-    def tt(out, a, b, o, rd, wr):
-        op("v", lambda: V.tensor_tensor(out, a, b, o), rd, wr)
+    def op(qs, fn, rd, wr, ext=(), dma=False):
+        k = pre[1][pre[0]] = pre[1].get(pre[0], -1) + 1
+        ops.append((pre[0] + str(k), qs, fn, _touched(rd), _touched(wr), ext, dma))
 
-    def scan(out, d0, d1, init, op0, op1, rd, wr):
-        op("v", lambda: V.tensor_tensor_scan(out, d0, d1, init, op0, op1), rd, wr)
+    def ts(out, in0, s1, op0, s2=None, op1=None):
+        tail = () if op1 is None else (op1,)
+        op("v", lambda q: V.tensor_scalar(ap(out), ap(in0), ap(s1), ap(s2), op0, *tail), [in0, s1, s2], [out])
 
-    def cp(out, in_, rd, wr):
-        op("v", lambda: V.tensor_copy(out, in_), rd, wr)
+    def tt(out, a, b, o):
+        op("v", lambda q: V.tensor_tensor(ap(out), ap(a), ap(b), o), [a, b], [out])
 
-    def fill(ap, c, wr):
-        op("v", lambda: V.memset(ap, c), [], wr)
+    def scan(out, d0, d1, init, op0, op1):
+        op("v", lambda q: V.tensor_tensor_scan(ap(out), ap(d0), ap(d1), ap(init), op0, op1), [d0, d1, init], [out])
 
-    def act(out, in_, func, rd, wr, **kw):
-        op("s", lambda: S.activation(out, in_, func, **kw), rd, wr)
+    def red(out, in_, o):
+        op("v", lambda q: V.tensor_reduce(ap(out), ap(in_), AxisListType.X, o), [in_], [out])
 
-    def gather(out, win, lst, rd, wr, func=AF.Copy, **kw):
-        act(out, win.indirect(lst), func, rd, wr, **kw)
+    def turn(out, in_):
+        op("v", lambda q: V.transpose(ap(out), ap(in_)), [in_], [out])
 
-    def quant(q, s, x, rd, wr):
-        op("v", lambda: V.quantize_mx(q, s, x), rd, wr)
+    def cp(out, in_, qs="v", scale=None):
+        def fn(q):
+            if q == "g":
+                return g.affine_select(ap(out), ap(in_), [[0, len(range(*out[1:]))]], A.is_ge, 0.0, 0, 0)
+            if q == "s":
+                return S.activation(ap(out), ap(in_), AF.Copy, **({} if scale is None else {"scale": scale}))
+            return V.tensor_copy(ap(out), ap(in_)) if scale is None else V.tensor_scalar(ap(out), ap(in_), scale, None, A.mult)
+        op(qs, fn, [in_], [out])
 
-    def mm(bank, w, ws, x, xs, cols, rd, ext=None):
-        op("t", lambda: g.tensor.matmul_mx(T[bank][:, 0:cols], w, ws, x, xs, True, True), rd, [bank], ext)
+    def iota(out, pattern, base, cm=0):
+        flag = {} if SCRATCH[out[0]][2] == "int32" else {"allow_small_or_imprecise_dtypes": True}
+        op("g", lambda q: g.iota(ap(out), pattern, base, cm, **flag), [], [out])
 
-    def dma(q, out, in_, rd, wr):
-        eng = g.sync if q == "y" else g.scalar
-        op(q, lambda: eng.dma_start(out, in_), rd, wr, None, True)
+    def ramp(out, base):
+        n = out[2] - out[1]
 
-    def iota(out, pattern, base, cm, wr, flt=True):
-        if flt:
-            op("g", lambda: g.iota(out, pattern, base, cm, allow_small_or_imprecise_dtypes=True), [], wr)
-        else:
-            op("g", lambda: g.iota(out, pattern, base, cm), [], wr)
+        def fn(q):
+            if q == "g":
+                return g.iota(ap(out), [[1, n]], base, 0, allow_small_or_imprecise_dtypes=True)
+            if q == "s":
+                return S.activation(ap(out), T.iot[:, 0:n], AF.Identity, bias=float(base))
+            return V.tensor_scalar(ap(out), T.iot[:, 0:n], float(base), None, A.add)
+        op("svg", fn, [v("iot")], [out])
 
-    def send(dst, src, sem, rd):
-        op("g", lambda: g.remote_dma(dst, src, T.sem[sem], T.sem.sent, pid, rid, mask), rd, [], None, "remote")
+    def fill(out, c):
+        def fn(q):
+            if q == "g":
+                return g.iota(ap(out), [[0, len(range(*out[1:]))]], int(c), 0, allow_small_or_imprecise_dtypes=True)
+            return V.memset(ap(out), c)
+        op("vg" if c == int(c) and out[3] == 1 else "v", fn, [], [out])
+
+    def act(out, in_, func, bias=0.0, scale=1.0, acc=None):
+        op("s", lambda q: S.activation(ap(out), ap(in_), func, bias=ap(bias), scale=ap(scale), accum_out=ap(acc)), [in_, bias, scale], [out, acc])
+
+    def planes(q):
+        return ({"Q": "S", "L": "LS", "W": "WS"}[q[0][0]] + q[0][(1 if q[0][0] == "Q" else 2):],) + q[1:]
+
+    def quant(q, x):
+        op("v", lambda _: V.quantize_mx(ap(q), ap(planes(q)), ap(x)), [x], [q, planes(q)])
+
+    def mm(bank, w, x, ext=()):
+        op("t", lambda _: g.tensor.matmul_mx(T[bank][:, 0:x[2] - x[1]], ap(w), ap(planes(w)), ap(x), ap(planes(x)), True, True),
+           [w, planes(w), x, planes(x)], [v(bank)], ext)
+
+    def dma(qs, out, in_, rd, wr):
+        op(qs, lambda q: (g.sync if q == "y" else S).dma_start(out, in_), rd, wr, (), True)
+
+    def store(out, in_, rd):
+        dma("ys", out, in_, [rd], [("out", len(ops), len(ops) + 1, 1)])
+
+    def send(dst, src, sem, codes):
+        def fn(q):
+            a, b = (ap(dst).bitcast(u8), ap(src).bitcast(u8)) if codes else (ap(dst), ap(src))
+            return g.remote_dma(a, b, T.sem[sem], T.sem.sent, pid, rid, mask)
+        op("g", fn, [src], [(sem, len(ops), len(ops) + 1, 1)], (), "remote")
         sent[0] += n_out
 
-    def col(name, j):
-        return T[name][:, j:j + 1]
-
     r_, r8, hf, off = col("sm", 0), col("sm", 1), col("sm", 2), col("sm", 3)
-    tau1, c1, m1 = col("sm", 4), col("sm", 5), col("tmp", 39)
+    tau1, c1, m1, off2 = col("sm", 4), col("sm", 5), col("tmp", 39), col("sm", 11)
 
-    def jumps(w, row0, key0, lst0, lkey0):
-        rows = [(row0, key0)] + [((T.rowA, "rowA"), (T.rowB, "rowB"))[k % 2] for k in range(7)]
-        lists = [(lambda a, b: lst0[0][:, lst0[1] + a // 16:lst0[1] + b // 16], lkey0)]
-        lists += [(lambda a, b, k=k: T.LJ[:, 32 * k + a // 16:32 * k + b // 16], "LJ.%d" % k) for k in range(7)]
+    def lst(k, a, b):
+        return v("LJ", 32 * k + a // 16, 32 * k + b // 16)
 
-        def jg(k):
-            a = SKIP[k] if k == 7 else 0
-            gather(rows[k][0][:, a:w], rows[k - 1][0][:, 0:w], lists[k - 1][0](a, w), [rows[k - 1][1], lists[k - 1][1]], [rows[k][1]])
+    def to_list(out, row, a, b, sc, at):
+        scan(v(sc, at + a, at + b), v("K1", a, b), row, 0.0, A.add, A.min)
+        if out:
+            ts(out, v(sc, at + a + 15, at + b, 16), off, A.add)
 
-        def jc(k):
-            a = SKIP[k] if k >= 6 else 0
-            scan(T.scJ[:, a:w], T.K1[:, a:w], rows[k][0][:, a:w], 0.0, A.add, A.min, ["K1", rows[k][1]], ["scJ"])
-            ts(lists[k][0](a, w), T.scJ[:, a + 15:w:16], off, A.add, ["scJ", "sm.off"], [lists[k][1]])
-        return jg, jc, lists
+    def jumps(t, w, row0):
+        for k in range(1, KB + 1):
+            a = 2 ** KB if k == KB else 0
+            src = row0 if k == 1 else ("rows", ROW * (k - 1))
+            named("%dj" % t)
+            cp(v("rows", ROW * k + PAD + a, ROW * k + PAD + w), ind(v(src[0], src[1], src[1] + PAD + w), lst(k - 1, a, w)), "sv")
+            named("%dl" % t)
+            to_list(lst(k, a, w), v("rows", ROW * k + PAD + a, ROW * k + PAD + w), a, w, "scJ", C * k)
 
-    def early(t):
-        mm("P7", T.QR[:], T.SR[:], T["Q%d" % t][:, 0:K], T["S%d" % t][:, 0:K], K, ["QR", "Q%d.lo" % t])
-        act(T.junk[:, 0:K], T.P7[:, 0:K], AF.Sign, ["P7", "tmp.m", "sm.tau1"], ["junk", "f.9"], bias=m1, scale=tau1, accum_out=col("f", 8))
+    def halve(t, a, b):
+        named("%dh" % t)
+        for e in range(4):
+            cp(v("Xh", C * e + a, C * e + b), v("X%d" % t, 4 * a + e, 4 * b, 4), "vs", 0.5)
 
-    def early2():
-        ts(T.nE[:], T.nC1[:], col("f", 8), A.subtract, ["nC1", "f.9"], ["nE"])
+    def early(t, bank, a, b, j, out, bounds):
+        named("%dy" % t)
+        mm(bank, v("QR"), v("Q%d" % t, a, b))
+        act(v("junk", C * j, C * j + b - a), v(bank, 0, b - a), AF.Sign, m1, tau1, col("f", j))
+        ts(v(out), v(bounds), col("f", j), A.subtract)
 
-    dma("y", T.pt[:], T.ptr[:], [], ["pt"])
-    dma("s", T.U[:], T.u[:], [], ["U"])
-    dma("y", T.X0[:, 0:1024], T.x[:, 0:1024], [], ["X0.lo"])
-    dma("s", T.X0[:, 1024:2048], T.x[:, 1024:2048], [], ["X0.hi"])
-    dma("y", T.WL[:].bitcast(u8), T.wc[:], ["X0"], ["WL"])
-    dma("y", T.WSL[:], T.ws[:], [], ["WSL"])
+    named("i")
+    dma("y", T.pt[:], T.ptr[:], [], [v("pt")])
+    dma("s", T.U[:], T.u[:], [], [v("U")])
+    dma("y", T.X0[:, 0:1024], T.x[:, 0:1024], [], [v("X0", 0, 1024)])
+    dma("s", T.X0[:, 1024:2048], T.x[:, 1024:2048], [], [v("X0", 1024, 2048)])
+    dma("y", T.WL[:].bitcast(u8), T.wc[:], [v("X0")], [v("WL")])
+    dma("y", T.WSL[:], T.ws[:], [v("X0")], [v("WSL")])
 
-    iota(T.pi[:, 0:1], [[1, 1]], 0, 1, ["pi.0"], False)
-    iota(T.t16[:], [[0, C // 16], [1, 16]], 0, 0, ["t16"])
-    iota(T.iot[:], [[1, C]], 0, 0, ["iot"])
-    iota(T.oi[:], [[16, 8]], 0, 0, ["oi"], False)
-    fill(T.one[:], 1.0, ["one"])
-    ts(T.pi[:, 1:2], T.pi[:, 0:1], 15, A.bitwise_and, ["pi.0"], ["pi.1"])
-    ts(T.pi[:, 2:3], T.pi[:, 0:1], 7, A.bitwise_and, ["pi.0"], ["pi.2"])
-    ts(T.pi[:, 3:4], T.pi[:, 0:1], 16, A.bitwise_and, ["pi.0"], ["pi.3"])
-    fill(T.zer[:], 0.0, ["zer"])
-    cp(T.sm[:, 0:3], T.pi[:, 1:4], ["pi"], ["sm.r"])
-    for nm in ("G2t", "G3t", "Tat", "Sgt"):
-        fill(T[nm][:], 1.0, [nm])
-    fill(T.Tt[:], 0.0, ["Tt"])
-    fill(T.Tb[:], 0.0, ["Tb"])
-    ts(T.K2[:], T.t16[:], r_, A.is_equal, ["t16", "sm.r"], ["K2"], BIG, A.mult)
-    act(T.K1[:], T.K2[:], AF.Identity, ["K2"], ["K1"], bias=-HOLD)
-    ts(off, r_, -HOLD, A.mult, ["sm.r"], ["sm.off"], 15 * HOLD, A.add)
-    fill(T.Dt[:], 0.0, ["Dt"])
-    fill(T.gtb[:, C:C + 2], 0.0, ["gtb.pad"])
-    fill(T.cnt[:, 0:1], 0.0, ["cnt.pad"])
-    fill(col("Tat", 32), -1.5, ["Tat"])
-    cp(T.L0[:], T.pt[:], ["pt"], ["L0"])
-    gather(T.prow0[:], T.iot[:], T.L0[:], ["iot", "L0"], ["prow0"])
-    jg, jc, lists = jumps(C, T.prow0, "prow0", (T.L0, 0), "L0")
-    jg(1)
-    ts(col("sm", 6), r_, 7.5, A.is_gt, ["sm.r"], ["sm.6"], 2.0, A.mult)
-    ts(col("sm", 7), r_, 0.25, A.mult, ["sm.r"], ["sm.7"], 0.25, A.add)
-    ts(col("sm", 8), r_, 0.125, A.mult, ["sm.r"], ["sm.8"], 1.125, A.add)
-    ts(col("sm", 9), r_, 8.0, A.not_equal, ["sm.r"], ["sm.9"], -BIG, A.mult)
-    ts(col("sm", 10), r_, 6.5, A.is_gt, ["sm.r"], ["sm.10"], 0.125, A.mult)
-    fill(col("sm", 13), 0.125, ["sm.13"])
-    unit = 2.0 ** -20
-    for j, step in enumerate((4624, 272, 16)):
-        ts(col("Kc", j), r_, 1.0, A.add, ["sm.r"], ["Kc.%d" % j], step * unit, A.mult)
-    ts(col("Kc", 3), r_, 0.5, A.add, ["sm.r"], ["Kc.3"], unit, A.mult)
-    ts(col("Kc", 4), r_, 1.0, A.add, ["sm.r"], ["Kc.4"], 78608 * unit, A.mult)
-    ts(col("Kc", 5), r_, 1.0, A.add, ["sm.r"], ["Kc.5"], unit, A.mult)
-    ts(tau1, col("sm", 6), -1.0, A.add, ["sm.6"], ["sm.tau1"])
-    ts(c1, col("sm", 6), -1.5, A.mult, ["sm.6"], ["sm.c1"], 1.5, A.add)
-    ts(col("G3t", 32), col("sm", 8), col("sm", 7), A.max, ["sm.7", "sm.8"], ["G3t"])
-    ts(col("sm", 12), col("sm", 10), 0.125, A.add, ["sm.10"], ["sm.12"])
-    ts(T.tmp[:, 0:16], T.iot[:, 0:16], r_, A.is_le, ["iot", "sm.r"], ["tmp.a"], 4.0, A.mult)
-    ts(T.tmp[:, 16:24], T.iot[:, 0:8], r8, A.is_le, ["iot", "sm.r"], ["tmp.b"], 2.0 ** 25, A.mult)
-    ts(T.l1[:], T.iot[:, 0:32], 15.5, A.is_gt, ["iot"], ["l1"], 16.0, A.mult)
-    ts(T.l2[:], T.iot[:, 0:16], 16.0, A.mult, ["iot", "sm.r"], ["l2"], r_, A.add)
-    cp(T.offU[:], T.oi[:], ["oi"], ["offU"])
-    ts(T.tmp[:, 0:16], T.tmp[:, 0:16], 1.0, A.max, ["tmp.a"], ["tmp.a"])
-    ts(T.tmp[:, 16:24], T.tmp[:, 16:24], 1.0, A.max, ["tmp.b"], ["tmp.b"])
-    ts(T.Msk[:], T.l1[:], hf, A.not_equal, ["l1", "sm.r"], ["Msk"], -BIG, A.mult)
-    quant(T.QU[:], T.SU[:], T.U[:], ["U"], ["QU"])
-    op("v", lambda: V.tensor_reduce(col("G2t", 32), T.tmp[:, 0:16], AxisListType.X, A.mult), ["tmp.a"], ["G2t"])
-    scan(T.tmp[:, 32:40], T.tmp[:, 16:24], T.zer[:, 0:8], 2.0 ** -125, A.mult, A.add, ["tmp.b", "zer"], ["tmp.m"])
-    ts(T.nC1[:, 0:32], T.Msk[:], c1, A.add, ["Msk", "sm.c1"], ["nC1.a"])
-    ts(T.nC1[:, 32:64], T.Msk[:], c1, A.add, ["Msk", "sm.c1", "sm.9"], ["nC1.b"], col("sm", 9), A.add)
-    cp(T.QR[:].bitcast(u32), T.QU[:].bitcast(u32).indirect(T.offU[:]), ["QU", "offU"], ["QR.c"])
-    jc(1)
-    jg(2)
-    cp(T.SR[:], T.SU[:].indirect(T.offU[:]), ["QU", "offU"], ["QR.s"])
-    quant(T.Q0[:, 0:K], T.S0[:, 0:K], T.X0[:, 0:1024], ["X0.lo"], ["Q0.lo"])
-    early(0)
-    quant(T.Q0[:, K:C], T.S0[:, K:C], T.X0[:, 1024:2048], ["X0.hi"], ["Q0.hi"])
-    early2()
-    jc(2)
-    ts(T.nl[:], T.l2[:], off, A.subtract, ["l2", "sm.off"], ["nl"])
-    ts(T.nb[:], T.l2[:], 1024.0, A.mult, ["l2"], ["nb"], 512.0, A.add)
-    ts(T.et[:], T.iot[:, 0:16], 32.0, A.mult, ["iot"], ["et"], float(WIN), A.add)
+    named("k")
+    iota(col("pi", 0), [[1, 1]], 0, 1)
+    iota(v("t16", 0, 16), [[1, 16]], 0)
+    iota(v("iot"), [[1, ROW]], 0)
+    iota(v("oi"), [[16, 8]], 0)
+    ramp(v("Pl"), -K - int(UNIT))
+    iota(v("l1"), [[16, 2], [0, 16]], 0)
+    iota(v("l2"), [[16, 32]], PAD)
+    iota(v("tmp", 68, 102), [[0, 17], [-2, 2]], 4)
+    iota(v("tmp", 102, 136), [[0, 17], [1, 2]], 2)
+    iota(v("tmp", 136, 170), [[0, 17], [1, 2]], 3)
+    ramp(v("prow", PAD + K, ROW), PAD)
+    ramp(v("pout", K, C), 0)
+    for j, m in enumerate((15, 7, 16)):
+        ts(col("pi", j + 1), col("pi", 0), m, A.bitwise_and)
+    cp(v("sm", 0, 3), v("pi", 1, 4))
+    ts(v("t16", 16, 32), v("t16", 0, 16), r_, A.is_equal, BIG, A.mult)
+    ts(v("t16", 32, 48), v("t16", 16, 32), -HOLD, A.add)
+    ts(v("Lr"), v("l1"), 0.0, A.mult, r_, A.add)
+    cp(v("K1"), ind(v("t16", 32, 48), v("Lr")), "sv")
+    ts(off, r_, -HOLD, A.mult, 15 * HOLD, A.add)
+    ts(off2, off, 1.0, A.add)
+    ts(v("l2"), v("l2"), r_, A.add)
+    for k in range(1, KB):
+        fill(v("rows", ROW * k, ROW * k + PAD), 0.0)
+    fill(v("rows", 0, PAD), 0.0)
+    fill(v("prow", 0, PAD), 0.0)
+    named("p")
+    ts(v("l3", 0, 32), v("pt"), float(PAD), A.add)
+    tt(v("l3", 32, 64), v("l3", 0, 32), v("l2"), A.not_equal)
+    tt(v("l3", 64, 96), v("l3", 0, 32), v("l3", 32, 64), A.mult)
+    cp(lst(0, 0, C), v("l3", 64, 96))
+    cp(v("rows", PAD, ROW), ind(v("iot"), lst(0, 0, C)), "sv")
+    jumps(0, C, ("rows", 0))
+    named("k")
+    fill(v("one"), 1.0)
+    fill(v("zer"), 0.0)
+    for nm in ("G2t", "Tat", "Sgt"):
+        fill(v(nm), 1.0)
+    for nm in ("Tt", "Tb", "Dt"):
+        fill(v(nm), 0.0)
+    fill(v("gtb", C, C + 2), 0.0)
+    fill(col("cnt", 0), 0.0)
+    fill(v("cnt", C + 1), (1 - PAD) * UNIT)
+    for k in range(KB + 1):
+        fill(v("M", ROW * k, ROW * k + PAD), -K - UNIT)
+    fill(col("Tat", 32), -1.5)
+    ts(col("sm", 6), r_, 7.5, A.is_gt, 2.0, A.mult)
+    ts(col("sm", 9), r_, 8.0, A.not_equal, -BIG, A.mult)
+    unit = 2.0 ** -23
+    for j, step in enumerate((78608, 4624, 272, 16)):
+        ts(col("Kc", j), r_, 1.0, A.add, step * unit, A.mult)
+    ts(col("Kc", 4), r_, 0.5, A.add, unit, A.mult)
+    ts(col("Kc", 5), r_, 1.0, A.add, unit, A.mult)
+    ts(col("Kc", 6), r_, 1.0, A.add, 17 * 78608 * unit, A.mult)
+    ts(tau1, col("sm", 6), -1.0, A.add)
+    ts(c1, col("sm", 6), -1.5, A.mult, 1.5, A.add)
+    ts(v("tmp", 16, 24), v("t16", 0, 8), r8, A.is_le, 2.0 ** 25, A.mult)
+    ts(v("tmp", 24, 32), v("tmp", 16, 24), 1.0, A.max)
+    scan(v("tmp", 32, 40), v("tmp", 24, 32), v("Dt", 0, 8), 2.0 ** -125, A.mult, A.add)
+    ts(v("Msk"), v("l1"), hf, A.not_equal, -BIG, A.mult)
+    ts(v("nC1", 0, 32), v("Msk"), c1, A.add)
+    ts(v("nC1", 32, 64), v("Msk"), c1, A.add, col("sm", 9), A.add)
+    fill(v("tmp", 68, 85, 16), 0.0)
+    scan(v("tmp", 170, 203), v("tmp", 68, 101), v("Sgt", 0, 33), 1.0, A.mult, A.max)
+    ts(v("tmp", 204, 236), v("l1"), hf, A.is_equal)
+    fill(col("tmp", 236), 1.0)
+    tt(v("TB", 66, 99), v("tmp", 170, 203), v("tmp", 204, 237), A.mult)
+    tt(v("tmp", 238, 271), v("TB", 66, 99), v("tmp", 102, 135), A.mult)
+    ts(v("TB", 33, 66), v("tmp", 238, 271), 0.5, A.mult)
+    ts(v("tmp", 170, 203), v("TB", 66, 99), col("Kc", 6), A.mult)
+    tt(v("TB", 0, 33), v("tmp", 170, 203), v("TB", 33, 66), A.add)
+    ts(col("sm", 7), r_, hf, A.add)
+    ts(v("tmp", 68, 100), v("iot", 0, 32), col("sm", 7), A.is_equal)
+    tt(v("tmp", 102, 134), v("TB", 66, 98), v("tmp", 136, 168), A.mult)
+    tt(v("tmp", 204, 236), v("tmp", 68, 100), v("tmp", 102, 134), A.mult)
+    red(col("G2t", 32), v("tmp", 204, 236), A.max)
+    ts(v("nb"), v("l2", 0, 16), 2 * UNIT, A.mult, (1 - 2 * PAD) * UNIT, A.add)
+    ts(v("tmp", 0, 16), v("t16", 0, 16), 16.0, A.mult, float(WIN), A.add)
+    ts(v("et"), v("tmp", 0, 16), off, A.subtract)
+    named("u")
+    cp(v("offU"), v("oi"))
+    quant(v("QU"), v("U"))
+    op("v", lambda q: V.tensor_copy(T.QR[:].bitcast(u32), T.QU[:].bitcast(u32).indirect(T.offU[:])), [v("QU"), v("offU")], [v("QR")])
+    cp(v("SR"), ind(v("SU"), v("offU")), "vs")
+    quant(v("Q0", 0, K), v("X0", 0, 1024))
+    early(0, "P7", 0, K, 8, "nF", "nC1")
+    named("u")
+    quant(v("Q0", K, C), v("X0", 1024, 2048))
+    halve(0, 0, K)
+    halve(0, K, C)
+    named("w")
     for b in range(4):
-        op("g", lambda b=b: g.affine_select(T.E[:, C * b:C * b + C], T.one[:], [[1, C]], A.is_equal, 0.0, -b, -4), ["one"], ["E.%d" % b])
-    send(T.WQ[:].bitcast(u8), T.WL[:].bitcast(u8), "warr", ["WL"])
-    send(T.WS[:], T.WSL[:], "warr", ["WSL"])
+        op("g", lambda q, b=b: g.affine_select(T.E[:, C * b:C * b + C], T.one[:], [[1, C]], A.is_equal, 0.0, -b, -4), [v("one")], [v("E", C * b, C * b + C)])
+    send(v("WQ"), v("WL"), "warr", True)
+    send(v("WS"), v("WSL"), "warr", False)
+    quant(v("QE"), v("E"))
 
     def oc(s, j):
         return col("o", 34 * s + j)
 
-    def select(t, fills, dstep):
-        Q, Sx, qk = T["Q%d" % t], T["S%d" % t], "Q%d" % t
-        mm("P3", T.QR[:], T.SR[:], Q[:, K:C], Sx[:, K:C], K, ["QR", qk + ".hi"])
-        mm("P0", T.QR[:], T.SR[:], Q[:], Sx[:], C, ["QR", qk])
-        mm("P1", T.QR[:], T.SR[:], Q[:], Sx[:], C, ["QR", qk])
-        tau, w = oc(0, 31), oc(9, 31)
+    def osl(s, k):
+        return v("o", 34 * s, 34 * s + k)
 
-        def count(s, bias, bk, scale, sk):
-            fk = "f.%d" % s
-            if s == 1:
-                act(T.junk[:, 0:K], T.P3[:, 0:K], AF.Sign, ["P3"] + bk + sk, ["junk", fk], bias=bias, scale=scale, accum_out=col("f", s - 1))
-            elif s < 8:
-                act(T.junk[:], T.P0[:], AF.Sign, ["P0"] + bk + sk, ["junk", fk], bias=bias, scale=scale, accum_out=col("f", s - 1))
-            else:
-                act(T.junk[:], T.D[:], AF.Sign, ["D"] + bk, ["junk", fk], bias=bias, accum_out=col("f", s - 1))
-            for fn in fills.get(s, []):
-                fn()
+    def select(t, a):
+        named("%ds" % t)
+        mm("P3", v("QR"), v("Q%d" % t, a, C))
+        mm("P0", v("QR"), v("Q%d" % t))
+        mm("P1", v("QR"), v("Q%d" % t))
+        tau = oc(0, 31)
 
-        def flag(s, blk, cap, ck, m, mk):
-            ts(T.F[:, 32 * blk:32 * blk + 32], cap, col("f", s - 1), A.is_ge, ck + ["f.%d" % s] + mk, ["F.%d" % blk], m, A.mult)
+        def step(s, src, bias, scale, cap, cmp, m):
+            act(v("junk", C * (s - 1), C * (s - 1) + src[2]), src, AF.Sign, bias, scale, col("f", s - 1))
+            ts(v("F", 32 * s, 32 * s + 32) if s > 1 else v("F", 0, 32), cap, col("f", s - 1), cmp, m, A.mult)
+            if s > 1:
+                turn(v("Tb", 34 * (s - 1), 34 * (s - 1) + 32), v("F", 32 * s, 32 * s + 32))
 
-        def turn(two):
-            if two:
-                op("v", lambda: V.transpose(T.Tt[:, 0:64], T.F[:]), ["F"], ["Tt"])
-            else:
-                op("v", lambda: V.transpose(T.Tb[:, 0:32], T.F[:, 0:32]), ["F.0"], ["Tb"])
+        step(1, v("P3", 0, C - a), m1, tau1, v("nF", 0, 32), A.is_ge, m1)
+        ts(v("F", 32, 64), v("nF", 32, 64), col("f", 0), A.is_ge, 2.0, A.mult)
+        turn(v("Tt", 0, 64), v("F", 0, 64))
+        scan(osl(0, 33), v("Tt", 32, 65), v("Tat", 0, 33), -1.0, A.add, A.mult)
+        scan(osl(1, 33), v("Tt", 0, 33), v("G2t", 0, 33), 0.0, A.max, A.mult)
+        ts(v("nC", 32, 64), v("Msk"), -1.0, A.mult, oc(0, 32), A.add)
+        ts(v("nC", 0, 32), v("Msk"), oc(0, 32), A.add)
+        ts(v("TM"), v("TB"), oc(1, 31), A.mult)
+        ts(col("Sgt", 32), tau, -1.0, A.mult)
+        step(2, v("P0"), oc(1, 32), tau, v("nC", 32, 64), A.is_lt, -HUGE)
+        for j, s in enumerate((2, 9, 10)):
+            scan(v("o", 34 * s + 33, 34 * s + 1, -1), v("Tb", 65, 33, -1), v("TM", 33 * j + 31, 33 * j - 1, -1), col("TM", 33 * j + 32), A.add, A.max)
+        w = oc(10, 2)
+        ts(v("Dt", 33, 170, 34), v("Kc", 0, 5), w, A.mult)
+        ts(col("sm", 16), col("Kc", 5), w, A.mult)
+        for s in range(3, 8):
+            bias, base = (oc(2, 2), oc(9, 2)) if s == 3 else (oc(s - 1, 33), oc(s - 1, 31))
+            step(s, v("P0"), bias, tau, v("nC", 0, 32), A.is_ge, bias)
+            scan(osl(s, 34), v("Tb", 34 * (s - 1), 34 * s), v("Dt", 34 * (s - 3), 34 * (s - 2)), base, A.max, A.add)
+            if s == 3:
+                ts(col("Dt", 4 * 34 + 32), oc(3, 31), -1.0, A.mult)
+                ts(v("D"), v("P1"), tau, A.mult, oc(3, 31), A.add)
+        ts(v("z"), v("D"), oc(7, 32), A.add, tau, A.mult)
+        step(8, v("D"), oc(7, 33), 1.0, v("nC", 0, 32), A.is_ge, col("sm", 16))
+        scan(osl(8, 33), v("Tb", 34 * 7, 34 * 7 + 33), v("Sgt", 0, 33), 0.0, A.max, A.mult)
 
-        def osl(s, k):
-            return T.o[:, 34 * s:34 * s + k]
-
-        count(1, m1, ["tmp.m"], tau1, ["sm.tau1"])
-        flag(1, 0, T.nE[:, 0:32], ["nE"], m1, ["tmp.m"])
-        flag(1, 1, T.nE[:, 32:64], ["nE"], 2.0, [])
-        turn(True)
-        scan(osl(1, 33), T.Tt[:, 0:33], T.G2t[:, 0:33], 0.0, A.max, A.mult, ["Tt", "G2t"], ["o.1"])
-        scan(osl(0, 33), T.Tt[:, 32:65], T.Tat[:, 0:33], -1.0, A.add, A.mult, ["Tt", "Tat"], ["o.0"])
-        ts(T.nC[:], T.Msk[:], oc(0, 32), A.add, ["Msk", "o.0"], ["nC"])
-        ts(col("Sgt", 32), tau, -1.0, A.mult, ["o.0"], ["Sgt"])
-        count(2, oc(1, 32), ["o.1"], tau, ["o.0"])
-        flag(2, 0, T.nC[:], ["nC"], oc(1, 32), ["o.1"])
-        turn(False)
-        scan(osl(2, 33), T.Tb[:, 0:33], T.G3t[:, 0:33], oc(1, 31), A.max, A.mult, ["Tb", "G3t", "o.1"], ["o.2"])
-        ts(T.sm[:, 14:16], T.sm[:, 12:14], oc(2, 31), A.mult, ["sm.12", "sm.13", "o.2"], ["sm.w"])
-        count(3, oc(2, 32), ["o.2"], tau, ["o.0"])
-        flag(3, 0, T.nC[:], ["nC"], oc(2, 32), ["o.2"])
-        flag(3, 1, T.nC[:], ["nC"], col("sm", 14), ["sm.w"])
-        turn(True)
-        scan(osl(3, 32), T.Tt[:, 0:32], T.G2t[:, 0:32], oc(2, 31), A.max, A.mult, ["Tt", "G2t", "o.2"], ["o.3.a"])
-        scan(osl(9, 32), T.Tt[:, 32:64], T.G2t[:, 0:32], col("sm", 15), A.max, A.mult, ["Tt", "G2t", "sm.w"], ["o.9"])
-        ts(oc(3, 33), col("Kc", 4), w, A.mult, ["Kc.4", "o.9", "o.3.a"], ["o.3.m"], oc(3, 31), A.add)
-        ts(col("sm", 16), col("Kc", 5), w, A.mult, ["Kc.5", "o.9"], ["sm.cand"])
-        ts(T.Dt[:, 33:136:34], T.Kc[:, 0:4], w, A.mult, ["Kc", "o.9"], ["Dt.a"])
-        ts(col("Dt", 3 * 34 + 32), oc(3, 31), -1.0, A.mult, ["o.3.a"], ["Dt.b"])
-        for s in range(4, 8):
-            pk = "o.%d" % (s - 1)
-            if s == dstep:
-                ts(T.D[:], T.P1[:], tau, A.mult, ["P1", "o.0", "o.3.a"], ["D"], oc(3, 31), A.add)
-            count(s, oc(s - 1, 33), [pk], tau, ["o.0"])
-            flag(s, 0, T.nC[:], ["nC"], oc(s - 1, 33), [pk])
-            turn(False)
-            scan(osl(s, 34), T.Tb[:], T.Dt[:, 34 * (s - 4):34 * (s - 3)], oc(s - 1, 31), A.max, A.add, ["Tb", "Dt", pk], ["o.%d" % s])
-        ts(col("sm", 17), oc(7, 31), tau, A.mult, ["o.7", "o.0"], ["sm.tl"])
-        ts(T.z[:], T.P1[:], col("sm", 17), A.add, ["P1", "sm.tl"], ["z"])
-        count(8, oc(7, 33), ["o.7"], None, [])
-        flag(8, 0, T.nC[:], ["nC"], col("sm", 16), ["sm.cand"])
-        turn(False)
-        scan(osl(8, 33), T.Tb[:, 0:33], T.Sgt[:, 0:33], 0.0, A.max, A.mult, ["Tb", "Sgt"], ["o.8"])
-
-    hs = [(h, HALF * h, HALF * h + HALF, 8 * h, 8 * h + 8) for h in range(2)]
+    hs = [(HALF * h, HALF * h + HALF, 8 * h, 8 * h + 8) for h in range(2)]
     for t in range(R):
-        X, Xn, xk, nk = T["X%d" % t], T["X%d" % (t + 1)], "X%d" % t, "X%d" % (t + 1)
-        Qn, Sn, qn = T["Q%d" % (t + 1)], T["S%d" % (t + 1)], "Q%d" % (t + 1)
-        fills, dstep = F0 if t == 0 else F1
-        select(t, {s: [lambda x=x, jg=jg, jc=jc: (jg if x[0] == "g" else jc)(int(x[1])) for x in v.split()] for s, v in fills.items()}, dstep)
+        Xn, Qn, Sn = "X%d" % (t + 1), "Q%d" % (t + 1), T["S%d" % (t + 1)]
+        select(t, K if t == 0 else K + HALF)
         thr = oc(8, 32)
-        ts(T.gtb[:, 0:C], T.z[:], thr, A.is_gt, ["z", "o.8"], ["gtb.a"], -1024.0, A.mult)
-        ts(T.geb[:], T.z[:], thr, A.is_ge, ["z", "o.8"], ["geb"], 1024.0, A.mult)
-        scan(T.bnd[:, ::-1], T.gtb[:, C:0:-1], T.zer[:], 1024.0 * K, A.add, A.add, ["gtb", "zer"], ["bnd"])
-        scan(T.cnt[:, 1:C + 1], T.geb[:], T.bnd[:], 0.0, A.add, A.min, ["geb", "bnd"], ["cnt.a"])
+        named("%dn" % t)
+        ts(v("gtb", 0, C), v("z"), thr, A.is_gt, -UNIT, A.mult)
+        ts(v("geb"), v("z"), thr, A.is_ge, UNIT, A.mult)
+        scan(v("bnd", C - 1, -1, -1), v("gtb", C, 0, -1), v("zer"), UNIT * K, A.add, A.add)
+        scan(v("cnt", 1, C + 1), v("geb"), v("bnd"), 0.0, A.add, A.min)
         w = C if t == 0 else K
-        order = [(7, 128)] + ([(7, K)] if t == 0 else []) + [(k, SKIP[k]) for k in range(6, -1, -1)]
-        bufs = [((T.val, "val"), (T.Aa, "Aa"))[k % 2] for k in range(len(order) + 1)]
-        pw, pk = (T.prow0[:], "prow0") if t == 0 else (T.prow[:], "prow")
-        LQ, LS, lk = T["LQ%d" % t], T["LS%d" % t], "Lna.%d" % t
+        B = 2 ** KB
+        named("%dv" % t)
+        for h in range(2):
+            a, b = h * w // 2, (h + 1) * w // 2
+            scan(v("al", a, b), v("cnt", a + 1, b + 1), v("cnt", a, b), 0.0, A.max, A.subtract)
+            scan(v("M", PAD + b - 1, PAD + a - 1, -1), v("Pl", b - 1, a - 1, -1), v("al", b - 1, a - 1, -1), BIG, A.min, A.add)
 
-        def work(name):
-            kind, i = name[0].lower(), int(name[1:])
-            h, e = i % 2, i // 2
-            a, b, c, d = hs[h][1:]
-            lna = T.Lna[:, 16 * t + c:16 * t + d]
+        def blocks(m):
+            named("%db" % t)
+            for a in range(B, w, B):
+                tt(v("M", m + PAD + a, m + PAD + a + B), ind(v("M", m, m + PAD + a), lst(KB, a, a + B)), v("M", m + PAD + a, m + PAD + a + B), A.max)
 
-            def copy(out, in_, rd, wr):
-                if name[0] == kind:
-                    act(out, in_, AF.Copy, rd, wr)
-                else:
-                    cp(out, in_, rd, wr)
-            if kind == "v":
-                if i == 0:
-                    ts(T.va[:, 0:w], T.cnt[:, 1:w + 1], 1025.0 / 1024, A.mult, ["cnt"], ["va"], -1025.0, A.add)
-                else:
-                    tt(T.val[:, 0:w], T.va[:, 0:w], T.cnt[:, 0:w], A.subtract, ["va", "cnt"], ["val"])
-            elif kind == "k":
-                if i == 0:
-                    copy(T.Aa[:, 0:128], T.val[:, 0:128], ["val.0"], ["Aa.0.k"])
-                else:
-                    copy(T.val[:, 128:K], T.Aa[:, 128:K], ["Aa.0.a"], ["val.0"])
-            elif kind == "a":
-                k, lo = order[e]
-                lo, hi = max(lo, h * w // 2), (h + 1) * w // 2
-                src, dst = bufs[e], bufs[e + 1]
-                tt(dst[0][:, lo:hi], src[0][:, 0:hi].indirect(lists[k][0](lo, hi)), T.Au[:, lo:hi], A.max,
-                   [src[1] if h else src[1] + ".0", lists[k][1], "Au.%d" % h], [dst[1] + ".%d" % h + (".a" if e == 0 else "")])
-            elif kind == "d":
-                lo = order[e - 1][1] if e else 0
-                lo, hi = max(lo, h * w // 2), (h + 1) * w // 2
-                copy(T.Au[:, lo:hi], bufs[e][0][:, lo:hi], [bufs[e][1] + ".%d" % h + (".a" if e == 1 else "")], ["Au.%d" % h])
-            elif kind == "c":
-                act(T.jk[:, WIN * i:WIN * i + WIN], T.cnt[:, 1 + 16 * i:1 + 16 * i + WIN], AF.Sign, ["cnt", "nb"],
-                    ["jk.%d" % i, "ec.%d.%d" % (i // 8, i)], bias=col("nb", i), scale=-1.0, accum_out=col("ec", i))
-            elif kind == "e":
-                tt(T.e2[:, c:d], T.ec[:, c:d], T.et[:, c:d], A.add, ["ec.%d" % h, "et"], ["e2.%d" % h])
-            elif kind == "l":
-                if e == 4:
-                    ts(T.el[:, 64 + c:64 + d], T.e2[:, c:d], 0.5, A.mult, ["e2.%d" % h], ["el.4.%d" % h])
-                else:
-                    ts(T.el[:, 16 * e + c:16 * e + d], T.e2[:, c:d], 2.0, A.mult, ["e2.%d" % h], ["el.%d.%d" % (e, h)], float(e), A.add)
-            elif kind == "p":
-                gather(T.pe[:, a:b], pw, T.el[:, 64 + c:64 + d], [pk, "el.4.%d" % h], ["pe.%d" % h])
-            elif kind == "q":
-                scan(T.scP[:, a:b], T.K1[:, a:b], T.pe[:, a:b], 0.0, A.add, A.min, ["K1", "pe.%d" % h], ["scP.%d" % h])
-            elif kind == "r":
-                ts(T.pel[:, c:d], T.scP[:, a + 15:b:16], off, A.add, ["scP.%d" % h, "sm.off"], ["pel.%d" % h])
-            elif kind == "g":
-                gather(T.V[:, K * e + a:K * e + b], X[:], T.el[:, 16 * e + c:16 * e + d], [xk, "el.%d.%d" % (e, h)], ["V.%d.%d" % (e, h)], scale=0.5)
-            elif kind == "u":
-                copy(T.V2[:, K * e + a:K * e + b], T.V[:, K * e + a:K * e + b], ["V.%d.%d" % (e, h)], ["V2.%d.%d" % (e, h)])
-            elif kind == "b":
-                gather(T.Br[:, a:b], bufs[-1][0][:, 0:w], T.pel[:, c:d], [bufs[-1][1], "pel.%d" % h], ["Br.%d" % h], func=AF.Abs)
-            elif kind == "s":
-                scan(T.scB[:, a:b], T.K1[:, a:b], T.Br[:, a:b], 0.0, A.add, A.min, ["K1", "Br.%d" % h], ["scB.%d" % h])
-            elif kind == "m":
-                tt(T.l4[:, c:d], T.scB[:, a + 15:b:16], T.nl[:, c:d], A.min, ["scB.%d" % h, "nl"], ["l4.%d" % h])
-            elif kind == "n":
-                ts(lna, T.l4[:, c:d], off, A.add, ["l4.%d" % h, "sm.off"], [lk + ".%d" % h])
-            elif kind == "x":
-                tt(Xn[:, 4 * a + e:4 * b:4], T.V[:, K * e:K * e + b].indirect(lna), T.V2[:, K * e + a:K * e + b], A.add,
-                   ["V.%d.%d" % (e, j) for j in range(h + 1)] + ["V2.%d.%d" % (e, h), lk + ".%d" % h], [nk + ".lo.%d.%d" % (h, e)])
-            elif kind == "w":
-                qk = qn + ".lo.%d" % h
-                quant(Qn[:, a:b], Sn[:, a:b], Xn[:, 4 * a:4 * b], [nk + ".lo.%d" % h], [qk])
-                send(LQ[:, a:b].bitcast(u8), Qn[:, a:b].bitcast(u8), "arr%d%d" % (t, h), [qk])
-                send(LS[:, a:b], Sn[:, a:b], "arr%d%d" % (t, h), [qk])
-
-        for name in (PLAN0 if t == 0 else PLAN1).split():
-            work(name)
-        gather(T.prow[:, 0:K], T.iot[:, 0:K], T.Lna[:, 16 * t:16 * t + 16], ["iot", lk], ["prow.lo"])
-        if t == 0:
-            act(T.prow[:, K:C], T.iot[:, 0:K], AF.Copy, ["iot"], ["prow.hi"])
-            quant(T.QE[:], T.SE[:], T.E[:], ["E"], ["QE"])
+        if LONG_FIRST:
+            blocks(0)
+        for j in range(KB):
+            k = KB - 1 - j if LONG_FIRST else j
+            for h in range(2):
+                a, b = h * w // 2, (h + 1) * w // 2
+                named("%dd" % t)
+                cp(v("Md", C * j + a, C * j + b), v("M", ROW * j + PAD + a, ROW * j + PAD + b), "vsg")
+                named("%da" % t)
+                tt(v("M", ROW * (j + 1) + PAD + a, ROW * (j + 1) + PAD + b), ind(v("M", ROW * j, ROW * j + PAD + b), lst(k, a, b)), v("Md", C * j + a, C * j + b), A.max)
+        if not LONG_FIRST:
+            blocks(ROW * KB)
+        named("%dc" % t)
+        scan(v("yy", K - 1, -1, -1), v("cnt", C - 1, -1, -2), v("cnt", C, 0, -2), BIG, A.min, A.add)
+        for i in range(16):
+            act(v("jk", WIN * i, WIN * i + WIN), v("yy", 8 * i, 8 * i + WIN), AF.Sign, col("nb", i), -1.0, col("ec", i))
+        for h in range(2):
+            a, b, c, d = hs[h]
+            named("%de" % t)
+            tt(v("e2", c, d), v("ec", c, d), v("et", c, d), A.add)
+            ts(v("el", c, d), v("e2", c, d), off, A.add)
+            named("%dp" % t)
+            cp(v("pe", a, b), ind(v("rows" if t == 0 else "prow", PAD, ROW), v("el", c, d)), "sv")
+            to_list(v("pel", c, d), v("pe", a, b), a, b, "scP", 0)
+            named("%dg" % t)
+            for e in range(4):
+                cp(v("V", K * e + a, K * e + b), ind(v("Xh", C * e, C * e + C), v("el", c, d)), "sv")
+            named("%dq" % t)
+            act(v("Br", a, b), ind(v("M", ROW * KB, ROW * KB + PAD + w), v("pel", c, d)), AF.Abs, float(K))
+            to_list(None, v("Br", a, b), a, b, "scB", 0)
+            tt(v("l4", c, d), v("scB", a + 15, b, 16), v("e2", c, d), A.min)
+            ts(v("La", c, d), v("l4", c, d), off, A.add)
+            named("%dx" % t)
+            for e in range(4):
+                tt(v(Xn, 4 * a + e, 4 * b, 4), ind(v("Xh", C * e, C * e + C), v("La", c, d)), v("V", K * e + a, K * e + b), A.add)
+            named("%dw" % t)
+            quant(v(Qn, a, b), v(Xn, 4 * a, 4 * b))
+            send(v("LQ%d" % t, a, b), v(Qn, a, b), "arr%d%d" % (t, h), True)
+            send(v("LS%d" % t, a, b), planes(v(Qn, a, b)), "arr%d%d" % (t, h), False)
+        named("%dr" % t)
+        ts(v("Lb"), v("scB", 15, K, 16) if t < R - 1 else v("l4"), off2, A.add)
         if t < R - 1:
-            jg, jc, lists = jumps(K, T.prow, "prow.lo", (T.Lna, 16 * t), lk)
-            jg(1)
-            early(t + 1)
-            jc(1)
-            jg(2)
-            early2()
-            jc(2)
+            act(v("prow", PAD, PAD + K), ind(v("cnt"), v("Lb")), AF.Identity, PAD - 1.0, 1 / UNIT)
+            to_list(lst(0, 0, K), v("prow", PAD, PAD + K), 0, K, "scJ", 0)
+            jumps(t + 1, K, ("prow", 0))
+            halve(t + 1, 0, K)
+            early(t + 1, "P7", 0, K, 8, "nE", "nC1")
         else:
-            dma("y", T.oc[:, 0:1024], Qn[:, 0:K].bitcast(u8), [qn + ".lo"], ["out.0"])
+            act(v("pout", 0, K), ind(v("cnt"), v("Lb")), AF.Identity, -1.0, 1 / UNIT)
+            named("o")
+            store(T.oc[:, 0:1024], T[Qn][:, 0:K].bitcast(u8), v(Qn, 0, K))
             for k in range(4):
-                dma("y", T.osc[4 * k:4 * k + 4, 0:K], Sn[32 * k:32 * k + 4, 0:K], [qn + ".lo"], ["out.1%d" % k])
-            mm("P0", T.QU[:], T.SU[:], Qn[:, 0:K], Sn[:, 0:K], K, ["QU", qn + ".lo"])
-            cp(T.ysb[:, 0:K], T.P0[:, 0:K], ["P0"], ["ysb.lo"])
-            dma("y", T.pl[:], T.prow[0:128:16, :], ["prow"], ["out.2"])
-            dma("y", T.y[:, 0:K], T.ysb[:, 0:K], ["ysb.lo"], ["out.3"])
-        if t == 0:
-            op("t", None, [], [], ("warr", 2 * n_in))
+                store(T.osc[4 * k:4 * k + 4, 0:K], Sn[32 * k:32 * k + 4, 0:K], planes(v(Qn, 0, K)))
+            mm("P0", v("QU"), v(Qn, 0, K))
+            cp(v("ysb", 0, K), v("P0", 0, K), "vs")
+            store(T.pl[:], T.pout[0:128:16, :], v("pout"))
+            store(T.y[:, 0:K], T.ysb[:, 0:K], v("ysb", 0, K))
         banks = ("P6", "P7", "P0", "P1")
 
-        def stage(name):
-            kind, h = name[0], int(name[1])
-            a, b = hs[h][1:3]
-            qk = qn + ".hi.%d" % h
+        def stage(kind, h):
+            a, b = hs[h][0:2]
+            named("%d%s" % (t, kind))
             if kind == "L":
+                arr = "arr%d%d" % (t, h)
                 for e in range(4):
-                    mm("P%d" % (2 + e), T.WQ[:, 128 * e:128 * e + 128], T.WS[:, 128 * e:128 * e + 128], LQ[:, a:b], LS[:, a:b], HALF, [],
-                       ("arr%d%d" % (t, h), 2 * n_in) if e == 0 else None)
+                    mm("P%d" % (2 + e), v("WQ", 128 * e, 128 * e + 128), v("LQ%d" % t, a, b), (("warr", 2 * n_in), (arr, 2 * n_in)))
+                    ops[-1][3].extend([(arr, -2), ("warr", -2)])
             elif kind == "R":
                 for e in range(4):
-                    bank = "P%d" % (2 + e)
-                    if e % 2:
-                        act(T.H[:, 4 * a + e:4 * b:4], T[bank][:, 0:HALF], AF.Relu, [bank], ["H.%d.%d" % (h, e)], scale=0.03125)
-                    else:
-                        ts(T.H[:, 4 * a + e:4 * b:4], T[bank][:, 0:HALF], 0.0, A.max, [bank], ["H.%d.%d" % (h, e)], 0.03125, A.mult)
+                    out, src = v("H", 4 * a + e, 4 * b, 4), v("P%d" % (2 + e), 0, HALF)
+                    op("vs", lambda q, out=out, src=src: S.activation(ap(out), ap(src), AF.Relu, scale=0.03125) if q == "s" else
+                       V.tensor_scalar(ap(out), ap(src), 0.0, 0.03125, A.max, A.mult), [src], [out])
             elif kind == "H":
-                quant(T.QH[:, a:b], T.SH[:, a:b], T.H[:, 4 * a:4 * b], ["H.%d" % h], ["QH.%d" % h])
+                quant(v("QH", a, b), v("H", 4 * a, 4 * b))
             elif kind == "D":
                 for e in range(4):
-                    mm(banks[e], T.QE[:, 128 * e:128 * e + 128], T.SE[:, 128 * e:128 * e + 128], T.QH[:, a:b], T.SH[:, a:b], HALF, ["QE", "QH.%d" % h])
+                    mm(banks[e], v("QE", 128 * e, 128 * e + 128), v("QH", a, b))
             elif kind == "C":
                 for e in range(4):
-                    dst, key = Xn[:, 4 * (K + a) + e:4 * (K + b):4], nk + ".hi.%d.%d" % (h, e)
-                    if e % 2:
-                        act(dst, T[banks[e]][:, 0:HALF], AF.Copy, [banks[e]], [key])
-                    else:
-                        cp(dst, T[banks[e]][:, 0:HALF], [banks[e]], [key])
+                    cp(v(Xn, 4 * (K + a) + e, 4 * (K + b), 4), v(banks[e], 0, HALF), "vs")
             elif kind == "X":
-                quant(Qn[:, K + a:K + b], Sn[:, K + a:K + b], Xn[:, 4 * (K + a):4 * (K + b)], [nk + ".hi.%d" % h], [qk])
-            elif t == R - 1 and kind == "Y":
-                mm("P2", T.QU[:], T.SU[:], Qn[:, K + a:K + b], Sn[:, K + a:K + b], HALF, ["QU", qk])
-                dma("y", T.oc[:, 4 * (K + a):4 * (K + b)], Qn[:, K + a:K + b].bitcast(u8), [qk], ["out.4%d" % h])
+                quant(v(Qn, K + a, K + b), v(Xn, 4 * (K + a), 4 * (K + b)))
+            elif t < R - 1:
+                if h == 0:
+                    early(t + 1, "P2", K, K + HALF, 9, "nF", "nE")
+                else:
+                    halve(t + 1, K, C)
+            else:
+                mm("P%d" % (2 + h), v("QU"), v(Qn, K + a, K + b))
+                store(T.oc[:, 4 * (K + a):4 * (K + b)], T[Qn][:, K + a:K + b].bitcast(u8), v(Qn, K + a, K + b))
                 if h == 1:
                     for k in range(4):
-                        dma("s" if k < 2 else "y", T.osc[4 * k:4 * k + 4, K:C], Sn[32 * k:32 * k + 4, K:C], [qn + ".hi"], ["out.5%d" % k])
-            elif t == R - 1:
-                cp(T.ysb[:, K + a:K + b], T.P2[:, 0:HALF], ["P2"], ["ysb.hi%d" % h])
-                dma("s" if h else "y", T.y[:, K + a:K + b], T.ysb[:, K + a:K + b], ["ysb.hi%d" % h], ["out.6%d" % h])
+                        store(T.osc[4 * k:4 * k + 4, K:C], Sn[32 * k:32 * k + 4, K:C], planes(v(Qn, K, C)))
+                cp(v("ysb", K + a, K + b), v("P%d" % (2 + h), 0, HALF), "vs")
+                store(T.y[:, K + a:K + b], T.ysb[:, K + a:K + b], v("ysb", K + a, K + b))
 
-        for name in STAGES.split():
-            stage(name)
+        for name in "L0 R0 H0 L1 D0 R1 C0 H1 D1 X0 Y0 C1 X1 Y1".split():
+            stage(name[0], int(name[1]))
 
-    op("g", None, ["out"], [], ("sent", sent[0]))
-    _emit(g, T, ops)
+    named("z")
+    op("g", lambda q: None, [], [], (("sent", sent[0]),))
+    ops[-1][3].extend([("out", -2)] + [(s, -2) for s in SEMAPHORES[-7:]])
+    return ops
+
+
+def rank_program(g, core, T, topo):
+    if T.rank_of(core) is not None:
+        _emit(g, T, program(g, core, T, topo))

@@ -6,21 +6,28 @@ WIN = HALF + 8
 PAD = 16
 ROW = C + PAD
 KB = 6
-LONG_FIRST = True
+NQ = (4, 2, 2)
+NJ = (2, 1, 1)
+TWICE = (0, 1, 1)
+XW = 2 * C + PAD
+CO = C + PAD
 A = AluOpType
 AF = ActivationFunctionType
 BIG = 1048576.0
 HUGE = 1e29
 HOLD = 4096.0
-UNIT = 1024.0
+UNIT = 2048.0
 NSEM, NDSEM = 112, 30
 ORDER = """
-k39 i1 k0 k1 k37 k43 k14 k6 k3 k7 k13 k69 k5 k12 k15 k60 k50 k16 k34 k68 k66 k2 k28 k8 i0 k17 k33 k31 k67 k63 k23:g i2 k9 i3 k38:g k57 k32 k35:g k42:g k22 k18 k30:g k70 u1 k61 k4 u0 k71 k27:g k20 k36 u3:s k49 p0 i5 k62 k51 k58 i4 k40:g k75 p1 p2 w3 w0 k77 k10 k76 u4 p3 u2 k73 0y0 0h0 k19 k52 k81 k59 k72 u5 k78 k25 k74 k65 0s0 k56 k48 k54 p4 0y1 k24:g k53 0s3 k64 k55 k79 k21 0j0 k80 0y2 0s5 0s4 0s6 k41:g 0s7 w4 0s8 0s11 0s9 0l0 0s10 0s1 0s13 0s14 k82 0l1 k11:g 0s15 0s16 0s21 0j1:v 0s18 0s22 0s17 0s19 0s23 0s24 0h2:s 0h7:s 0l2 0s27 0h6 0l3 0j2 k44:g k29 0s28 0s29 0h3 0s30 0s2 0s26 0s31 0l4 0s32 k26 0s20 0s33 0l5 0s34 0j3:v 0s35 0s36 0s37 0s25 w1 0s38 0l6 0l7 0h4:s 0s12 k47 0s39 0s40 0h1:s k45 0s41 0j4 0s42 0s44 w2 w6 0s43 0s45 0l8 0s46 0s47 0l9 0j5 w5
-0n0 0n1 0n2 0n3 0l10 0v0 0v2 0l11 0v1 0c0 0c8 0c12 0c3 0c2 0c9 0c11 0c1 0c10 0c15 0b0 0v3 0b1 0b2 0h5 0c6 0b3 0b4 0b5 0b6 k46:g 0d0:g 0a0 0c5 0c4 0c14 0d1:s 0a1 0c7 0e0 0d2:s 0a2 0c13 0d3:s 0a3 0d4:s 0c16 0a4 0e2 0d5:s 0e1 0a5 0d6:s 0p0 0d7:s 0a6 0d8:s 0a7 0e3 0a8 0p1 0g1 0d9:s 0a9 0g3 0d10:s 0a10 0g0 0p2 0d11:s 0p3 0a11 0p4 0p5 0q0 0q1 0q2 0q4 0q5 0q3 0q6 0r0 0x3 0g2 0x0 0q7 0g4 0g5 0g6 0x2 0r1 0x1 0x4 0g7 0w0 0x6 1h0:s 0w2 0x5 1h1:s 1h2:s 0x7 0w3 1y0 0w1 1y1 0r2 0r3 0L0 1j0 1l0 1l1 0L3 1h3:s 0L2 0L1 0R1 0w5 0R0:s 0w4 0L4 0L5 0R3 0L7 0R2 0H0 0L6 0R4 1j1 0D0 1y2 0R5:s 0D1 0R6 0D2 0R7:s 0C0 0C1:s 0C2:s 0H1 0D3 0C3:s 0D4 1l2 0X0 0D5 0D7 0D6 1l3 0C4 1y3 0C5:s 0C6 0C7:s 1h4 0X1
-1h5 1j2 1l4 1y4 1y5 1s0 1s3 1s4 1s5 1l5 1s6 1s2 1s7 1h6:s 1s8 1s9 1j3 1s12 1l6 1s1 1s11 1s13 1s14 1s15 1s16 1s21 1s17 1l7 1j4 1s18 1s19 1s10 1s22 1s23 1s24 1l8 1s25 1l9 1s27 1s28 1s29 1s30 1s31 1j5:v 1h7 1s32 1s33 1s34 1s35 1l10 1s36 1l11 1s37 1s38 1s39 1s20 1s26 1s40 1s41 1s42 1s44 1s43 1s45 1s46 1s47
-1n0 1n1 1n2 1n3 1v0 1c0 1v2 1v1 1c9 1v3 1b0 1b1 1d0 1b2 1a0 1d1 1c14 1c4 1d2 1c10 1a1 1c2 1c8 1c3 1c5 1a2 1c1 1c6 1c7 1d3 1c11 1e0 1d4 1a3 1c13 1a4 1c16 1d5 1c15 1c12 1e1 1d6 1a5 1p0 1a6 1g0 1d7 1e2 1g1 1p1 1g2 1d8 1a7 1a8 1g3 1d9 1p2 1e3 1p3 1d10 1a9 1a10 1g4 1d11 1g5 1p4 1g6 1a11 1q0 1p5 1g7:v 1q1 1q4 1q5 1q2 1q6 1q3 1r0 1q7 1r1 1x0 1x1 1x2 1x3 1x4 2h0:s 1w0 1w1 1w2 1L1 1x6 1R1:s 1x5 1x7 1r2 1w3 2y0 1r3 2j0:v 2l0 2h2 2l1 2y1 1w4 1L2 1L0 2j1:v 1R0:s 1R2 1L3 1R3 1w5 1L5 1R5:s 1L6 2l2 1L7 1L4 1H0 1D3 1D0 1D1 1D2 1R6 1R4 1R7:s 2y2 1C3:s 2l3 1C1:s 1H1 1D5 1C2:s 1D6 1D7 1C0 1X0 1D4 2j2 1C6:s 1C5 1C4 1C7:s 1X1
-2y3 2y4 2y5 2s0 2l4 2h7 2s1 2l5 2s3 2s5 2j3 2s4 2s6 2s8 2s7 2l6 2s11 2s9 2s13 2l7 2s14 2s12 2s15 2s16 2s18 2s21 2s17 2s19 2h1:s 2h5:s 2s2 2s10 2j4 2s22 2s23 2s24 2s25 2l8 2h4 2s27 2s28 2s29 2s30 2s31 2s32 2s20 2s33 2s34 2s35 2l9 2j5 2s36 2s37 2h6:s 2s38 2s39 2s26 2s40 2l10 2s41 2s42 2l11 2s44 2s43 2s45 2s46 2s47
-2n0 2n1 2n2 2n3 2v0 2c0 2c3 2c4 2c10 2c5 2c16 2c2 2v2 2c8 2v1 2v3 2b0 2b1 2d0 2b2 2c6 2a0 2d1 2c7 2d2 2a1 2a2 2c12 2c1 2d3 2c14 2e0 2h3:s 2d4 2a3 2c9 2a4 2d5 2c13 2e1 2d6 2a5 2a6 2d7 2c15 2c11 2e2 2p0 2p1 2d8 2a7 2g1 2g2 2a8 2g3 2d9 2g0 2e3 2p3 2p2 2d10 2a9 2a10 2d11 2p4 2a11 2q0 2p5 2q4 2g7:v 2g6:v 2q1 2q5 2q2 2q6 2q3 2q7 2x2 2x0 2x1 2x3 2g5 2x5 2w0 2w2 2x7 2g4 2w1 2x4 2x6 2w3 2r0 2w5 2w4 o4 o1 o5 o2 2L1 2R1 2L0 2L3 2L2 o0 2R0 2L4 o6:s 2L5 2r1 o7:s 2R2:s 2R3 2L7 2R7:s o8 2L6 2H0 2D1 2R4 2R5 2C1:s 2D2 2R6 2D0 2C0:s 2C2 2D3 2H1 2D4 2C3:s 2X0 2D7 2D5 2C7 2Y1:s 2C4 2C5:s 2D6 2C6:s o3 2Y0 2Y2 2Y3:s 2X1 2Y7 2Y5 2Y4 2Y10:s 2Y8 2Y9 2Y6 2Y11:s z0
+k27 i1 k33 k0 k34 k36 i0 k13 k15 k14 k39 k7 i2 k3 k37 k1 k72 k5 k16 k6 k47 k75:g k49 u0 k87 k66 k69 k63 k17 k2 k74 k19 i3 k8 k9 k26:g k40:g k55 k30:g k18 k20 k4 k67 k73 k59 k43:g k28 k65 k81 k24 k25:g k38:g k68 k42 k56 p0 k21 k32 w3 w2 k61 w0 p1 u1 u3:s 0h0:s 0h14:s k70 w1 k76 k35 k82 k64 u4 0h4:s p2 u2 0y0 u5 k58 k77 k79 k22 k71 k83 k54 0h6 p3 k78 0y1 0s0 0s3 i4 w4 k84 k41:g 0y2 0h5:s 0h1 k80 0s4 0s5 k85 k12:g 0h10 0s6 k57 k60 0h15:s k23 p5 0s8 0s7 0s1 p4:v k62 0s9 0s11 0s13 k48:g 0h3 0s14 0h13 0h11 k10:g 0s15 0s2 0s10 0j0 0h12 0s16 0s18 0l0 0j1 k44:g 0s21 k86 0s19 0s12 k31 0l1 0j2 0l2 0s22 0s17 0l3 0s23 0s24 0l4 0s26 k46:g 0l5 k45:g 0s27 0h2 0s28 0s29 0s30 0j3 0l6 w6 0l7 0j4 0s31 0s32 0h8:s 0s20 0j5 0s33 0s34 0s35 0l8 0l9 0j6 0l10 0h7 0s36 0l11 i5 0s25 w5 0j7 0s37 0s38 0l12 0s39 k29:g k11:g k53:g k88 0l13 0j8 0l14 0s40 0s41 k50 0l15 0s42 0s44 0j9 0l16 0s43 0l17 0j10 0h9:s 0s45 0s46 0s47
+0l18 0n0 0n1 0n2 0l20 0n3 0l19 0l21 0j11 0v0 0m0 0v2 0v1 0v6 0d0:s 0v4 0v3 0d1:s 0c0 0c5 0v5 0d2:s 0a0 0c12 0d4:s 0a1 0c1 0v7 0a2 k52:g 0c3 0d5:s 0c10 0a4 0c8 0l22 0d3:g 0d8:s 0c6 0a5 0c13 0c4 0d9:s 0c2 0a3 0d7:s 0a8 0c7 0d6:g 0a6 0d10:s 0l23 0c11 0a9 0a7 k51:g 0e0 0a10 0d12:g 0a12 0d13:s 0a13 0c9 0e1 0d11:s 0a11 0d15:g 0c16 0d14:s 0a14 0c15 0d16:s 0a16 0c14 0e2 0d17:s 0p4 0a17 0d18:s 0g0 0b0 0g2 0a18 0b1 0a15 0b2 0p1 0e3 0g3 0d19 0p2 0g1 0b3 0p0 0a19 0b4 0p3 0p8 0p11 0p9 0b5 0p12 0p5 0b6 0p13 0p10 0g7 0p6 0p7 0q0 0q4 0q1 0q5 0q2 0q6 0q3 0q7 0x3 0x0 0g4 0x2 0x1 0g6 0x6 0w0 0g5 0w2 0x7 0x4 0x5 0w3 0r0 0w1
+0L2 0L3 0w5 0r1 0r3 0L1 0r2 0w4 0R1:s 0R3 0L0 0R0:s 1y0 1y1 0L7 0R7:s 0r4 0R2 0H0 1y2 0L5 0R5 0L6 0R6:s 0L4 0D0 0D1 0R4 1j0 0H1 0D2 0D3 1h5 1h3 1h0 0C3:s 0C2:s 1h2:s 0C1 0C0 0D7 0D6 0C6:s 0C7 0D5 0D4 0C4:s 0C5 0X0 1y3 0X1
+1s0 1l0 1h8:s 1l1 1y4 1y5 1s3 1s4 1s5 1s6 1h6 1h4:s 1s1 1j1 1s8 1s7 1h7:s 1s11 1s10 1s9 1l2 1h10 1h11 1s13 1h1:s 1h12:s 1s14 1h15 1s2 1s15 1s16 1s21 1s18 1l3 1h9 1s19 1s12 1s17 1s22 1h14 1s23 1s24 1s20 1h13 1j2 1s26 1s27 1s28 1s29 1s30 1s31 1l4 1l5 1s25 1j3 1s32 1s33 1s34 1l6 1l7 1s35 1j4 1s36 1s37 1s38 1s39 1l8 1l9 1s40 1s41 1s42 1j5 1s44 1l10 1s43 1s45 1s46 1s47
+1n0 1n1 1n2 1n3 1v0 1c0 1c4 1c2 1c1 1c7 1c5 1c8 1c3 1c15 1v3 1v2 1v1 1c13 1v5 1v4 1a0 1a1 1d0 1d1 1a2 1a3 1d2 1l11 1c6 1e0 1d3 1c10 1a4 1c12 1a5 1d4 1e1 1c14 1c9 1c11 1c16 1e2 1d5 1p4 1a6 1a7 1d6 1e3 1p5 1p1 1a8 1d7:s 1a9 1b0 1p8 1p11 1p2 1p0 1p7 1p9 1b1 1p3 1p12 1b2 1p6 1p10 1p13 1g7 1g0 1q0 1q4 1g5 1q1 1q5 1q2 1q6 1g2 1q3 1q7 1x0 1g1 1x1 1g6 1g3 1x3 1x2 1g4 1x4 1w0 1w1 1w2 1x5 1x6 1x7 1r0 1w3
+1r1 2h4:s 1r2 1r3 1r4 2j0 2y0 1L1 1R1 1L2 1L3 1R3 1R2 1w5 1w4 1L0 1L6 1R0 2l0 2h2:s 1L5 1H0 2h3 2y1 2y2 1R6 1R5 1L4 1R4:s 1L7 1R7 2h0 1D0 1D2 1H1 2l1 1C2:s 1D3 1C3:s 1D1 1C1 1C0 1D6 1C6:s 1D5 1C5:s 2h1 1D7 1C7:s 2h5 1X0 1D4 1C4 2h9:s 1X1
+2y3 2s0 2h6 2y4 2h10 2h12 2s3 2h8:s 2h14 2s1 2y5 2s2 2h11 2s5 2s4 2s6 2s7 2h7:s 2s8 2s13 2s10 2s9 2s11 2s12 2j1 2h15:s 2s14 2s15 2s16 2s17 2s18 2s19 2l2 2h13 2s21 2l3 2j2 2s22 2s23 2s24 2l4 2l5 2s27 2s28 2s29 2s30 2j3 2l6 2s31 2l7 2s25 2s32 2s33 2s34 2j4 2l8 2l9 2s20 2s35 2s36 2s37 2j5 2s38 2s39 2l10 2s26 2s40 2s41 2s42 2s44 2s43 2s45 2s46 2s47
+2n0 2n1 2n2 2n3 2v0 2c0 2v3 2c4 2c7 2c6 2c15 2c3 2v1 2v2 2v5 2v4 2a0 2a1 2c5 2c16 2d0 2d1 2a2 2a3 2d2 2c8 2l11 2c2 2c1 2e0 2d3 2a4 2a5 2d4 2c10 2c13 2c11 2c12 2c14 2e1 2c9 2e2 2d5 2p1 2a6 2d6:s 2a7 2d7:s 2e3 2p2 2a8 2a9 2p11 2b0 2p3 2p12 2b1 2p4 2p5 2p8 2p9 2b2 2p13 2p6 2p0 2p10 2q0 2p7 2q4 2q1 2q5 2q2 2q6 2q3 2q7 2g5 2g3 2x3 2g2 2x2 2g1 2x1 2g0 2x0 2g6 2x6 2g4 2w0 2g7 2w1 2x4 2x7 2x5 2r0 2r1 2w3
+o5 2w2 2L3 2L0 o6:s 2L2 2r2 2R0 2R2 2L1 2w5 2R1:s 2R3 2w4 2L4 2H0 2R4 2L6 2R6:s 2L5 2L7 2R7 2R5:s 2D0 2C0:s 2D2 2C2 o8 o7 2D1 2D3 2C1:s 2H1 o0 2C3:s 2X0 2D4 2Y1:s 2D6 2C4:s o3 o1 2C6 o2 2D5 2D7 o4 2C5:s 2Y0 2Y2:s 2Y3:s 2C7 2X1 2Y8:s 2Y9:s 2Y5:s 2Y7:s 2Y4 2Y10:s 2Y6 2Y11 z0
 """
 
 SCRATCH = {}
@@ -38,21 +45,21 @@ for _t in range(R + 1):
 for _t in range(R):
     _sb("LQ%d" % _t, K, "float8_e4m3fn_x4")
     _sb("LS%d" % _t, K, "uint8")
-for _n, _w in (("U", 512), ("E", 2048), ("H", 1024), ("Xh", 4 * C), ("V", 1024), ("zer", C), ("junk", 10 * C), ("gtb", C + 2),
-               ("geb", C), ("bnd", C), ("cnt", 2 * C + 16), ("one", C), ("z", C), ("jk", 16 * WIN), ("al", C), ("M", (KB + 1) * ROW),
+for _n, _w in (("U", 512), ("E", 2048), ("H", 1024), ("Xh", 4 * XW), ("V", 1024), ("zer", C), ("junk", 10 * C), ("gtb", C + 2),
+               ("geb", C), ("bnd", C), ("cnt", CO + C + 1), ("one", C), ("z", C), ("jk", 16 * WIN), ("al", C), ("M", (KB + 1) * ROW),
                ("Md", KB * C)):
     _sb(_n, _w, "bfloat16")
 for _n, _s, _w in (("QU", "SU", 128), ("QR", "SR", 128), ("WL", "WSL", 512), ("WQ", "WS", 512), ("QE", "SE", 512), ("QH", "SH", K)):
     _sb(_n, _w, "float8_e4m3fn_x4")
     _sb(_s, _w, "uint8")
-for _n, _w in (("iot", ROW), ("t16", 48), ("yy", K), ("K1", C), ("Pl", C), ("D", C), ("scJ", (KB + 1) * C), ("scP", K), ("scB", K),
-               ("rows", (KB + 1) * ROW),
-               ("prow", ROW), ("pout", C), ("pe", K), ("Br", K), ("ysb", C), ("sm", 32), ("F", 9 * 32), ("Tt", 66), ("Tb", 8 * 34),
+for _n, _w in (("iot", ROW), ("t16", 48), ("yy", K), ("K1", C), ("Pl", C), ("D", C), ("scJ", (KB + 1) * C), ("scP", 2 * K), ("Ng", C),
+               ("Gr", K), ("scB", K), ("rows", (KB + 1) * ROW),
+               ("prow", ROW), ("pout", C), ("pe", 2 * K), ("Br", K), ("ysb", C), ("sm", 32), ("F", 9 * 32), ("Tt", 66), ("Tb", 8 * 34),
                ("o", 12 * 34), ("Dt", 5 * 34), ("G2t", 34), ("Tat", 34), ("Sgt", 34), ("nC1", 64), ("nE", 64), ("nF", 64), ("nC", 64),
-               ("Msk", 32), ("l1", 32), ("l2", 32), ("l3", 3 * 32), ("l4", 16), ("tmp", 8 * 34), ("TB", 3 * 33), ("TM", 3 * 33), ("f", 10),
+               ("Msk", 32), ("l1", 32), ("l2", 32), ("l3", 3 * 32), ("tmp", 8 * 34), ("TB", 3 * 33), ("TM", 3 * 33), ("f", 10),
                ("Kc", 8), ("ec", 16), ("e2", 16), ("nb", 16), ("et", 16)):
     _sb(_n, _w, "float32")
-for _n, _w in (("LJ", (KB + 1) * 32), ("Lb", 16), ("La", 16), ("el", 16), ("pel", 16), ("offU", 8), ("Lr", 32)):
+for _n, _w in (("LJ", (KB + 1) * 32), ("Lb", 16), ("La", 16), ("el", 16), ("pel", 32), ("offU", 8), ("Lr", 32)):
     _sb(_n, _w, "uint16")
 for _n, _w in (("pt", 32), ("pi", 4), ("oi", 8)):
     _sb(_n, _w, "int32")
@@ -87,11 +94,12 @@ def _touched(xs):
 
 
 def _needs(ops):
-    out = []
+    out, past = [], {}
     for i, o in enumerate(ops):
-        out.append([j for j in range(i)
-                    if any(a == b and m & n for a, m in o[3] + o[4] for b, n in ops[j][4])
-                    or any(a == b and m & n and (w or m == -1) for w, xs in ((0, o[3]), (1, o[4])) for a, m in xs for b, n in ops[j][3])])
+        out.append(sorted({j for w in (0, 1) for a, m in o[3 + w] for j, n, x in past.get(a, ()) if m & n and (w or x or m == -1)}))
+        for w in (0, 1):
+            for a, m in o[3 + w]:
+                past.setdefault(a, []).append((i, m, w))
     return out
 
 
@@ -185,15 +193,15 @@ def program(g, core, T, topo):
         flag = {} if SCRATCH[out[0]][2] == "int32" else {"allow_small_or_imprecise_dtypes": True}
         op("g", lambda q: g.iota(ap(out), pattern, base, cm, **flag), [], [out])
 
-    def ramp(out, base):
+    def ramp(out, base, step=1):
         n = out[2] - out[1]
 
         def fn(q):
             if q == "g":
-                return g.iota(ap(out), [[1, n]], base, 0, allow_small_or_imprecise_dtypes=True)
+                return g.iota(ap(out), [[step, n]], base, 0, allow_small_or_imprecise_dtypes=True)
             if q == "s":
-                return S.activation(ap(out), T.iot[:, 0:n], AF.Identity, bias=float(base))
-            return V.tensor_scalar(ap(out), T.iot[:, 0:n], float(base), None, A.add)
+                return S.activation(ap(out), T.iot[:, 0:n], AF.Identity, bias=float(base), scale=float(step))
+            return V.tensor_scalar(ap(out), T.iot[:, 0:n], float(step), float(base), A.mult, A.add)
         op("svg", fn, [v("iot")], [out])
 
     def fill(out, c):
@@ -230,7 +238,7 @@ def program(g, core, T, topo):
         sent[0] += n_out
 
     r_, r8, hf, off = col("sm", 0), col("sm", 1), col("sm", 2), col("sm", 3)
-    tau1, c1, m1, off2 = col("sm", 4), col("sm", 5), col("tmp", 39), col("sm", 11)
+    tau1, c1, m1, off1, off2 = col("sm", 4), col("sm", 5), col("tmp", 39), col("sm", 10), col("sm", 11)
 
     def lst(k, a, b):
         return v("LJ", 32 * k + a // 16, 32 * k + b // 16)
@@ -242,17 +250,19 @@ def program(g, core, T, topo):
 
     def jumps(t, w, row0):
         for k in range(1, KB + 1):
-            a = 2 ** KB if k == KB else 0
             src = row0 if k == 1 else ("rows", ROW * (k - 1))
-            named("%dj" % t)
-            cp(v("rows", ROW * k + PAD + a, ROW * k + PAD + w), ind(v(src[0], src[1], src[1] + PAD + w), lst(k - 1, a, w)), "sv")
-            named("%dl" % t)
-            to_list(lst(k, a, w), v("rows", ROW * k + PAD + a, ROW * k + PAD + w), a, w, "scJ", C * k)
+            for h in range(NJ[t]):
+                a, b = max(h * w // NJ[t], 2 ** KB if k == KB else 0), (h + 1) * w // NJ[t]
+                named("%dj" % t)
+                cp(v("rows", ROW * k + PAD + a, ROW * k + PAD + b), ind(v(src[0], src[1], src[1] + PAD + b), lst(k - 1, a, b)), "sv")
+                named("%dl" % t)
+                to_list(lst(k, a, b), v("rows", ROW * k + PAD + a, ROW * k + PAD + b), a, b, "scJ", C * k)
 
     def halve(t, a, b):
         named("%dh" % t)
         for e in range(4):
-            cp(v("Xh", C * e + a, C * e + b), v("X%d" % t, 4 * a + e, 4 * b, 4), "vs", 0.5)
+            cp(v("Xh", XW * e + CO + a, XW * e + CO + b), v("X%d" % t, 4 * a + e, 4 * b, 4), "vs", 0.5)
+            cp(v("Xh", XW * e + C - 1 - a, XW * e + C - 1 - b, -1), v("X%d" % t, 4 * a + e, 4 * b, 4), "vs", 0.5)
 
     def early(t, bank, a, b, j, out, bounds):
         named("%dy" % t)
@@ -281,6 +291,7 @@ def program(g, core, T, topo):
     iota(v("tmp", 136, 170), [[0, 17], [1, 2]], 3)
     ramp(v("prow", PAD + K, ROW), PAD)
     ramp(v("pout", K, C), 0)
+    ramp(v("Ng"), -K - PAD - 1, -1)
     for j, m in enumerate((15, 7, 16)):
         ts(col("pi", j + 1), col("pi", 0), m, A.bitwise_and)
     cp(v("sm", 0, 3), v("pi", 1, 4))
@@ -289,7 +300,8 @@ def program(g, core, T, topo):
     ts(v("Lr"), v("l1"), 0.0, A.mult, r_, A.add)
     cp(v("K1"), ind(v("t16", 32, 48), v("Lr")), "sv")
     ts(off, r_, -HOLD, A.mult, 15 * HOLD, A.add)
-    ts(off2, off, 1.0, A.add)
+    ts(off1, off, float(K + CO), A.add)
+    ts(off2, off, K + CO + 1.0, A.add)
     ts(v("l2"), v("l2"), r_, A.add)
     for k in range(1, KB):
         fill(v("rows", ROW * k, ROW * k + PAD), 0.0)
@@ -300,7 +312,8 @@ def program(g, core, T, topo):
     tt(v("l3", 32, 64), v("l3", 0, 32), v("l2"), A.not_equal)
     tt(v("l3", 64, 96), v("l3", 0, 32), v("l3", 32, 64), A.mult)
     cp(lst(0, 0, C), v("l3", 64, 96))
-    cp(v("rows", PAD, ROW), ind(v("iot"), lst(0, 0, C)), "sv")
+    for a in (0, K):
+        cp(v("rows", PAD + a, PAD + a + K), ind(v("iot"), lst(0, a, a + K)), "sv")
     jumps(0, C, ("rows", 0))
     named("k")
     fill(v("one"), 1.0)
@@ -310,8 +323,10 @@ def program(g, core, T, topo):
     for nm in ("Tt", "Tb", "Dt"):
         fill(v(nm), 0.0)
     fill(v("gtb", C, C + 2), 0.0)
-    fill(col("cnt", 0), 0.0)
-    fill(v("cnt", C + 1), (1 - PAD) * UNIT)
+    fill(col("cnt", CO), 0.0)
+    fill(v("cnt", 0, CO), -C * UNIT)
+    for e in range(4):
+        fill(v("Xh", XW * e + C, XW * e + CO), 0.0)
     for k in range(KB + 1):
         fill(v("M", ROW * k, ROW * k + PAD), -K - UNIT)
     fill(col("Tat", 32), -1.5)
@@ -420,34 +435,32 @@ def program(g, core, T, topo):
         ts(v("gtb", 0, C), v("z"), thr, A.is_gt, -UNIT, A.mult)
         ts(v("geb"), v("z"), thr, A.is_ge, UNIT, A.mult)
         scan(v("bnd", C - 1, -1, -1), v("gtb", C, 0, -1), v("zer"), UNIT * K, A.add, A.add)
-        scan(v("cnt", 1, C + 1), v("geb"), v("bnd"), 0.0, A.add, A.min)
+        m = K if t == 0 else C
+        scan(v("cnt", CO + 1, CO + 1 + m), v("geb", 0, m), v("bnd", 0, m), 0.0, A.add, A.min)
+        if m < C:
+            named("%dm" % t)
+            scan(v("cnt", CO + 1 + m), v("geb", m), v("bnd", m), col("cnt", CO + m), A.add, A.min)
         w = C if t == 0 else K
-        B = 2 ** KB
+        B, m = 2 ** KB, ROW * (KB - 1)
+        pieces = [(h * w // NQ[t], (h + 1) * w // NQ[t]) for h in range(NQ[t])]
         named("%dv" % t)
-        for h in range(2):
-            a, b = h * w // 2, (h + 1) * w // 2
-            scan(v("al", a, b), v("cnt", a + 1, b + 1), v("cnt", a, b), 0.0, A.max, A.subtract)
+        for a, b in pieces:
+            scan(v("al", a, b), v("cnt", CO + a + 1, CO + b + 1), v("cnt", CO + a, CO + b), 0.0, A.max, A.subtract)
             scan(v("M", PAD + b - 1, PAD + a - 1, -1), v("Pl", b - 1, a - 1, -1), v("al", b - 1, a - 1, -1), BIG, A.min, A.add)
-
-        def blocks(m):
-            named("%db" % t)
-            for a in range(B, w, B):
-                tt(v("M", m + PAD + a, m + PAD + a + B), ind(v("M", m, m + PAD + a), lst(KB, a, a + B)), v("M", m + PAD + a, m + PAD + a + B), A.max)
-
-        if LONG_FIRST:
-            blocks(0)
-        for j in range(KB):
-            k = KB - 1 - j if LONG_FIRST else j
-            for h in range(2):
-                a, b = h * w // 2, (h + 1) * w // 2
+            if TWICE[t]:
+                scan(v("Md", b - 1, a - 1, -1), v("Pl", b - 1, a - 1, -1), v("al", b - 1, a - 1, -1), BIG, A.min, A.add)
+        for j in range(KB - 1):
+            for a, b in pieces:
                 named("%dd" % t)
-                cp(v("Md", C * j + a, C * j + b), v("M", ROW * j + PAD + a, ROW * j + PAD + b), "vsg")
+                if j or not TWICE[t]:
+                    cp(v("Md", C * j + a, C * j + b), v("M", ROW * j + PAD + a, ROW * j + PAD + b), "vsg")
                 named("%da" % t)
-                tt(v("M", ROW * (j + 1) + PAD + a, ROW * (j + 1) + PAD + b), ind(v("M", ROW * j, ROW * j + PAD + b), lst(k, a, b)), v("Md", C * j + a, C * j + b), A.max)
-        if not LONG_FIRST:
-            blocks(ROW * KB)
+                tt(v("M", ROW * (j + 1) + PAD + a, ROW * (j + 1) + PAD + b), ind(v("M", ROW * j, ROW * j + PAD + b), lst(j + 1, a, b)), v("Md", C * j + a, C * j + b), A.max)
+        named("%db" % t)
+        for a in range(B, w, B):
+            tt(v("M", m + PAD + a, m + PAD + a + B), ind(v("M", m, m + PAD + a), lst(KB, a, a + B)), v("M", m + PAD + a, m + PAD + a + B), A.max)
         named("%dc" % t)
-        scan(v("yy", K - 1, -1, -1), v("cnt", C - 1, -1, -2), v("cnt", C, 0, -2), BIG, A.min, A.add)
+        scan(v("yy", K - 1, -1, -1), v("cnt", CO + C - 1, CO, -2), v("cnt", CO + C, CO, -2), BIG, A.min, A.add)
         for i in range(16):
             act(v("jk", WIN * i, WIN * i + WIN), v("yy", 8 * i, 8 * i + WIN), AF.Sign, col("nb", i), -1.0, col("ec", i))
         for h in range(2):
@@ -456,33 +469,38 @@ def program(g, core, T, topo):
             tt(v("e2", c, d), v("ec", c, d), v("et", c, d), A.add)
             ts(v("el", c, d), v("e2", c, d), off, A.add)
             named("%dp" % t)
-            cp(v("pe", a, b), ind(v("rows" if t == 0 else "prow", PAD, ROW), v("el", c, d)), "sv")
-            to_list(v("pel", c, d), v("pe", a, b), a, b, "scP", 0)
+            cp(v("Gr", a, b), ind(v("Ng"), v("el", c, d)), "sv")
+            for j in range(2):
+                src = (("rows" if t == 0 else "prow", 0), ("rows", ROW))[j]
+                cp(v("pe", K * j + a, K * j + b), ind(v(src[0], src[1] + PAD, src[1] + ROW), v("el", c, d)), "sv")
+                to_list(v("pel", 16 * j + c, 16 * j + d), v("pe", K * j + a, K * j + b), a, b, "scP", K * j)
             named("%dg" % t)
             for e in range(4):
-                cp(v("V", K * e + a, K * e + b), ind(v("Xh", C * e, C * e + C), v("el", c, d)), "sv")
+                cp(v("V", K * e + a, K * e + b), ind(v("Xh", XW * e + CO, XW * e + XW), v("el", c, d)), "sv")
             named("%dq" % t)
-            act(v("Br", a, b), ind(v("M", ROW * KB, ROW * KB + PAD + w), v("pel", c, d)), AF.Abs, float(K))
+            for j in range(2):
+                tt(v("Br", a, b), ind(v("M", m, m + PAD + w), v("pel", 16 * j + c, 16 * j + d)), v("Br" if j else "Gr", a, b), A.max)
             to_list(None, v("Br", a, b), a, b, "scB", 0)
-            tt(v("l4", c, d), v("scB", a + 15, b, 16), v("e2", c, d), A.min)
-            ts(v("La", c, d), v("l4", c, d), off, A.add)
+            ts(v("La", c, d), v("scB", a + 15, b, 16), off1, A.add)
             named("%dx" % t)
             for e in range(4):
-                tt(v(Xn, 4 * a + e, 4 * b, 4), ind(v("Xh", C * e, C * e + C), v("La", c, d)), v("V", K * e + a, K * e + b), A.add)
+                tt(v(Xn, 4 * a + e, 4 * b, 4), ind(v("Xh", XW * e, XW * e + XW), v("La", c, d)), v("V", K * e + a, K * e + b), A.add)
             named("%dw" % t)
             quant(v(Qn, a, b), v(Xn, 4 * a, 4 * b))
             send(v("LQ%d" % t, a, b), v(Qn, a, b), "arr%d%d" % (t, h), True)
             send(v("LS%d" % t, a, b), planes(v(Qn, a, b)), "arr%d%d" % (t, h), False)
         named("%dr" % t)
-        ts(v("Lb"), v("scB", 15, K, 16) if t < R - 1 else v("l4"), off2, A.add)
+        ts(v("Lb"), v("scB", 15, K, 16), off2, A.add)
         if t < R - 1:
-            act(v("prow", PAD, PAD + K), ind(v("cnt"), v("Lb")), AF.Identity, PAD - 1.0, 1 / UNIT)
+            act(v("prow", PAD, PAD + K), ind(v("cnt"), v("Lb")), AF.Relu, PAD - 1.0, 1 / UNIT)
+            cp(v("rows", ROW + PAD + K, 2 * ROW), v("prow", PAD, PAD + K), "svg")
             to_list(lst(0, 0, K), v("prow", PAD, PAD + K), 0, K, "scJ", 0)
             jumps(t + 1, K, ("prow", 0))
             halve(t + 1, 0, K)
             early(t + 1, "P7", 0, K, 8, "nE", "nC1")
         else:
-            act(v("pout", 0, K), ind(v("cnt"), v("Lb")), AF.Identity, -1.0, 1 / UNIT)
+            act(v("pe", 0, K), ind(v("cnt"), v("Lb")), AF.Abs, -1.0, 1 / UNIT)
+            tt(v("pout", 0, K), v("pe", 0, K), v("iot", 0, K), A.min)
             named("o")
             store(T.oc[:, 0:1024], T[Qn][:, 0:K].bitcast(u8), v(Qn, 0, K))
             for k in range(4):
@@ -491,10 +509,10 @@ def program(g, core, T, topo):
             cp(v("ysb", 0, K), v("P0", 0, K), "vs")
             store(T.pl[:], T.pout[0:128:16, :], v("pout"))
             store(T.y[:, 0:K], T.ysb[:, 0:K], v("ysb", 0, K))
-        banks = ("P6", "P7", "P0", "P1")
 
         def stage(kind, h):
             a, b = hs[h][0:2]
+            banks = (("P6", "P7", "P0", "P1"), ("P2", "P3", "P4", "P5"))[h]
             named("%d%s" % (t, kind))
             if kind == "L":
                 arr = "arr%d%d" % (t, h)
@@ -518,16 +536,16 @@ def program(g, core, T, topo):
                 quant(v(Qn, K + a, K + b), v(Xn, 4 * (K + a), 4 * (K + b)))
             elif t < R - 1:
                 if h == 0:
-                    early(t + 1, "P2", K, K + HALF, 9, "nF", "nE")
+                    early(t + 1, "P6", K, K + HALF, 9, "nF", "nE")
                 else:
                     halve(t + 1, K, C)
             else:
-                mm("P%d" % (2 + h), v("QU"), v(Qn, K + a, K + b))
+                mm("P%d" % (6 + h), v("QU"), v(Qn, K + a, K + b))
                 store(T.oc[:, 4 * (K + a):4 * (K + b)], T[Qn][:, K + a:K + b].bitcast(u8), v(Qn, K + a, K + b))
                 if h == 1:
                     for k in range(4):
                         store(T.osc[4 * k:4 * k + 4, K:C], Sn[32 * k:32 * k + 4, K:C], planes(v(Qn, K, C)))
-                cp(v("ysb", K + a, K + b), v("P%d" % (2 + h), 0, HALF), "vs")
+                cp(v("ysb", K + a, K + b), v("P%d" % (6 + h), 0, HALF), "vs")
                 store(T.y[:, K + a:K + b], T.ysb[:, K + a:K + b], v("ysb", K + a, K + b))
 
         for name in "L0 R0 H0 L1 D0 R1 C0 H1 D1 X0 Y0 C1 X1 Y1".split():

@@ -19,15 +19,15 @@ HOLD = 4096.0
 UNIT = 2048.0
 NSEM, NDSEM = 112, 30
 ORDER = """
-k27 i1 k33 k0 k34 k36 i0 k13 k15 k14 k39 k7 i2 k3 k37 k1 k72 k5 k16 k6 k47 k75:g k49 u0 k87 k66 k69 k63 k17 k2 k74 k19 i3 k8 k9 k26:g k40:g k55 k30:g k18 k20 k4 k67 k73 k59 k43:g k28 k65 k81 k24 k25:g k38:g k68 k42 k56 p0 k21 k32 w3 w2 k61 w0 p1 u1 u3:s 0h0:s 0h14:s k70 w1 k76 k35 k82 k64 u4 0h4:s p2 u2 0y0 u5 k58 k77 k79 k22 k71 k83 k54 0h6 p3 k78 0y1 0s0 0s3 i4 w4 k84 k41:g 0y2 0h5:s 0h1 k80 0s4 0s5 k85 k12:g 0h10 0s6 k57 k60 0h15:s k23 p5 0s8 0s7 0s1 p4:v k62 0s9 0s11 0s13 k48:g 0h3 0s14 0h13 0h11 k10:g 0s15 0s2 0s10 0j0 0h12 0s16 0s18 0l0 0j1 k44:g 0s21 k86 0s19 0s12 k31 0l1 0j2 0l2 0s22 0s17 0l3 0s23 0s24 0l4 0s26 k46:g 0l5 k45:g 0s27 0h2 0s28 0s29 0s30 0j3 0l6 w6 0l7 0j4 0s31 0s32 0h8:s 0s20 0j5 0s33 0s34 0s35 0l8 0l9 0j6 0l10 0h7 0s36 0l11 i5 0s25 w5 0j7 0s37 0s38 0l12 0s39 k29:g k11:g k53:g k88 0l13 0j8 0l14 0s40 0s41 k50 0l15 0s42 0s44 0j9 0l16 0s43 0l17 0j10 0h9:s 0s45 0s46 0s47
-0l18 0n0 0n1 0n2 0l20 0n3 0l19 0l21 0j11 0v0 0m0 0v2 0v1 0v6 0d0:s 0v4 0v3 0d1:s 0c0 0c5 0v5 0d2:s 0a0 0c12 0d4:s 0a1 0c1 0v7 0a2 k52:g 0c3 0d5:s 0c10 0a4 0c8 0l22 0d3:g 0d8:s 0c6 0a5 0c13 0c4 0d9:s 0c2 0a3 0d7:s 0a8 0c7 0d6:g 0a6 0d10:s 0l23 0c11 0a9 0a7 k51:g 0e0 0a10 0d12:g 0a12 0d13:s 0a13 0c9 0e1 0d11:s 0a11 0d15:g 0c16 0d14:s 0a14 0c15 0d16:s 0a16 0c14 0e2 0d17:s 0p4 0a17 0d18:s 0g0 0b0 0g2 0a18 0b1 0a15 0b2 0p1 0e3 0g3 0d19 0p2 0g1 0b3 0p0 0a19 0b4 0p3 0p8 0p11 0p9 0b5 0p12 0p5 0b6 0p13 0p10 0g7 0p6 0p7 0q0 0q4 0q1 0q5 0q2 0q6 0q3 0q7 0x3 0x0 0g4 0x2 0x1 0g6 0x6 0w0 0g5 0w2 0x7 0x4 0x5 0w3 0r0 0w1
-0L2 0L3 0w5 0r1 0r3 0L1 0r2 0w4 0R1:s 0R3 0L0 0R0:s 1y0 1y1 0L7 0R7:s 0r4 0R2 0H0 1y2 0L5 0R5 0L6 0R6:s 0L4 0D0 0D1 0R4 1j0 0H1 0D2 0D3 1h5 1h3 1h0 0C3:s 0C2:s 1h2:s 0C1 0C0 0D7 0D6 0C6:s 0C7 0D5 0D4 0C4:s 0C5 0X0 1y3 0X1
-1s0 1l0 1h8:s 1l1 1y4 1y5 1s3 1s4 1s5 1s6 1h6 1h4:s 1s1 1j1 1s8 1s7 1h7:s 1s11 1s10 1s9 1l2 1h10 1h11 1s13 1h1:s 1h12:s 1s14 1h15 1s2 1s15 1s16 1s21 1s18 1l3 1h9 1s19 1s12 1s17 1s22 1h14 1s23 1s24 1s20 1h13 1j2 1s26 1s27 1s28 1s29 1s30 1s31 1l4 1l5 1s25 1j3 1s32 1s33 1s34 1l6 1l7 1s35 1j4 1s36 1s37 1s38 1s39 1l8 1l9 1s40 1s41 1s42 1j5 1s44 1l10 1s43 1s45 1s46 1s47
-1n0 1n1 1n2 1n3 1v0 1c0 1c4 1c2 1c1 1c7 1c5 1c8 1c3 1c15 1v3 1v2 1v1 1c13 1v5 1v4 1a0 1a1 1d0 1d1 1a2 1a3 1d2 1l11 1c6 1e0 1d3 1c10 1a4 1c12 1a5 1d4 1e1 1c14 1c9 1c11 1c16 1e2 1d5 1p4 1a6 1a7 1d6 1e3 1p5 1p1 1a8 1d7:s 1a9 1b0 1p8 1p11 1p2 1p0 1p7 1p9 1b1 1p3 1p12 1b2 1p6 1p10 1p13 1g7 1g0 1q0 1q4 1g5 1q1 1q5 1q2 1q6 1g2 1q3 1q7 1x0 1g1 1x1 1g6 1g3 1x3 1x2 1g4 1x4 1w0 1w1 1w2 1x5 1x6 1x7 1r0 1w3
-1r1 2h4:s 1r2 1r3 1r4 2j0 2y0 1L1 1R1 1L2 1L3 1R3 1R2 1w5 1w4 1L0 1L6 1R0 2l0 2h2:s 1L5 1H0 2h3 2y1 2y2 1R6 1R5 1L4 1R4:s 1L7 1R7 2h0 1D0 1D2 1H1 2l1 1C2:s 1D3 1C3:s 1D1 1C1 1C0 1D6 1C6:s 1D5 1C5:s 2h1 1D7 1C7:s 2h5 1X0 1D4 1C4 2h9:s 1X1
-2y3 2s0 2h6 2y4 2h10 2h12 2s3 2h8:s 2h14 2s1 2y5 2s2 2h11 2s5 2s4 2s6 2s7 2h7:s 2s8 2s13 2s10 2s9 2s11 2s12 2j1 2h15:s 2s14 2s15 2s16 2s17 2s18 2s19 2l2 2h13 2s21 2l3 2j2 2s22 2s23 2s24 2l4 2l5 2s27 2s28 2s29 2s30 2j3 2l6 2s31 2l7 2s25 2s32 2s33 2s34 2j4 2l8 2l9 2s20 2s35 2s36 2s37 2j5 2s38 2s39 2l10 2s26 2s40 2s41 2s42 2s44 2s43 2s45 2s46 2s47
-2n0 2n1 2n2 2n3 2v0 2c0 2v3 2c4 2c7 2c6 2c15 2c3 2v1 2v2 2v5 2v4 2a0 2a1 2c5 2c16 2d0 2d1 2a2 2a3 2d2 2c8 2l11 2c2 2c1 2e0 2d3 2a4 2a5 2d4 2c10 2c13 2c11 2c12 2c14 2e1 2c9 2e2 2d5 2p1 2a6 2d6:s 2a7 2d7:s 2e3 2p2 2a8 2a9 2p11 2b0 2p3 2p12 2b1 2p4 2p5 2p8 2p9 2b2 2p13 2p6 2p0 2p10 2q0 2p7 2q4 2q1 2q5 2q2 2q6 2q3 2q7 2g5 2g3 2x3 2g2 2x2 2g1 2x1 2g0 2x0 2g6 2x6 2g4 2w0 2g7 2w1 2x4 2x7 2x5 2r0 2r1 2w3
-o5 2w2 2L3 2L0 o6:s 2L2 2r2 2R0 2R2 2L1 2w5 2R1:s 2R3 2w4 2L4 2H0 2R4 2L6 2R6:s 2L5 2L7 2R7 2R5:s 2D0 2C0:s 2D2 2C2 o8 o7 2D1 2D3 2C1:s 2H1 o0 2C3:s 2X0 2D4 2Y1:s 2D6 2C4:s o3 o1 2C6 o2 2D5 2D7 o4 2C5:s 2Y0 2Y2:s 2Y3:s 2C7 2X1 2Y8:s 2Y9:s 2Y5:s 2Y7:s 2Y4 2Y10:s 2Y6 2Y11 z0
+i1 i0 i2 i3 k6 k32 k0 k36 b4 b26 k13 k7 k1 k12 k14 k29 k34 b0 k15 k20 b5 k3 k4 b23 k31 k2 b7 b2 b20 u0 k16 k18 b24 b1 b6 k17 b16 b25 k23 p0 k19 b17 u1 p1 w0 b18 b27 p2 u6 u8 p3 b19 b28 w1 u7:s 0y0 b32 b22 b15 b29 b14 u9 b21 p4 b33 0y1 0s0 b3 b34 0y2 0h0:s 0s3 b30 b35 i4 i5 k54 0s4 0s5 k40:g w2 w4 k45 0j0 k25:g b8 0h4:s 0s6 k42:g 0s1 k24 0s2 b31 0s7 0s8 0s13 0l0 0s9 p5:v b12 0s14 0h12:s 0s11 0s15 b9 0s16 0l1 0j1 0s12 0s10 b10 0s18 0l2 b11 0l3 0s19 w3 k28 0s21 0s22 0s17 0s23 0h2 k51 k62 0s24 0j2 0l4 b13 k41 0s26 0j3 k26:g 0s27 w5 0l5 0s28 k30:g k43:g k33:g k79:g k8 k52:g k38:g k37:g k46:g k10:g k47:g k44 k27 k50:g k82 k81:g 0s29 k78 k55 k58 0s30 0l6 0h1 k53:g k59 k61 k80:g k5:v k11 k63 0j4 0l7 k39:g 0s31 k48:g 0s32 0h8:s k35 0s20 0j5 0s33 k60 k64 0s34 0s35 0l8 0l9 0j6 0l10 k68 0s36 k9:g 0l11 k57 k76 0s25 0j7 0s37 0h6 k67 0s38 k56 0l12 k65 k74 0l13 0s39 k66 0j8 k91 0l14 0s40 0l15 0s41 k69 0s42 0s44 0j9 0l16 0s43 0l17 0j10 k77 0h10:s 0h14:s 0h11:s 0s45 k92 0s46 k22 k21 0s47
+0l18 0n0 0n1 0h15:s 0n2 0l19 0j11 k90 0n3 0l20 0v0 0m0 0v2 0v1 0d0:s 0v6 0v4 0v3 0d1:s 0c0 0c6 0v5 0v7 0d2:s 0h7 0c5 0a0 0d4:s 0a1 0l22 0d5:s 0c16 0h13 0c7 0d3:g 0a2 0d6:s 0c4 k49:g 0a4 0d8:s 0c1 0a5 0d9:s 0c3 0a3 0d7:g 0a6 0a8 0d10:s 0l23 0c15 0l21 0d12:s 0c8 0a9 0d13:s 0a10 0h3 0a7 0a12 0a13 0c2 0e0 0d14:s 0a14 0d11:s 0c9 0d16:s 0a11 0d17:s 0a16 0a17 0c13 0b0 0c12 0e1 0d15:s 0a15 0c11 0b1 0c14 0d18:g 0a18 0c10 0e2 0p1 0b2 k75 0d19:g 0p2 0p0 0p4 0e3 u5:s 0b3 0p11 0a19 0b4 0p8 0g2 0p3 0p7 0g0 0g3 0p5 0b5 0g1 0p12 0p9 0b6 0g6 0p13 0p6 0p10 0q0 0q4 0q1 0q5 0g7 0q2 k70 0q6 u3:s 0q3 0h5 k83 0q7 0x2 0h9 0g4 0x3 0x0 0x1 0g5 0x5 0w0 0x4 0w2 0x6 0x7 0w1 1h0:s k72 0r0 k71 0w3 u4 0w4 k84 k87 0w5
+k73 0r1 1y7 1h1 u2 1y0 k88 1h2:s 1h3 1y8 0L1 0r3 1y10 k89 1y1 k85 0r4 w6 1y3 1j0:v 0L2 0L0 0R1 0L3 1y5 0R2:s 0R0:s 0L5 0L6 0R3 1y11 0L7 0L4 k86 1y4 0H0 1l0 0R5 0D2 0D3 0R4 1y12 0D1 0R6:s 1l1 0R7:s 0D0 0C2:s 0C3 0C1:s 0H1 0D7 0D5 0C0:s 0D4 0r2:g 0X0 1y6 0C5:s 0D6 0C7 1y9 1y2 0C4:s 1y14 1y17 1y21 1y19 1y22 0C6 0X1
+1y26 1j1:v 1y13 1y15 1y20 1y18 1y24 1y23 1y16 1s0 1s1 1l2 1A2 1y25 1A3 1A4 1A0 1A1 1y27 1A5 1A6 1l3 1B2 1B4 1A7 1B0 1B3 1B5 1B1 1s3 1B6 1A9 1A8 1s2 1B7 1A10 1j2 1A14 1A12 1B8 1B9 1B14 1s4 1l4 1B11 1B10 1A15 1A11 1A16 1l5 1B15 1A17 1A19 1A18 1B16 1B12 1A20 1B17 1A23 1A24 1A25 1B18 1B19 1A26 1B24 1B25 1j3 1A27 1B20 1s5 1A28 1B26 1B27 1B28 1A21 1l6 1h10 1A29 1l7 1A13 1A30 1h8 1h9 1j4 1B29 1A31 1A22 1B21 1A32 1B30 1B22 1B31 1B32 1B23 1A33 1l8 1A34 1B33 1A35 1B13 1B34 1h12:s 1A36 1l9 1B35 1h4 1j5:v 1B36 1A37 1A38 1l10 1A39 1B38 1B39 1A40 1B40 1h14 1s6 1B37:s 1B41
+1n0 1n1 1h6:s 1n2 1h11:s 1l11 1n3 1v0 1v3 1c0 1c5 1c4 1c3 1c2 1v2 1v1 1v4 1c6 1c8 1v5 1a0 1a1 1d0 1h15 1d1 1a2 1a3 1h7 1h13 1d2 1c7 1c1 1c11 1c10 1e0 1d3 1a4 1a5 1c9 1c14 1d4 1e1 1c16 1c13 1c12 1d5 1a6 1c15 1a7 1p1 1e2 1p2 1d6:s 1e3 1d7:s 1p4 1a8 1a9 1b0 1p11 1p5 1p12 1b1 1p8 1p9 1p3 1b2 1p13 1p6 1p0 1p7 1p10 1h5 1q0 1q4 1q1 1q5 1g3 1g1 1g6 1g0 1g2 1q2 1q6 1q3 1q7 1g5 1g7 1x1 1x2 1x3 1x0 1x7 1w0 1w1 1g4 1x6 1w2 1x4 2h0:s 1x5 2h2:s 1r0 1w3 1w4 1w5
+2h1:v 1r1 1r3 2y0 1r4 2j0:v 2y3 2y5 2y7 2y4 2y12 2y8 1L2 1L3 2h3 1R3 2y6 1L0 1R0 1R2:s 1L1 1R1:s 2l0 1L5 1H0 2y1 2y2 1L4 2y10 1L7 1L6 1R5:s 2y13 1R4 1R7:s 1D0 1C0:s 1R6 2y9 2l1 1D3 1D2 1D1 1H1 1C3:s 1C1 1D6 1D4 1C2:s 2j1 1C4:s 1D5 1X0 1C5:s 1C6 2y11 1r2:g 1D7 1C7 2y14 2y17 2y15 2y19 2l2 2y21 2y24 2y26 1X1
+2s0 2l3 2y16 2y18 2j2:v 2y20 2A5 2A6 2A2 2A3 2A0 2s3 2s1 2A4 2A1 2y22 2y25 2y27 2y23 2A7 2s2 2B2 2B3 2B5 2B0 2B4 2B6 2B1 2A9 2h8:s 2A8 2B7 2A10 2B9 2s4 2s5 2B8 2s6 2h4:s 2l4 2B10 2A12 2A14 2A15 2l5 2B14 2A11 2j3 2A16 2A17 2B15 2A19 2A18 2B11 2B16 2B17 2l6 2A24 2A25 2B19 2A20 2A26 2B20 2A27 2B24 2B25 2l7 2B18 2B26 2B27 2A23 2A28 2A29 2B21 2A22 2B12 2B28 2j4 2A30 2B29 2A31 2A21 2B30 2h12 2B31 2B23 2A32 2A33 2A34 2B22 2B13 2A35 2B32 2B33 2B34 2h6 2B35 2A13 2A36 2h14 2A37 2A38 2B36 2l8 2A39 2B38 2B39 2l9 2A40 2B37:s 2j5 2B40 2B41
+2n0 2h10:s 2h9:s 2n1 2n2 2n3 2l10 2v0 2h11:s 2h13 2c0 2c8 2c1 2h7 2h15 2v3 2v1 2v2 2v5 2c5 2c9 2c7 2c2 2c6 2v4 2a0 2a1 2c4 2d0 2l11 2h5 2d1 2c3 2a2 2c12 2c10 2a3 2d2 2e0 2d3 2a4 2a5 2c15 2d4 2e1 2d5 2c16 2c14 2c11 2a6 2c13 2e2 2a7 2e3 2p1 2p2 2d6:s 2a8 2d7:s 2p8 2p11 2a9 2b0 2p9 2p3 2b1 2p12 2p4 2p0 2p5 2b2 2p10 2p13 2p6 2q0 2p7 2g0 2q4 2q1 2q5 2q2 2q6 2g3 2g1 2q3 2g2 2q7 2x2 2x1 2x3 2g4 2x0 2g5 2x5 2g6 2w0 2w1 2g7 2x6 2w2 2L3 2x4 2x7 2L0 2L2 2L1 2w3 2w4 2r0 2w5
+2r1 2R3:s o5 2R2:s 2r2 2R0 2R1 2L4 o6 2L6 2H0 o7:s o4 2L7 2L5 2R4 2R7:s 2D1 2C1:s 2R6 2R5 2D3 2C3 o8 o0 2D2 2C2:s o2 2D0 2C0:s 2H1 2D7 o3 2C7:s 2D6 2D5 2C5:s 2X0 2C6 2D4 2Y1:s 2Y0 o1:s 2C4 2Y2 2Y3 2X1 2Y6 2Y5 2Y4 2Y7 2Y9 2Y10 2Y8:s 2Y11 z0
 """
 
 SCRATCH = {}
@@ -45,23 +45,24 @@ for _t in range(R + 1):
 for _t in range(R):
     _sb("LQ%d" % _t, K, "float8_e4m3fn_x4")
     _sb("LS%d" % _t, K, "uint8")
-for _n, _w in (("U", 512), ("E", 2048), ("H", 1024), ("Xh", 4 * XW), ("V", 1024), ("zer", C), ("junk", 10 * C), ("gtb", C + 2),
+for _n, _w in (("U", 512), ("E", 2048), ("H", 1024), ("Xh", 4 * XW), ("V", 1024), ("zer", C), ("junk", 14 * C), ("gtb", C + 2),
                ("geb", C), ("bnd", C), ("cnt", CO + C + 1), ("one", C), ("z", C), ("jk", 16 * WIN), ("al", C), ("M", (KB + 1) * ROW),
                ("Md", KB * C)):
     _sb(_n, _w, "bfloat16")
-for _n, _s, _w in (("QU", "SU", 128), ("QR", "SR", 128), ("WL", "WSL", 512), ("WQ", "WS", 512), ("QE", "SE", 512), ("QH", "SH", K)):
+for _n, _s, _w in (("QU", "SU", 128), ("QR", "SR", 128), ("QA", "SA", 128), ("QB", "SB", 128), ("WL", "WSL", 512), ("WQ", "WS", 512),
+                   ("QE", "SE", 512), ("QH", "SH", K)):
     _sb(_n, _w, "float8_e4m3fn_x4")
     _sb(_s, _w, "uint8")
-for _n, _w in (("iot", ROW), ("t16", 48), ("yy", K), ("K1", C), ("Pl", C), ("D", C), ("scJ", (KB + 1) * C), ("scP", 2 * K), ("Ng", C),
+for _n, _w in (("iot", ROW), ("t16", 48), ("yy", K), ("K1", C), ("Pl", C), ("D", 2 * C), ("scJ", (KB + 1) * C), ("scP", 2 * K), ("Ng", C),
                ("Gr", K), ("scB", K), ("rows", (KB + 1) * ROW),
-               ("prow", ROW), ("pout", C), ("pe", 2 * K), ("Br", K), ("ysb", C), ("sm", 32), ("F", 9 * 32), ("Tt", 66), ("Tb", 8 * 34),
-               ("o", 12 * 34), ("Dt", 5 * 34), ("G2t", 34), ("Tat", 34), ("Sgt", 34), ("nC1", 64), ("nE", 64), ("nF", 64), ("nC", 64),
-               ("Msk", 32), ("l1", 32), ("l2", 32), ("l3", 3 * 32), ("tmp", 8 * 34), ("TB", 3 * 33), ("TM", 3 * 33), ("f", 10),
-               ("Kc", 8), ("ec", 16), ("e2", 16), ("nb", 16), ("et", 16)):
+               ("prow", ROW), ("pout", C), ("pe", 2 * K), ("Br", K), ("ysb", C), ("sm", 32), ("F", 2 * 288), ("Tt", 2 * 132), ("Tb", 2 * 5 * 68),
+               ("o", 2 * 10 * 100), ("Dt", 2 * 3 * 34), ("G2t", 98), ("Tat", 34), ("Sgt", 2 * 34), ("cap", 4 * 96), ("nC", 64), ("sg", 2 * 8),
+               ("one32", 34), ("l1", 32), ("l2", 32), ("l3", 3 * 32), ("tmp", 8 * 34), ("TB", 3 * 33), ("TM", 2 * 99), ("f", 2 * 16),
+               ("m1", 16), ("w0", 1700), ("c0", 700), ("mk", 3 * 48), ("mo", 3 * 48), ("Kc", 8), ("ec", 16), ("e2", 16), ("nb", 16), ("et", 16)):
     _sb(_n, _w, "float32")
-for _n, _w in (("LJ", (KB + 1) * 32), ("Lb", 16), ("La", 16), ("el", 16), ("pel", 32), ("offU", 8), ("Lr", 32)):
+for _n, _w in (("LJ", (KB + 1) * 32), ("Lb", 16), ("La", 16), ("el", 16), ("pel", 32), ("offU", 24), ("Lr", 32)):
     _sb(_n, _w, "uint16")
-for _n, _w in (("pt", 32), ("pi", 4), ("oi", 8)):
+for _n, _w in (("pt", 32), ("pi", 4), ("oi", 24)):
     _sb(_n, _w, "int32")
 for _b in range(8):
     SCRATCH["P%d" % _b] = ("psum", [128, 512], "float32")
@@ -96,7 +97,8 @@ def _touched(xs):
 def _needs(ops):
     out, past = [], {}
     for i, o in enumerate(ops):
-        out.append(sorted({j for w in (0, 1) for a, m in o[3 + w] for j, n, x in past.get(a, ()) if m & n and (w or x or m == -1)}))
+        out.append(sorted({j for w in (0, 1) for a, m in o[3 + w] for j, n, x in past.get(a, ())
+                           if m & n and (w or x or m == -1 and not o[1] == ops[j][1] == "s")}))
         for w in (0, 1):
             for a, m in o[3 + w]:
                 past.setdefault(a, []).append((i, m, w))
@@ -168,6 +170,10 @@ def program(g, core, T, topo):
         tail = () if op1 is None else (op1,)
         op("v", lambda q: V.tensor_scalar(ap(out), ap(in0), ap(s1), ap(s2), op0, *tail), [in0, s1, s2], [out])
 
+    def affine(out, in_, scale, bias):
+        op("vs", lambda q: S.activation(ap(out), ap(in_), AF.Identity, bias=ap(bias), scale=ap(scale)) if q == "s" else
+           V.tensor_scalar(ap(out), ap(in_), ap(scale), ap(bias), A.mult, A.add), [in_, scale, bias], [out])
+
     def tt(out, a, b, o):
         op("v", lambda q: V.tensor_tensor(ap(out), ap(a), ap(b), o), [a, b], [out])
 
@@ -237,8 +243,8 @@ def program(g, core, T, topo):
         op("g", fn, [src], [(sem, len(ops), len(ops) + 1, 1)], (), "remote")
         sent[0] += n_out
 
-    r_, r8, hf, off = col("sm", 0), col("sm", 1), col("sm", 2), col("sm", 3)
-    tau1, c1, m1, off1, off2 = col("sm", 4), col("sm", 5), col("tmp", 39), col("sm", 10), col("sm", 11)
+    r_, hf, off = col("sm", 0), col("sm", 2), col("sm", 3)
+    off1, off2, p32 = col("sm", 10), col("sm", 11), col("sm", 1)
 
     def lst(k, a, b):
         return v("LJ", 32 * k + a // 16, 32 * k + b // 16)
@@ -262,13 +268,22 @@ def program(g, core, T, topo):
         named("%dh" % t)
         for e in range(4):
             cp(v("Xh", XW * e + CO + a, XW * e + CO + b), v("X%d" % t, 4 * a + e, 4 * b, 4), "vs", 0.5)
-            cp(v("Xh", XW * e + C - 1 - a, XW * e + C - 1 - b, -1), v("X%d" % t, 4 * a + e, 4 * b, 4), "vs", 0.5)
+            cp(v("Xh", XW * e + C - 1 - a, XW * e + C - 1 - b, -1), v("Xh", XW * e + CO + a, XW * e + CO + b), "gvs")
 
-    def early(t, bank, a, b, j, out, bounds):
+    def early(t, n=0):
         named("%dy" % t)
-        mm(bank, v("QR"), v("Q%d" % t, a, b))
-        act(v("junk", C * j, C * j + b - a), v(bank, 0, b - a), AF.Sign, m1, tau1, col("f", j))
-        ts(v(out), v(bounds), col("f", j), A.subtract)
+        for x in range(2):
+            bank = "P%d" % (6 + x)
+            mm(bank, v("Q" + "AB"[x]), v("Q%d" % t, n * K, K + n * HALF))
+            for j in range(3):
+                f, at = col("f", 16 * x + 8 + j), 96 * x + 32 * j
+                if n:
+                    f, lo = col("f", 16 * x + 11 + j), C * (12 + x) + HALF * j
+                    act(v("junk", lo, lo + HALF), v(bank, 0, HALF), AF.Sign, col("m1", j), col("m1", 3 + j), f)
+                    ts(v("cap", 192 + at, 192 + at + 32), v("cap", at, at + 32), f, A.subtract)
+                    continue
+                act(v("jk", K * (3 * x + j), K * (3 * x + j + 1)), v(bank, 0, K), AF.Sign, col("m1", j), col("m1", 3 + j), f)
+                ts(v("cap", at, at + 32), v("Dt", 0, 32), col("m1", 6 + j), A.add, f, A.subtract)
 
     named("i")
     dma("y", T.pt[:], T.ptr[:], [], [v("pt")])
@@ -282,17 +297,16 @@ def program(g, core, T, topo):
     iota(col("pi", 0), [[1, 1]], 0, 1)
     iota(v("t16", 0, 16), [[1, 16]], 0)
     iota(v("iot"), [[1, ROW]], 0)
-    iota(v("oi"), [[16, 8]], 0)
+    iota(v("oi", 0, 8), [[16, 8]], 0)
+    iota(v("oi", 8, 24), [[16, 2], [32, 4], [0, 2]], 0)
     ramp(v("Pl"), -K - int(UNIT))
     iota(v("l1"), [[16, 2], [0, 16]], 0)
     iota(v("l2"), [[16, 32]], PAD)
-    iota(v("tmp", 68, 102), [[0, 17], [-2, 2]], 4)
-    iota(v("tmp", 102, 136), [[0, 17], [1, 2]], 2)
-    iota(v("tmp", 136, 170), [[0, 17], [1, 2]], 3)
+    iota(v("tmp", 68, 108), [[0, 5], [1, 8]], 8)
     ramp(v("prow", PAD + K, ROW), PAD)
     ramp(v("pout", K, C), 0)
     ramp(v("Ng"), -K - PAD - 1, -1)
-    for j, m in enumerate((15, 7, 16)):
+    for j, m in enumerate((15, 31, 16)):
         ts(col("pi", j + 1), col("pi", 0), m, A.bitwise_and)
     cp(v("sm", 0, 3), v("pi", 1, 4))
     ts(v("t16", 16, 32), v("t16", 0, 16), r_, A.is_equal, BIG, A.mult)
@@ -318,7 +332,7 @@ def program(g, core, T, topo):
     named("k")
     fill(v("one"), 1.0)
     fill(v("zer"), 0.0)
-    for nm in ("G2t", "Tat", "Sgt"):
+    for nm in ("G2t", "Tat", "Sgt", "one32"):
         fill(v(nm), 1.0)
     for nm in ("Tt", "Tb", "Dt"):
         fill(v(nm), 0.0)
@@ -330,46 +344,90 @@ def program(g, core, T, topo):
     for k in range(KB + 1):
         fill(v("M", ROW * k, ROW * k + PAD), -K - UNIT)
     fill(col("Tat", 32), -1.5)
-    ts(col("sm", 6), r_, 7.5, A.is_gt, 2.0, A.mult)
-    ts(col("sm", 9), r_, 8.0, A.not_equal, -BIG, A.mult)
+    ts(col("sm", 6), hf, 1 / 16, A.mult)
+    ts(col("sm", 7), col("sm", 6), -1.0, A.mult, 1.0, A.add)
+    ts(col("sm", 8), p32, 16.0, A.is_equal, 2.0, A.mult)
+    ts(col("sm", 12), p32, 0.0, A.add)
+    ts(col("sm", 13), hf, -2.0, A.mult, 32.0, A.add)
+    ts(col("sm", 13), col("sm", 13), r_, A.add)
+    ts(col("sm", 14), p32, 16.0, A.add)
+    fill(col("m1", 3), -1.0)
+    ts(col("m1", 4), col("sm", 6), 2.0, A.mult, -1.0, A.add)
+    fill(col("m1", 5), 1.0)
+    ts(v("m1", 6, 9), v("m1", 3, 6), -1.5, A.mult)
+    for j in range(3):
+        ts(v("mk", 48 * j, 48 * j + 48), v("iot", 0, 48), col("sm", 12 + j), A.is_lt, 16.0, A.mult)
+    ts(v("mk"), v("mk"), 1.0, A.max)
+    for j in range(3):
+        scan(v("mo", 48 * j, 48 * j + 48), v("mk", 48 * j, 48 * j + 48), v("zer", 0, 48), 2.0 ** -100, A.mult, A.add)
+    cp(v("m1", 0, 3), v("mo", 47, 144, 48))
     unit = 2.0 ** -23
-    for j, step in enumerate((78608, 4624, 272, 16)):
-        ts(col("Kc", j), r_, 1.0, A.add, step * unit, A.mult)
-    ts(col("Kc", 4), r_, 0.5, A.add, unit, A.mult)
-    ts(col("Kc", 5), r_, 1.0, A.add, unit, A.mult)
-    ts(col("Kc", 6), r_, 1.0, A.add, 17 * 78608 * unit, A.mult)
-    ts(tau1, col("sm", 6), -1.0, A.add)
-    ts(c1, col("sm", 6), -1.5, A.mult, 1.5, A.add)
-    ts(v("tmp", 16, 24), v("t16", 0, 8), r8, A.is_le, 2.0 ** 25, A.mult)
-    ts(v("tmp", 24, 32), v("tmp", 16, 24), 1.0, A.max)
-    scan(v("tmp", 32, 40), v("tmp", 24, 32), v("Dt", 0, 8), 2.0 ** -125, A.mult, A.add)
-    ts(v("Msk"), v("l1"), hf, A.not_equal, -BIG, A.mult)
-    ts(v("nC1", 0, 32), v("Msk"), c1, A.add)
-    ts(v("nC1", 32, 64), v("Msk"), c1, A.add, col("sm", 9), A.add)
-    fill(v("tmp", 68, 85, 16), 0.0)
-    scan(v("tmp", 170, 203), v("tmp", 68, 101), v("Sgt", 0, 33), 1.0, A.mult, A.max)
-    ts(v("tmp", 204, 236), v("l1"), hf, A.is_equal)
-    fill(col("tmp", 236), 1.0)
-    tt(v("TB", 66, 99), v("tmp", 170, 203), v("tmp", 204, 237), A.mult)
-    tt(v("tmp", 238, 271), v("TB", 66, 99), v("tmp", 102, 135), A.mult)
-    ts(v("TB", 33, 66), v("tmp", 238, 271), 0.5, A.mult)
+    for j, step in enumerate((1056, 32)):
+        ts(col("Kc", j), p32, 1.0, A.add, step * unit, A.mult)
+    ts(col("Kc", 2), p32, 0.5, A.add, unit, A.mult)
+    ts(col("Kc", 6), p32, 1.0, A.add, 33 * 1056 * unit, A.mult)
+    for j in range(5):
+        fill(v("TB", 66 + 8 * j, min(74 + 8 * j, 99)), 2.0 ** j)
+    tt(v("tmp", 238, 271), v("TB", 66, 99), v("tmp", 68, 101), A.mult)
+    ts(v("TB", 33, 66), v("tmp", 238, 271), 0.125, A.mult)
     ts(v("tmp", 170, 203), v("TB", 66, 99), col("Kc", 6), A.mult)
     tt(v("TB", 0, 33), v("tmp", 170, 203), v("TB", 33, 66), A.add)
-    ts(col("sm", 7), r_, hf, A.add)
-    ts(v("tmp", 68, 100), v("iot", 0, 32), col("sm", 7), A.is_equal)
-    tt(v("tmp", 102, 134), v("TB", 66, 98), v("tmp", 136, 168), A.mult)
-    tt(v("tmp", 204, 236), v("tmp", 68, 100), v("tmp", 102, 134), A.mult)
-    red(col("G2t", 32), v("tmp", 204, 236), A.max)
+    ts(v("tmp", 110, 142), v("iot", 0, 32), p32, A.is_equal)
+    tt(v("tmp", 204, 236), v("tmp", 110, 142), v("TB", 34, 66), A.mult)
+    red(col("G2t", 96), v("tmp", 204, 236), A.max)
     ts(v("nb"), v("l2", 0, 16), 2 * UNIT, A.mult, (1 - 2 * PAD) * UNIT, A.add)
     ts(v("tmp", 0, 16), v("t16", 0, 16), 16.0, A.mult, float(WIN), A.add)
     ts(v("et"), v("tmp", 0, 16), off, A.subtract)
+    named("b")
+
+    def c0(a, b=None, s=1):
+        return v("c0", a, a + 1 if b is None else b, s)
+    iota(c0(300, 334), [[0, 17], [-2, 2]], 4)
+    iota(c0(334, 368), [[0, 17], [1, 2]], 2)
+    iota(c0(368, 402), [[0, 17], [1, 2]], 3)
+    fill(v("w0", 0, 520), 0.0)
+    fill(c0(200, 268), 1.0)
+    ts(c0(0), r_, 7.5, A.is_gt, 2.0, A.mult)
+    ts(c0(3), r_, 8.0, A.not_equal, -BIG, A.mult)
+    ts(c0(4), c0(0), -4.0, A.mult, r_, A.add)
+    for j, step in enumerate((78608, 4624, 272, 16)):
+        ts(c0(8 + j), r_, 1.0, A.add, step * unit, A.mult)
+    ts(c0(12), r_, 0.5, A.add, unit, A.mult)
+    ts(c0(13), r_, 1.0, A.add, unit, A.mult)
+    ts(c0(14), r_, 1.0, A.add, 17 * 78608 * unit, A.mult)
+    ts(c0(1), c0(0), -1.0, A.add)
+    ts(c0(2), c0(0), -1.5, A.mult, 1.5, A.add)
+    ts(c0(16, 24), v("t16", 0, 8), c0(4), A.is_le, 2.0 ** 25, A.mult)
+    ts(c0(24, 32), c0(16, 24), 1.0, A.max)
+    scan(c0(32, 40), c0(24, 32), v("zer", 0, 8), 2.0 ** -125, A.mult, A.add)
+    ts(c0(268, 300), v("l1"), hf, A.not_equal, -BIG, A.mult)
+    ts(c0(64, 96), c0(268, 300), c0(2), A.add)
+    ts(c0(96, 128), c0(268, 300), c0(2), A.add, c0(3), A.add)
+    fill(c0(300, 317, 16), 0.0)
+    scan(c0(402, 435), c0(300, 333), v("one32", 0, 33), 1.0, A.mult, A.max)
+    ts(c0(436, 468), v("l1"), hf, A.is_equal)
+    fill(c0(468), 1.0)
+    tt(c0(666, 699), c0(402, 435), c0(436, 469), A.mult)
+    tt(c0(470, 503), c0(666, 699), c0(334, 367), A.mult)
+    ts(c0(633, 666), c0(470, 503), 0.5, A.mult)
+    ts(c0(504, 537), c0(666, 699), c0(14), A.mult)
+    tt(c0(600, 633), c0(504, 537), c0(633, 666), A.add)
+    ts(c0(538, 570), v("iot", 0, 32), p32, A.is_equal)
+    tt(c0(402, 434), c0(666, 698), c0(368, 400), A.mult)
+    tt(c0(436, 468), c0(538, 570), c0(402, 434), A.mult)
+    red(c0(232), c0(436, 468), A.max)
     named("u")
     cp(v("offU"), v("oi"))
     quant(v("QU"), v("U"))
-    op("v", lambda q: V.tensor_copy(T.QR[:].bitcast(u32), T.QU[:].bitcast(u32).indirect(T.offU[:])), [v("QU"), v("offU")], [v("QR")])
-    cp(v("SR"), ind(v("SU"), v("offU")), "vs")
+    for j, nm in ((1, "A"), (2, "B"), (0, "R")):
+        off_u = v("offU", 8 * j, 8 * j + 8)
+        op("v", lambda q, nm=nm, o=off_u: V.tensor_copy(T["Q" + nm][:].bitcast(u32), T.QU[:].bitcast(u32).indirect(ap(o))), [v("QU"), off_u], [v("Q" + nm)])
+        cp(v("S" + nm), ind(v("SU"), off_u), "vs")
     quant(v("Q0", 0, K), v("X0", 0, 1024))
-    early(0, "P7", 0, K, 8, "nF", "nC1")
+    named("0y")
+    mm("P7", v("QR"), v("Q0", 0, K))
+    act(v("jk", 0, K), v("P7", 0, K), AF.Sign, c0(39), c0(1), col("f", 8))
+    ts(v("c0", 128, 192), v("c0", 64, 128), col("f", 8), A.subtract)
     named("u")
     quant(v("Q0", K, C), v("X0", 1024, 2048))
     halve(0, 0, K)
@@ -381,56 +439,127 @@ def program(g, core, T, topo):
     send(v("WS"), v("WSL"), "warr", False)
     quant(v("QE"), v("E"))
 
-    def oc(s, j):
-        return col("o", 34 * s + j)
-
-    def osl(s, k):
-        return v("o", 34 * s, 34 * s + k)
-
     def select(t, a):
         named("%ds" % t)
-        mm("P3", v("QR"), v("Q%d" % t, a, C))
-        mm("P0", v("QR"), v("Q%d" % t))
-        mm("P1", v("QR"), v("Q%d" % t))
-        tau = oc(0, 31)
+        for x in range(2):
+            mm("P%d" % (2 + x), v("Q" + "AB"[x]), v("Q%d" % t, a, C))
+        for x in range(4):
+            mm("P%d" % (0, 1, 4, 5)[x], v("Q" + "AB"[x % 2]), v("Q%d" % t))
+        mm("P6", v("QR"), v("Q%d" % t))
+        for x in range(2):
+            named("%d%s" % (t, "AB"[x]))
+
+            def oc(s, j):
+                return col("o", 1000 * x + 100 * s + j)
+
+            def osl(s, k):
+                return v("o", 1000 * x + 100 * s, 1000 * x + 100 * s + k)
+
+            def sg(j):
+                return col("sg", 8 * x + j)
+            tau, nc, row, f0, t0 = oc(0, 31), v("nC", 32 * x, 32 * x + 32), v("P%d" % x), 288 * x, 132 * x
+
+            def step(s, src, bias, scale, cmp, m):
+                f, tb = col("f", 16 * x + s + 1), 340 * x + 68 * (s - 2)
+                act(v("junk", C * (6 * x + s - 1), C * (6 * x + s)), src, AF.Sign, bias, scale, f)
+                ts(v("F", f0 + 64 + 32 * s, f0 + 96 + 32 * s), nc, f, cmp, m, A.mult)
+                turn(v("Tb", tb, tb + 32), v("F", f0 + 64 + 32 * s, f0 + 96 + 32 * s))
+                return tb
+
+            for j in range(3):
+                f, at = col("f", 16 * x + j), 192 + 96 * x + 32 * j
+                act(v("jk", K * (3 * x + j), K * (3 * x + j) + C - a), v("P%d" % (2 + x), 0, C - a), AF.Sign, col("m1", j), col("m1", 3 + j), f)
+                ts(v("F", f0 + 32 * j, f0 + 32 * j + 32), v("cap", at, at + 32), f, A.is_ge, col("m1", j), A.mult)
+                if j == 1:
+                    ts(v("F", f0 + 96, f0 + 128), v("cap", at, at + 32), f, A.is_ge, col("sm", 8), A.mult)
+            turn(v("Tt", t0, t0 + 128), v("F", f0, f0 + 128))
+            scan(osl(0, 33), v("Tt", t0 + 96, t0 + 129), v("Tat", 0, 33), -1.0, A.add, A.mult)
+            scan(osl(1, 97), v("Tt", t0, t0 + 97), v("G2t", 0, 97), 0.0, A.max, A.mult)
+            ts(nc, v("Dt", 0, 32), oc(0, 32), A.add)
+            ts(v("TM", 99 * x, 99 * x + 99), v("TB"), oc(1, 95), A.mult)
+            ts(sg(0), tau, col("sm", 7 - x), A.mult)
+            ts(col("Sgt", 34 * x + 32), sg(0), -1.0, A.mult)
+            tb = step(2, row, oc(1, 96), tau, A.is_lt, -HUGE)
+            for j, s in enumerate((2, 7, 8)):
+                m = 99 * x + 33 * j
+                scan(v("o", 1000 * x + 100 * s + 33, 1000 * x + 100 * s + 1, -1), v("Tb", tb + 31, tb - 1, -1), v("TM", m + 31, m - 1, -1), col("TM", m + 32), A.add, A.max)
+            w, lo, dt_ = oc(8, 2), oc(7, 2), 102 * x
+            ts(v("Dt", dt_ + 33, dt_ + 102, 34), v("Kc", 0, 3), w, A.mult)
+            ts(sg(1), w, unit, A.mult)
+            ts(col("Dt", dt_ + 100), lo, -1.0, A.mult)
+            affine(v("D", C * x, C * x + C), v("P%d" % (4 + x)), tau, lo)
+            for s in range(3, 6):
+                bias, base = (oc(2, 2), lo) if s == 3 else (oc(s - 1, 33), oc(s - 1, 31))
+                tb = step(s, row, bias, tau, A.is_ge, bias)
+                scan(osl(s, 34), v("Tb", tb, tb + 34), v("Dt", dt_ + 34 * (s - 3), dt_ + 34 * (s - 2)), base, A.max, A.add)
+            if x:
+                ts(sg(2), oc(5, 31), sg(0), A.mult, col("sg", 2), A.add)
+                affine(v("z"), v("P6"), 1.0, sg(2))
+            else:
+                ts(sg(2), oc(5, 31), sg(0), A.mult)
+            tb = step(6, v("D", C * x, C * x + C), oc(5, 33), 1.0, A.is_ge, sg(1))
+            if x:
+                scan(osl(6, 34), v("Tb", tb, tb + 34), v("Sgt", 34, 68), 0.0, A.add, A.mult)
+            else:
+                scan(v("Tb", 340 + tb + 65, 340 + tb + 32, -1), v("Tb", tb, tb + 33), v("Sgt", 0, 33), 0.0, A.add, A.mult)
+
+    def select0():
+        named("0s")
+        mm("P3", v("QR"), v("Q0", K, C))
+        mm("P0", v("QR"), v("Q0"))
+        mm("P1", v("QR"), v("Q0"))
+
+        def w0(a, b=None, s=1):
+            return v("w0", a, a + 1 if b is None else b, s)
+
+        def oc(s, j):
+            return w0(520 + 34 * s + j)
+
+        def osl(s, k):
+            return w0(520 + 34 * s, 520 + 34 * s + k)
+        tau, msk, tt0, dt0, f0, nc, tm = oc(0, 31), c0(268, 300), 272, 340, 950, 1250, 1320
 
         def step(s, src, bias, scale, cap, cmp, m):
+            at = f0 + 32 * s if s > 1 else f0
             act(v("junk", C * (s - 1), C * (s - 1) + src[2]), src, AF.Sign, bias, scale, col("f", s - 1))
-            ts(v("F", 32 * s, 32 * s + 32) if s > 1 else v("F", 0, 32), cap, col("f", s - 1), cmp, m, A.mult)
+            ts(w0(at, at + 32), cap, col("f", s - 1), cmp, m, A.mult)
             if s > 1:
-                turn(v("Tb", 34 * (s - 1), 34 * (s - 1) + 32), v("F", 32 * s, 32 * s + 32))
+                turn(w0(34 * (s - 1), 34 * (s - 1) + 32), w0(at, at + 32))
 
-        step(1, v("P3", 0, C - a), m1, tau1, v("nF", 0, 32), A.is_ge, m1)
-        ts(v("F", 32, 64), v("nF", 32, 64), col("f", 0), A.is_ge, 2.0, A.mult)
-        turn(v("Tt", 0, 64), v("F", 0, 64))
-        scan(osl(0, 33), v("Tt", 32, 65), v("Tat", 0, 33), -1.0, A.add, A.mult)
-        scan(osl(1, 33), v("Tt", 0, 33), v("G2t", 0, 33), 0.0, A.max, A.mult)
-        ts(v("nC", 32, 64), v("Msk"), -1.0, A.mult, oc(0, 32), A.add)
-        ts(v("nC", 0, 32), v("Msk"), oc(0, 32), A.add)
-        ts(v("TM"), v("TB"), oc(1, 31), A.mult)
-        ts(col("Sgt", 32), tau, -1.0, A.mult)
-        step(2, v("P0"), oc(1, 32), tau, v("nC", 32, 64), A.is_lt, -HUGE)
+        step(1, v("P3", 0, K), c0(39), c0(1), c0(128, 160), A.is_ge, c0(39))
+        ts(w0(f0 + 32, f0 + 64), c0(160, 192), col("f", 0), A.is_ge, 2.0, A.mult)
+        turn(w0(tt0, tt0 + 64), w0(f0, f0 + 64))
+        scan(osl(0, 33), w0(tt0 + 32, tt0 + 65), v("Tat", 0, 33), -1.0, A.add, A.mult)
+        scan(osl(1, 33), w0(tt0, tt0 + 33), c0(200, 233), 0.0, A.max, A.mult)
+        ts(w0(nc + 32, nc + 64), msk, -1.0, A.mult, oc(0, 32), A.add)
+        ts(w0(nc, nc + 32), msk, oc(0, 32), A.add)
+        ts(w0(tm, tm + 99), c0(600, 699), oc(1, 31), A.mult)
+        ts(c0(266), tau, -1.0, A.mult)
+        step(2, v("P0"), oc(1, 32), tau, w0(nc + 32, nc + 64), A.is_lt, -HUGE)
         for j, s in enumerate((2, 9, 10)):
-            scan(v("o", 34 * s + 33, 34 * s + 1, -1), v("Tb", 65, 33, -1), v("TM", 33 * j + 31, 33 * j - 1, -1), col("TM", 33 * j + 32), A.add, A.max)
+            scan(w0(520 + 34 * s + 33, 520 + 34 * s + 1, -1), w0(65, 33, -1), w0(tm + 33 * j + 31, tm + 33 * j - 1, -1), w0(tm + 33 * j + 32), A.add, A.max)
         w = oc(10, 2)
-        ts(v("Dt", 33, 170, 34), v("Kc", 0, 5), w, A.mult)
-        ts(col("sm", 16), col("Kc", 5), w, A.mult)
+        ts(w0(dt0 + 33, dt0 + 170, 34), c0(8, 13), w, A.mult)
+        ts(w0(1430), c0(13), w, A.mult)
         for s in range(3, 8):
             bias, base = (oc(2, 2), oc(9, 2)) if s == 3 else (oc(s - 1, 33), oc(s - 1, 31))
-            step(s, v("P0"), bias, tau, v("nC", 0, 32), A.is_ge, bias)
-            scan(osl(s, 34), v("Tb", 34 * (s - 1), 34 * s), v("Dt", 34 * (s - 3), 34 * (s - 2)), base, A.max, A.add)
+            step(s, v("P0"), bias, tau, w0(nc, nc + 32), A.is_ge, bias)
+            scan(osl(s, 34), w0(34 * (s - 1), 34 * s), w0(dt0 + 34 * (s - 3), dt0 + 34 * (s - 2)), base, A.max, A.add)
             if s == 3:
-                ts(col("Dt", 4 * 34 + 32), oc(3, 31), -1.0, A.mult)
-                ts(v("D"), v("P1"), tau, A.mult, oc(3, 31), A.add)
-        ts(v("z"), v("D"), oc(7, 32), A.add, tau, A.mult)
-        step(8, v("D"), oc(7, 33), 1.0, v("nC", 0, 32), A.is_ge, col("sm", 16))
-        scan(osl(8, 33), v("Tb", 34 * 7, 34 * 7 + 33), v("Sgt", 0, 33), 0.0, A.max, A.mult)
+                ts(w0(dt0 + 4 * 34 + 32), oc(3, 31), -1.0, A.mult)
+                affine(v("D", 0, C), v("P1"), tau, oc(3, 31))
+        ts(v("z"), v("D", 0, C), oc(7, 32), A.add, tau, A.mult)
+        step(8, v("D", 0, C), oc(7, 33), 1.0, w0(nc, nc + 32), A.is_ge, w0(1430))
+        scan(osl(8, 33), w0(34 * 7, 34 * 7 + 33), c0(234, 267), 0.0, A.max, A.mult)
 
     hs = [(HALF * h, HALF * h + HALF, 8 * h, 8 * h + 8) for h in range(2)]
     for t in range(R):
         Xn, Qn, Sn = "X%d" % (t + 1), "Q%d" % (t + 1), T["S%d" % (t + 1)]
-        select(t, K if t == 0 else K + HALF)
-        thr = oc(8, 32)
+        if t:
+            select(t, K + HALF)
+        else:
+            select0()
+        thr = col("o", 1000 + 600 + 33) if t else col("w0", 520 + 34 * 8 + 32)
         named("%dn" % t)
         ts(v("gtb", 0, C), v("z"), thr, A.is_gt, -UNIT, A.mult)
         ts(v("geb"), v("z"), thr, A.is_ge, UNIT, A.mult)
@@ -497,7 +626,7 @@ def program(g, core, T, topo):
             to_list(lst(0, 0, K), v("prow", PAD, PAD + K), 0, K, "scJ", 0)
             jumps(t + 1, K, ("prow", 0))
             halve(t + 1, 0, K)
-            early(t + 1, "P7", 0, K, 8, "nE", "nC1")
+            early(t + 1)
         else:
             act(v("pe", 0, K), ind(v("cnt"), v("Lb")), AF.Abs, -1.0, 1 / UNIT)
             tt(v("pout", 0, K), v("pe", 0, K), v("iot", 0, K), A.min)
@@ -535,10 +664,10 @@ def program(g, core, T, topo):
             elif kind == "X":
                 quant(v(Qn, K + a, K + b), v(Xn, 4 * (K + a), 4 * (K + b)))
             elif t < R - 1:
-                if h == 0:
-                    early(t + 1, "P6", K, K + HALF, 9, "nF", "nE")
-                else:
+                if h == 1:
                     halve(t + 1, K, C)
+                else:
+                    early(t + 1, 1)
             else:
                 mm("P%d" % (6 + h), v("QU"), v(Qn, K + a, K + b))
                 store(T.oc[:, 4 * (K + a):4 * (K + b)], T[Qn][:, K + a:K + b].bitcast(u8), v(Qn, K + a, K + b))

from concourse.mybir import dt, AluOpType, AxisListType, ActivationFunctionType

C, K, R = 512, 256, 3
HALF = K // 2
WIN = HALF + 8
PAD = 16
ROW = C + PAD
KB = 6
NQ = (4, 2, 2)
NJ = (2, 1, 1)
TWICE = (0, 1, 1)
XW = 2 * C + PAD
CO = C + PAD
A = AluOpType
AF = ActivationFunctionType
BIG = 1048576.0
HUGE = 1e29
HOLD = 4096.0
UNIT = 2048.0
NSEM, NDSEM = 112, 30
ORDER = """
i1 i0 i2 i3 k6 k32 k0 k36 b4 b26 k13 k7 k1 k12 k14 k29 k34 b0 k15 k20 b5 k3 k4 b23 k31 k2 b7 b2 b20 u0 k16 k18 b24 b1 b6 k17 b16 b25 k23 p0 k19 b17 u1 p1 w0 b18 b27 p2 u6 u8 p3 b19 b28 w1 u7:s 0y0 b32 b22 b15 b29 b14 u9 b21 p4 b33 0y1 0s0 b3 b34 0y2 0h0:s 0s3 b30 b35 i4 i5 k54 0s4 0s5 k40:g w2 w4 k45 0j0 k25:g b8 0h4:s 0s6 k42:g 0s1 k24 0s2 b31 0s7 0s8 0s13 0l0 0s9 p5:v b12 0s14 0h12:s 0s11 0s15 b9 0s16 0l1 0j1 0s12 0s10 b10 0s18 0l2 b11 0l3 0s19 w3 k28 0s21 0s22 0s17 0s23 0h2 k51 k62 0s24 0j2 0l4 b13 k41 0s26 0j3 k26:g 0s27 w5 0l5 0s28 k30:g k43:g k33:g k79:g k8 k52:g k38:g k37:g k46:g k10:g k47:g k44 k27 k50:g k82 k81:g 0s29 k78 k55 k58 0s30 0l6 0h1 k53:g k59 k61 k80:g k5:v k11 k63 0j4 0l7 k39:g 0s31 k48:g 0s32 0h8:s k35 0s20 0j5 0s33 k60 k64 0s34 0s35 0l8 0l9 0j6 0l10 k68 0s36 k9:g 0l11 k57 k76 0s25 0j7 0s37 0h6 k67 0s38 k56 0l12 k65 k74 0l13 0s39 k66 0j8 k91 0l14 0s40 0l15 0s41 k69 0s42 0s44 0j9 0l16 0s43 0l17 0j10 k77 0h10:s 0h14:s 0h11:s 0s45 k92 0s46 k22 k21 0s47
0l18 0n0 0n1 0h15:s 0n2 0l19 0j11 k90 0n3 0l20 0v0 0m0 0v2 0v1 0d0:s 0v6 0v4 0v3 0d1:s 0c0 0c6 0v5 0v7 0d2:s 0h7 0c5 0a0 0d4:s 0a1 0l22 0d5:s 0c16 0h13 0c7 0d3:g 0a2 0d6:s 0c4 k49:g 0a4 0d8:s 0c1 0a5 0d9:s 0c3 0a3 0d7:g 0a6 0a8 0d10:s 0l23 0c15 0l21 0d12:s 0c8 0a9 0d13:s 0a10 0h3 0a7 0a12 0a13 0c2 0e0 0d14:s 0a14 0d11:s 0c9 0d16:s 0a11 0d17:s 0a16 0a17 0c13 0b0 0c12 0e1 0d15:s 0a15 0c11 0b1 0c14 0d18:g 0a18 0c10 0e2 0p1 0b2 k75 0d19:g 0p2 0p0 0p4 0e3 u5:s 0b3 0p11 0a19 0b4 0p8 0g2 0p3 0p7 0g0 0g3 0p5 0b5 0g1 0p12 0p9 0b6 0g6 0p13 0p6 0p10 0q0 0q4 0q1 0q5 0g7 0q2 k70 0q6 u3:s 0q3 0h5 k83 0q7 0x2 0h9 0g4 0x3 0x0 0x1 0g5 0x5 0w0 0x4 0w2 0x6 0x7 0w1 1h0:s k72 0r0 k71 0w3 u4 0w4 k84 k87 0w5
k73 0r1 1y7 1h1 u2 1y0 k88 1h2:s 1h3 1y8 0L1 0r3 1y10 k89 1y1 k85 0r4 w6 1y3 1j0:v 0L2 0L0 0R1 0L3 1y5 0R2:s 0R0:s 0L5 0L6 0R3 1y11 0L7 0L4 k86 1y4 0H0 1l0 0R5 0D2 0D3 0R4 1y12 0D1 0R6:s 1l1 0R7:s 0D0 0C2:s 0C3 0C1:s 0H1 0D7 0D5 0C0:s 0D4 0r2:g 0X0 1y6 0C5:s 0D6 0C7 1y9 1y2 0C4:s 1y14 1y17 1y21 1y19 1y22 0C6 0X1
1y26 1j1:v 1y13 1y15 1y20 1y18 1y24 1y23 1y16 1s0 1s1 1l2 1A2 1y25 1A3 1A4 1A0 1A1 1y27 1A5 1A6 1l3 1B2 1B4 1A7 1B0 1B3 1B5 1B1 1s3 1B6 1A9 1A8 1s2 1B7 1A10 1j2 1A14 1A12 1B8 1B9 1B14 1s4 1l4 1B11 1B10 1A15 1A11 1A16 1l5 1B15 1A17 1A19 1A18 1B16 1B12 1A20 1B17 1A23 1A24 1A25 1B18 1B19 1A26 1B24 1B25 1j3 1A27 1B20 1s5 1A28 1B26 1B27 1B28 1A21 1l6 1h10 1A29 1l7 1A13 1A30 1h8 1h9 1j4 1B29 1A31 1A22 1B21 1A32 1B30 1B22 1B31 1B32 1B23 1A33 1l8 1A34 1B33 1A35 1B13 1B34 1h12:s 1A36 1l9 1B35 1h4 1j5:v 1B36 1A37 1A38 1l10 1A39 1B38 1B39 1A40 1B40 1h14 1s6 1B37:s 1B41
1n0 1n1 1h6:s 1n2 1h11:s 1l11 1n3 1v0 1v3 1c0 1c5 1c4 1c3 1c2 1v2 1v1 1v4 1c6 1c8 1v5 1a0 1a1 1d0 1h15 1d1 1a2 1a3 1h7 1h13 1d2 1c7 1c1 1c11 1c10 1e0 1d3 1a4 1a5 1c9 1c14 1d4 1e1 1c16 1c13 1c12 1d5 1a6 1c15 1a7 1p1 1e2 1p2 1d6:s 1e3 1d7:s 1p4 1a8 1a9 1b0 1p11 1p5 1p12 1b1 1p8 1p9 1p3 1b2 1p13 1p6 1p0 1p7 1p10 1h5 1q0 1q4 1q1 1q5 1g3 1g1 1g6 1g0 1g2 1q2 1q6 1q3 1q7 1g5 1g7 1x1 1x2 1x3 1x0 1x7 1w0 1w1 1g4 1x6 1w2 1x4 2h0:s 1x5 2h2:s 1r0 1w3 1w4 1w5
2h1:v 1r1 1r3 2y0 1r4 2j0:v 2y3 2y5 2y7 2y4 2y12 2y8 1L2 1L3 2h3 1R3 2y6 1L0 1R0 1R2:s 1L1 1R1:s 2l0 1L5 1H0 2y1 2y2 1L4 2y10 1L7 1L6 1R5:s 2y13 1R4 1R7:s 1D0 1C0:s 1R6 2y9 2l1 1D3 1D2 1D1 1H1 1C3:s 1C1 1D6 1D4 1C2:s 2j1 1C4:s 1D5 1X0 1C5:s 1C6 2y11 1r2:g 1D7 1C7 2y14 2y17 2y15 2y19 2l2 2y21 2y24 2y26 1X1
2s0 2l3 2y16 2y18 2j2:v 2y20 2A5 2A6 2A2 2A3 2A0 2s3 2s1 2A4 2A1 2y22 2y25 2y27 2y23 2A7 2s2 2B2 2B3 2B5 2B0 2B4 2B6 2B1 2A9 2h8:s 2A8 2B7 2A10 2B9 2s4 2s5 2B8 2s6 2h4:s 2l4 2B10 2A12 2A14 2A15 2l5 2B14 2A11 2j3 2A16 2A17 2B15 2A19 2A18 2B11 2B16 2B17 2l6 2A24 2A25 2B19 2A20 2A26 2B20 2A27 2B24 2B25 2l7 2B18 2B26 2B27 2A23 2A28 2A29 2B21 2A22 2B12 2B28 2j4 2A30 2B29 2A31 2A21 2B30 2h12 2B31 2B23 2A32 2A33 2A34 2B22 2B13 2A35 2B32 2B33 2B34 2h6 2B35 2A13 2A36 2h14 2A37 2A38 2B36 2l8 2A39 2B38 2B39 2l9 2A40 2B37:s 2j5 2B40 2B41
2n0 2h10:s 2h9:s 2n1 2n2 2n3 2l10 2v0 2h11:s 2h13 2c0 2c8 2c1 2h7 2h15 2v3 2v1 2v2 2v5 2c5 2c9 2c7 2c2 2c6 2v4 2a0 2a1 2c4 2d0 2l11 2h5 2d1 2c3 2a2 2c12 2c10 2a3 2d2 2e0 2d3 2a4 2a5 2c15 2d4 2e1 2d5 2c16 2c14 2c11 2a6 2c13 2e2 2a7 2e3 2p1 2p2 2d6:s 2a8 2d7:s 2p8 2p11 2a9 2b0 2p9 2p3 2b1 2p12 2p4 2p0 2p5 2b2 2p10 2p13 2p6 2q0 2p7 2g0 2q4 2q1 2q5 2q2 2q6 2g3 2g1 2q3 2g2 2q7 2x2 2x1 2x3 2g4 2x0 2g5 2x5 2g6 2w0 2w1 2g7 2x6 2w2 2L3 2x4 2x7 2L0 2L2 2L1 2w3 2w4 2r0 2w5
2r1 2R3:s o5 2R2:s 2r2 2R0 2R1 2L4 o6 2L6 2H0 o7:s o4 2L7 2L5 2R4 2R7:s 2D1 2C1:s 2R6 2R5 2D3 2C3 o8 o0 2D2 2C2:s o2 2D0 2C0:s 2H1 2D7 o3 2C7:s 2D6 2D5 2C5:s 2X0 2C6 2D4 2Y1:s 2Y0 o1:s 2C4 2Y2 2Y3 2X1 2Y6 2Y5 2Y4 2Y7 2Y9 2Y10 2Y8:s 2Y11 z0
"""

SCRATCH = {}
_NEEDS = []


def _sb(name, n, dtype):
    SCRATCH[name] = ("sbuf", [128, n], dtype)


for _t in range(R + 1):
    _sb("X%d" % _t, 4 * C, "bfloat16")
    _sb("Q%d" % _t, C, "float8_e4m3fn_x4")
    _sb("S%d" % _t, C, "uint8")
for _t in range(R):
    _sb("LQ%d" % _t, K, "float8_e4m3fn_x4")
    _sb("LS%d" % _t, K, "uint8")
for _n, _w in (("U", 512), ("E", 2048), ("H", 1024), ("Xh", 4 * XW), ("V", 1024), ("zer", C), ("junk", 14 * C), ("gtb", C + 2),
               ("geb", C), ("bnd", C), ("cnt", CO + C + 1), ("one", C), ("z", C), ("jk", 16 * WIN), ("al", C), ("M", (KB + 1) * ROW),
               ("Md", KB * C)):
    _sb(_n, _w, "bfloat16")
for _n, _s, _w in (("QU", "SU", 128), ("QR", "SR", 128), ("QA", "SA", 128), ("QB", "SB", 128), ("WL", "WSL", 512), ("WQ", "WS", 512),
                   ("QE", "SE", 512), ("QH", "SH", K)):
    _sb(_n, _w, "float8_e4m3fn_x4")
    _sb(_s, _w, "uint8")
for _n, _w in (("iot", ROW), ("t16", 48), ("yy", K), ("K1", C), ("Pl", C), ("D", 2 * C), ("scJ", (KB + 1) * C), ("scP", 2 * K), ("Ng", C),
               ("Gr", K), ("scB", K), ("rows", (KB + 1) * ROW),
               ("prow", ROW), ("pout", C), ("pe", 2 * K), ("Br", K), ("ysb", C), ("sm", 32), ("F", 2 * 288), ("Tt", 2 * 132), ("Tb", 2 * 5 * 68),
               ("o", 2 * 10 * 100), ("Dt", 2 * 3 * 34), ("G2t", 98), ("Tat", 34), ("Sgt", 2 * 34), ("cap", 4 * 96), ("nC", 64), ("sg", 2 * 8),
               ("one32", 34), ("l1", 32), ("l2", 32), ("l3", 3 * 32), ("tmp", 8 * 34), ("TB", 3 * 33), ("TM", 2 * 99), ("f", 2 * 16),
               ("m1", 16), ("w0", 1700), ("c0", 700), ("mk", 3 * 48), ("mo", 3 * 48), ("Kc", 8), ("ec", 16), ("e2", 16), ("nb", 16), ("et", 16)):
    _sb(_n, _w, "float32")
for _n, _w in (("LJ", (KB + 1) * 32), ("Lb", 16), ("La", 16), ("el", 16), ("pel", 32), ("offU", 24), ("Lr", 32)):
    _sb(_n, _w, "uint16")
for _n, _w in (("pt", 32), ("pi", 4), ("oi", 24)):
    _sb(_n, _w, "int32")
for _b in range(8):
    SCRATCH["P%d" % _b] = ("psum", [128, 512], "float32")

SEMAPHORES = (["c%d" % i for i in range(NSEM)] + ["d%d" % i for i in range(NDSEM)] + ["sent", "warr"]
              + ["arr%d%d" % (t, h) for t in range(R) for h in range(2)])


def v(name, a=0, b=None, s=1):
    return (name, a, SCRATCH[name][1][1] if b is None else b, s)


def col(name, j):
    return (name, j, j + 1, 1)


def ind(win, off):
    return ("*", win, off)


def _touched(xs):
    out = []
    for x in xs:
        if isinstance(x, tuple):
            if x[0] == "*":
                out += _touched(x[1:])
            else:
                out.append((x[0], -1 if x[0][0] == "P" and len(x[0]) == 2 and x[0] != "Pl" else sum(1 << c for c in range(*x[1:]))))
    return out


def _needs(ops):
    out, past = [], {}
    for i, o in enumerate(ops):
        out.append(sorted({j for w in (0, 1) for a, m in o[3 + w] for j, n, x in past.get(a, ())
                           if m & n and (w or x or m == -1 and not o[1] == ops[j][1] == "s")}))
        for w in (0, 1):
            for a, m in o[3 + w]:
                past.setdefault(a, []).append((i, m, w))
    return out


def _emit(g, T, ops):
    queues = {"v": g.vector, "s": g.scalar, "t": g.tensor, "y": g.sync, "g": g}
    if not _NEEDS:
        _NEEDS.extend(_needs(ops))
    needs, at = _NEEDS, {o[0]: i for i, o in enumerate(ops)}
    plan = [(at[w.split(":")[0]], w.split(":")[-1]) for w in ORDER.split()] or [(i, "") for i in range(len(ops))]
    plan = [(i, q if q in queues else ops[i][1][0]) for i, q in plan]
    assert sorted(i for i, q in plan) == list(range(len(ops)))
    pos = {i: k for k, (i, q) in enumerate(plan)}
    known, seen, waits, needed = {}, {q: set() for q in queues}, {}, set()
    for i, q in plan:
        waits[i] = []
        for j in sorted(needs[i], key=lambda j: -pos[j]):
            assert pos[j] < pos[i]
            if j not in seen[q] and ops[j][6] != "remote":
                waits[i].append(j)
                seen[q] |= known[j] | {j}
        known[i] = set(seen[q])
        needed.update(waits[i])
    last, count, mark = {}, {}, {}
    for i, q in plan:
        for j in waits[i]:
            queues[q].wait_ge(T.sem[mark[j][0]], mark[j][1])
        for name, n in ops[i][5]:
            queues[q].wait_ge(T.sem[name], n)
        ins = ops[i][2](q)
        if i in needed:
            dma = ops[i][6]
            pool = ["d%d" % k for k in range(NDSEM)] if dma else ["c%d" % k for k in range(NSEM)]
            name = [s for s in pool if s not in last or last[s] in known[i]][0]
            step = 16 if dma else 1
            last[name] = i
            count[name] = count.get(name, 0) + step
            mark[i] = (name, count[name])
            ins.then_inc(T.sem[name], step)


def program(g, core, T, topo):
    rank, n = T.rank_of(core), len(T.cores)
    nxt, prv = T.cores[(rank + 1) % n], T.cores[(rank - 1) % n]
    assert topo.may_write(core, nxt)
    rid, pid = topo.addr(nxt)[0], topo.addr(nxt)[1]
    mask, n_out, n_in = topo.mask(core, nxt), len(topo.engines(core, nxt)), len(topo.engines(prv, core))
    ops, sent, pre = [], [0], ["k", {}]
    V, S = g.vector, g.scalar
    u8, u32 = dt.uint8, dt.uint32

    def ap(x):
        if not isinstance(x, tuple):
            return x
        if x[0] == "*":
            return ap(x[1]).indirect(ap(x[2]))
        return T[x[0]][:, x[1]:(None if x[2] < 0 else x[2]):x[3]]

    def named(s):
        pre[0] = s

    def op(qs, fn, rd, wr, ext=(), dma=False):
        k = pre[1][pre[0]] = pre[1].get(pre[0], -1) + 1
        ops.append((pre[0] + str(k), qs, fn, _touched(rd), _touched(wr), ext, dma))

    def ts(out, in0, s1, op0, s2=None, op1=None):
        tail = () if op1 is None else (op1,)
        op("v", lambda q: V.tensor_scalar(ap(out), ap(in0), ap(s1), ap(s2), op0, *tail), [in0, s1, s2], [out])

    def affine(out, in_, scale, bias):
        op("vs", lambda q: S.activation(ap(out), ap(in_), AF.Identity, bias=ap(bias), scale=ap(scale)) if q == "s" else
           V.tensor_scalar(ap(out), ap(in_), ap(scale), ap(bias), A.mult, A.add), [in_, scale, bias], [out])

    def tt(out, a, b, o):
        op("v", lambda q: V.tensor_tensor(ap(out), ap(a), ap(b), o), [a, b], [out])

    def scan(out, d0, d1, init, op0, op1):
        op("v", lambda q: V.tensor_tensor_scan(ap(out), ap(d0), ap(d1), ap(init), op0, op1), [d0, d1, init], [out])

    def red(out, in_, o):
        op("v", lambda q: V.tensor_reduce(ap(out), ap(in_), AxisListType.X, o), [in_], [out])

    def turn(out, in_):
        op("v", lambda q: V.transpose(ap(out), ap(in_)), [in_], [out])

    def cp(out, in_, qs="v", scale=None):
        def fn(q):
            if q == "g":
                return g.affine_select(ap(out), ap(in_), [[0, len(range(*out[1:]))]], A.is_ge, 0.0, 0, 0)
            if q == "s":
                return S.activation(ap(out), ap(in_), AF.Copy, **({} if scale is None else {"scale": scale}))
            return V.tensor_copy(ap(out), ap(in_)) if scale is None else V.tensor_scalar(ap(out), ap(in_), scale, None, A.mult)
        op(qs, fn, [in_], [out])

    def iota(out, pattern, base, cm=0):
        flag = {} if SCRATCH[out[0]][2] == "int32" else {"allow_small_or_imprecise_dtypes": True}
        op("g", lambda q: g.iota(ap(out), pattern, base, cm, **flag), [], [out])

    def ramp(out, base, step=1):
        n = out[2] - out[1]

        def fn(q):
            if q == "g":
                return g.iota(ap(out), [[step, n]], base, 0, allow_small_or_imprecise_dtypes=True)
            if q == "s":
                return S.activation(ap(out), T.iot[:, 0:n], AF.Identity, bias=float(base), scale=float(step))
            return V.tensor_scalar(ap(out), T.iot[:, 0:n], float(step), float(base), A.mult, A.add)
        op("svg", fn, [v("iot")], [out])

    def fill(out, c):
        def fn(q):
            if q == "g":
                return g.iota(ap(out), [[0, len(range(*out[1:]))]], int(c), 0, allow_small_or_imprecise_dtypes=True)
            return V.memset(ap(out), c)
        op("vg" if c == int(c) and out[3] == 1 else "v", fn, [], [out])

    def act(out, in_, func, bias=0.0, scale=1.0, acc=None):
        op("s", lambda q: S.activation(ap(out), ap(in_), func, bias=ap(bias), scale=ap(scale), accum_out=ap(acc)), [in_, bias, scale], [out, acc])

    def planes(q):
        return ({"Q": "S", "L": "LS", "W": "WS"}[q[0][0]] + q[0][(1 if q[0][0] == "Q" else 2):],) + q[1:]

    def quant(q, x):
        op("v", lambda _: V.quantize_mx(ap(q), ap(planes(q)), ap(x)), [x], [q, planes(q)])

    def mm(bank, w, x, ext=()):
        op("t", lambda _: g.tensor.matmul_mx(T[bank][:, 0:x[2] - x[1]], ap(w), ap(planes(w)), ap(x), ap(planes(x)), True, True),
           [w, planes(w), x, planes(x)], [v(bank)], ext)

    def dma(qs, out, in_, rd, wr):
        op(qs, lambda q: (g.sync if q == "y" else S).dma_start(out, in_), rd, wr, (), True)

    def store(out, in_, rd):
        dma("ys", out, in_, [rd], [("out", len(ops), len(ops) + 1, 1)])

    def send(dst, src, sem, codes):
        def fn(q):
            a, b = (ap(dst).bitcast(u8), ap(src).bitcast(u8)) if codes else (ap(dst), ap(src))
            return g.remote_dma(a, b, T.sem[sem], T.sem.sent, pid, rid, mask)
        op("g", fn, [src], [(sem, len(ops), len(ops) + 1, 1)], (), "remote")
        sent[0] += n_out

    r_, hf, off = col("sm", 0), col("sm", 2), col("sm", 3)
    off1, off2, p32 = col("sm", 10), col("sm", 11), col("sm", 1)

    def lst(k, a, b):
        return v("LJ", 32 * k + a // 16, 32 * k + b // 16)

    def to_list(out, row, a, b, sc, at):
        scan(v(sc, at + a, at + b), v("K1", a, b), row, 0.0, A.add, A.min)
        if out:
            ts(out, v(sc, at + a + 15, at + b, 16), off, A.add)

    def jumps(t, w, row0):
        for k in range(1, KB + 1):
            src = row0 if k == 1 else ("rows", ROW * (k - 1))
            for h in range(NJ[t]):
                a, b = max(h * w // NJ[t], 2 ** KB if k == KB else 0), (h + 1) * w // NJ[t]
                named("%dj" % t)
                cp(v("rows", ROW * k + PAD + a, ROW * k + PAD + b), ind(v(src[0], src[1], src[1] + PAD + b), lst(k - 1, a, b)), "sv")
                named("%dl" % t)
                to_list(lst(k, a, b), v("rows", ROW * k + PAD + a, ROW * k + PAD + b), a, b, "scJ", C * k)

    def halve(t, a, b):
        named("%dh" % t)
        for e in range(4):
            cp(v("Xh", XW * e + CO + a, XW * e + CO + b), v("X%d" % t, 4 * a + e, 4 * b, 4), "vs", 0.5)
            cp(v("Xh", XW * e + C - 1 - a, XW * e + C - 1 - b, -1), v("Xh", XW * e + CO + a, XW * e + CO + b), "gvs")

    def early(t, n=0):
        named("%dy" % t)
        for x in range(2):
            bank = "P%d" % (6 + x)
            mm(bank, v("Q" + "AB"[x]), v("Q%d" % t, n * K, K + n * HALF))
            for j in range(3):
                f, at = col("f", 16 * x + 8 + j), 96 * x + 32 * j
                if n:
                    f, lo = col("f", 16 * x + 11 + j), C * (12 + x) + HALF * j
                    act(v("junk", lo, lo + HALF), v(bank, 0, HALF), AF.Sign, col("m1", j), col("m1", 3 + j), f)
                    ts(v("cap", 192 + at, 192 + at + 32), v("cap", at, at + 32), f, A.subtract)
                    continue
                act(v("jk", K * (3 * x + j), K * (3 * x + j + 1)), v(bank, 0, K), AF.Sign, col("m1", j), col("m1", 3 + j), f)
                ts(v("cap", at, at + 32), v("Dt", 0, 32), col("m1", 6 + j), A.add, f, A.subtract)

    named("i")
    dma("y", T.pt[:], T.ptr[:], [], [v("pt")])
    dma("s", T.U[:], T.u[:], [], [v("U")])
    dma("y", T.X0[:, 0:1024], T.x[:, 0:1024], [], [v("X0", 0, 1024)])
    dma("s", T.X0[:, 1024:2048], T.x[:, 1024:2048], [], [v("X0", 1024, 2048)])
    dma("y", T.WL[:].bitcast(u8), T.wc[:], [v("X0")], [v("WL")])
    dma("y", T.WSL[:], T.ws[:], [v("X0")], [v("WSL")])

    named("k")
    iota(col("pi", 0), [[1, 1]], 0, 1)
    iota(v("t16", 0, 16), [[1, 16]], 0)
    iota(v("iot"), [[1, ROW]], 0)
    iota(v("oi", 0, 8), [[16, 8]], 0)
    iota(v("oi", 8, 24), [[16, 2], [32, 4], [0, 2]], 0)
    ramp(v("Pl"), -K - int(UNIT))
    iota(v("l1"), [[16, 2], [0, 16]], 0)
    iota(v("l2"), [[16, 32]], PAD)
    iota(v("tmp", 68, 108), [[0, 5], [1, 8]], 8)
    ramp(v("prow", PAD + K, ROW), PAD)
    ramp(v("pout", K, C), 0)
    ramp(v("Ng"), -K - PAD - 1, -1)
    for j, m in enumerate((15, 31, 16)):
        ts(col("pi", j + 1), col("pi", 0), m, A.bitwise_and)
    cp(v("sm", 0, 3), v("pi", 1, 4))
    ts(v("t16", 16, 32), v("t16", 0, 16), r_, A.is_equal, BIG, A.mult)
    ts(v("t16", 32, 48), v("t16", 16, 32), -HOLD, A.add)
    ts(v("Lr"), v("l1"), 0.0, A.mult, r_, A.add)
    cp(v("K1"), ind(v("t16", 32, 48), v("Lr")), "sv")
    ts(off, r_, -HOLD, A.mult, 15 * HOLD, A.add)
    ts(off1, off, float(K + CO), A.add)
    ts(off2, off, K + CO + 1.0, A.add)
    ts(v("l2"), v("l2"), r_, A.add)
    for k in range(1, KB):
        fill(v("rows", ROW * k, ROW * k + PAD), 0.0)
    fill(v("rows", 0, PAD), 0.0)
    fill(v("prow", 0, PAD), 0.0)
    named("p")
    ts(v("l3", 0, 32), v("pt"), float(PAD), A.add)
    tt(v("l3", 32, 64), v("l3", 0, 32), v("l2"), A.not_equal)
    tt(v("l3", 64, 96), v("l3", 0, 32), v("l3", 32, 64), A.mult)
    cp(lst(0, 0, C), v("l3", 64, 96))
    for a in (0, K):
        cp(v("rows", PAD + a, PAD + a + K), ind(v("iot"), lst(0, a, a + K)), "sv")
    jumps(0, C, ("rows", 0))
    named("k")
    fill(v("one"), 1.0)
    fill(v("zer"), 0.0)
    for nm in ("G2t", "Tat", "Sgt", "one32"):
        fill(v(nm), 1.0)
    for nm in ("Tt", "Tb", "Dt"):
        fill(v(nm), 0.0)
    fill(v("gtb", C, C + 2), 0.0)
    fill(col("cnt", CO), 0.0)
    fill(v("cnt", 0, CO), -C * UNIT)
    for e in range(4):
        fill(v("Xh", XW * e + C, XW * e + CO), 0.0)
    for k in range(KB + 1):
        fill(v("M", ROW * k, ROW * k + PAD), -K - UNIT)
    fill(col("Tat", 32), -1.5)
    ts(col("sm", 6), hf, 1 / 16, A.mult)
    ts(col("sm", 7), col("sm", 6), -1.0, A.mult, 1.0, A.add)
    ts(col("sm", 8), p32, 16.0, A.is_equal, 2.0, A.mult)
    ts(col("sm", 12), p32, 0.0, A.add)
    ts(col("sm", 13), hf, -2.0, A.mult, 32.0, A.add)
    ts(col("sm", 13), col("sm", 13), r_, A.add)
    ts(col("sm", 14), p32, 16.0, A.add)
    fill(col("m1", 3), -1.0)
    ts(col("m1", 4), col("sm", 6), 2.0, A.mult, -1.0, A.add)
    fill(col("m1", 5), 1.0)
    ts(v("m1", 6, 9), v("m1", 3, 6), -1.5, A.mult)
    for j in range(3):
        ts(v("mk", 48 * j, 48 * j + 48), v("iot", 0, 48), col("sm", 12 + j), A.is_lt, 16.0, A.mult)
    ts(v("mk"), v("mk"), 1.0, A.max)
    for j in range(3):
        scan(v("mo", 48 * j, 48 * j + 48), v("mk", 48 * j, 48 * j + 48), v("zer", 0, 48), 2.0 ** -100, A.mult, A.add)
    cp(v("m1", 0, 3), v("mo", 47, 144, 48))
    unit = 2.0 ** -23
    for j, step in enumerate((1056, 32)):
        ts(col("Kc", j), p32, 1.0, A.add, step * unit, A.mult)
    ts(col("Kc", 2), p32, 0.5, A.add, unit, A.mult)
    ts(col("Kc", 6), p32, 1.0, A.add, 33 * 1056 * unit, A.mult)
    for j in range(5):
        fill(v("TB", 66 + 8 * j, min(74 + 8 * j, 99)), 2.0 ** j)
    tt(v("tmp", 238, 271), v("TB", 66, 99), v("tmp", 68, 101), A.mult)
    ts(v("TB", 33, 66), v("tmp", 238, 271), 0.125, A.mult)
    ts(v("tmp", 170, 203), v("TB", 66, 99), col("Kc", 6), A.mult)
    tt(v("TB", 0, 33), v("tmp", 170, 203), v("TB", 33, 66), A.add)
    ts(v("tmp", 110, 142), v("iot", 0, 32), p32, A.is_equal)
    tt(v("tmp", 204, 236), v("tmp", 110, 142), v("TB", 34, 66), A.mult)
    red(col("G2t", 96), v("tmp", 204, 236), A.max)
    ts(v("nb"), v("l2", 0, 16), 2 * UNIT, A.mult, (1 - 2 * PAD) * UNIT, A.add)
    ts(v("tmp", 0, 16), v("t16", 0, 16), 16.0, A.mult, float(WIN), A.add)
    ts(v("et"), v("tmp", 0, 16), off, A.subtract)
    named("b")

    def c0(a, b=None, s=1):
        return v("c0", a, a + 1 if b is None else b, s)
    iota(c0(300, 334), [[0, 17], [-2, 2]], 4)
    iota(c0(334, 368), [[0, 17], [1, 2]], 2)
    iota(c0(368, 402), [[0, 17], [1, 2]], 3)
    fill(v("w0", 0, 520), 0.0)
    fill(c0(200, 268), 1.0)
    ts(c0(0), r_, 7.5, A.is_gt, 2.0, A.mult)
    ts(c0(3), r_, 8.0, A.not_equal, -BIG, A.mult)
    ts(c0(4), c0(0), -4.0, A.mult, r_, A.add)
    for j, step in enumerate((78608, 4624, 272, 16)):
        ts(c0(8 + j), r_, 1.0, A.add, step * unit, A.mult)
    ts(c0(12), r_, 0.5, A.add, unit, A.mult)
    ts(c0(13), r_, 1.0, A.add, unit, A.mult)
    ts(c0(14), r_, 1.0, A.add, 17 * 78608 * unit, A.mult)
    ts(c0(1), c0(0), -1.0, A.add)
    ts(c0(2), c0(0), -1.5, A.mult, 1.5, A.add)
    ts(c0(16, 24), v("t16", 0, 8), c0(4), A.is_le, 2.0 ** 25, A.mult)
    ts(c0(24, 32), c0(16, 24), 1.0, A.max)
    scan(c0(32, 40), c0(24, 32), v("zer", 0, 8), 2.0 ** -125, A.mult, A.add)
    ts(c0(268, 300), v("l1"), hf, A.not_equal, -BIG, A.mult)
    ts(c0(64, 96), c0(268, 300), c0(2), A.add)
    ts(c0(96, 128), c0(268, 300), c0(2), A.add, c0(3), A.add)
    fill(c0(300, 317, 16), 0.0)
    scan(c0(402, 435), c0(300, 333), v("one32", 0, 33), 1.0, A.mult, A.max)
    ts(c0(436, 468), v("l1"), hf, A.is_equal)
    fill(c0(468), 1.0)
    tt(c0(666, 699), c0(402, 435), c0(436, 469), A.mult)
    tt(c0(470, 503), c0(666, 699), c0(334, 367), A.mult)
    ts(c0(633, 666), c0(470, 503), 0.5, A.mult)
    ts(c0(504, 537), c0(666, 699), c0(14), A.mult)
    tt(c0(600, 633), c0(504, 537), c0(633, 666), A.add)
    ts(c0(538, 570), v("iot", 0, 32), p32, A.is_equal)
    tt(c0(402, 434), c0(666, 698), c0(368, 400), A.mult)
    tt(c0(436, 468), c0(538, 570), c0(402, 434), A.mult)
    red(c0(232), c0(436, 468), A.max)
    named("u")
    cp(v("offU"), v("oi"))
    quant(v("QU"), v("U"))
    for j, nm in ((1, "A"), (2, "B"), (0, "R")):
        off_u = v("offU", 8 * j, 8 * j + 8)
        op("v", lambda q, nm=nm, o=off_u: V.tensor_copy(T["Q" + nm][:].bitcast(u32), T.QU[:].bitcast(u32).indirect(ap(o))), [v("QU"), off_u], [v("Q" + nm)])
        cp(v("S" + nm), ind(v("SU"), off_u), "vs")
    quant(v("Q0", 0, K), v("X0", 0, 1024))
    named("0y")
    mm("P7", v("QR"), v("Q0", 0, K))
    act(v("jk", 0, K), v("P7", 0, K), AF.Sign, c0(39), c0(1), col("f", 8))
    ts(v("c0", 128, 192), v("c0", 64, 128), col("f", 8), A.subtract)
    named("u")
    quant(v("Q0", K, C), v("X0", 1024, 2048))
    halve(0, 0, K)
    halve(0, K, C)
    named("w")
    for b in range(4):
        op("g", lambda q, b=b: g.affine_select(T.E[:, C * b:C * b + C], T.one[:], [[1, C]], A.is_equal, 0.0, -b, -4), [v("one")], [v("E", C * b, C * b + C)])
    send(v("WQ"), v("WL"), "warr", True)
    send(v("WS"), v("WSL"), "warr", False)
    quant(v("QE"), v("E"))

    def select(t, a):
        named("%ds" % t)
        for x in range(2):
            mm("P%d" % (2 + x), v("Q" + "AB"[x]), v("Q%d" % t, a, C))
        for x in range(4):
            mm("P%d" % (0, 1, 4, 5)[x], v("Q" + "AB"[x % 2]), v("Q%d" % t))
        mm("P6", v("QR"), v("Q%d" % t))
        for x in range(2):
            named("%d%s" % (t, "AB"[x]))

            def oc(s, j):
                return col("o", 1000 * x + 100 * s + j)

            def osl(s, k):
                return v("o", 1000 * x + 100 * s, 1000 * x + 100 * s + k)

            def sg(j):
                return col("sg", 8 * x + j)
            tau, nc, row, f0, t0 = oc(0, 31), v("nC", 32 * x, 32 * x + 32), v("P%d" % x), 288 * x, 132 * x

            def step(s, src, bias, scale, cmp, m):
                f, tb = col("f", 16 * x + s + 1), 340 * x + 68 * (s - 2)
                act(v("junk", C * (6 * x + s - 1), C * (6 * x + s)), src, AF.Sign, bias, scale, f)
                ts(v("F", f0 + 64 + 32 * s, f0 + 96 + 32 * s), nc, f, cmp, m, A.mult)
                turn(v("Tb", tb, tb + 32), v("F", f0 + 64 + 32 * s, f0 + 96 + 32 * s))
                return tb

            for j in range(3):
                f, at = col("f", 16 * x + j), 192 + 96 * x + 32 * j
                act(v("jk", K * (3 * x + j), K * (3 * x + j) + C - a), v("P%d" % (2 + x), 0, C - a), AF.Sign, col("m1", j), col("m1", 3 + j), f)
                ts(v("F", f0 + 32 * j, f0 + 32 * j + 32), v("cap", at, at + 32), f, A.is_ge, col("m1", j), A.mult)
                if j == 1:
                    ts(v("F", f0 + 96, f0 + 128), v("cap", at, at + 32), f, A.is_ge, col("sm", 8), A.mult)
            turn(v("Tt", t0, t0 + 128), v("F", f0, f0 + 128))
            scan(osl(0, 33), v("Tt", t0 + 96, t0 + 129), v("Tat", 0, 33), -1.0, A.add, A.mult)
            scan(osl(1, 97), v("Tt", t0, t0 + 97), v("G2t", 0, 97), 0.0, A.max, A.mult)
            ts(nc, v("Dt", 0, 32), oc(0, 32), A.add)
            ts(v("TM", 99 * x, 99 * x + 99), v("TB"), oc(1, 95), A.mult)
            ts(sg(0), tau, col("sm", 7 - x), A.mult)
            ts(col("Sgt", 34 * x + 32), sg(0), -1.0, A.mult)
            tb = step(2, row, oc(1, 96), tau, A.is_lt, -HUGE)
            for j, s in enumerate((2, 7, 8)):
                m = 99 * x + 33 * j
                scan(v("o", 1000 * x + 100 * s + 33, 1000 * x + 100 * s + 1, -1), v("Tb", tb + 31, tb - 1, -1), v("TM", m + 31, m - 1, -1), col("TM", m + 32), A.add, A.max)
            w, lo, dt_ = oc(8, 2), oc(7, 2), 102 * x
            ts(v("Dt", dt_ + 33, dt_ + 102, 34), v("Kc", 0, 3), w, A.mult)
            ts(sg(1), w, unit, A.mult)
            ts(col("Dt", dt_ + 100), lo, -1.0, A.mult)
            affine(v("D", C * x, C * x + C), v("P%d" % (4 + x)), tau, lo)
            for s in range(3, 6):
                bias, base = (oc(2, 2), lo) if s == 3 else (oc(s - 1, 33), oc(s - 1, 31))
                tb = step(s, row, bias, tau, A.is_ge, bias)
                scan(osl(s, 34), v("Tb", tb, tb + 34), v("Dt", dt_ + 34 * (s - 3), dt_ + 34 * (s - 2)), base, A.max, A.add)
            if x:
                ts(sg(2), oc(5, 31), sg(0), A.mult, col("sg", 2), A.add)
                affine(v("z"), v("P6"), 1.0, sg(2))
            else:
                ts(sg(2), oc(5, 31), sg(0), A.mult)
            tb = step(6, v("D", C * x, C * x + C), oc(5, 33), 1.0, A.is_ge, sg(1))
            if x:
                scan(osl(6, 34), v("Tb", tb, tb + 34), v("Sgt", 34, 68), 0.0, A.add, A.mult)
            else:
                scan(v("Tb", 340 + tb + 65, 340 + tb + 32, -1), v("Tb", tb, tb + 33), v("Sgt", 0, 33), 0.0, A.add, A.mult)

    def select0():
        named("0s")
        mm("P3", v("QR"), v("Q0", K, C))
        mm("P0", v("QR"), v("Q0"))
        mm("P1", v("QR"), v("Q0"))

        def w0(a, b=None, s=1):
            return v("w0", a, a + 1 if b is None else b, s)

        def oc(s, j):
            return w0(520 + 34 * s + j)

        def osl(s, k):
            return w0(520 + 34 * s, 520 + 34 * s + k)
        tau, msk, tt0, dt0, f0, nc, tm = oc(0, 31), c0(268, 300), 272, 340, 950, 1250, 1320

        def step(s, src, bias, scale, cap, cmp, m):
            at = f0 + 32 * s if s > 1 else f0
            act(v("junk", C * (s - 1), C * (s - 1) + src[2]), src, AF.Sign, bias, scale, col("f", s - 1))
            ts(w0(at, at + 32), cap, col("f", s - 1), cmp, m, A.mult)
            if s > 1:
                turn(w0(34 * (s - 1), 34 * (s - 1) + 32), w0(at, at + 32))

        step(1, v("P3", 0, K), c0(39), c0(1), c0(128, 160), A.is_ge, c0(39))
        ts(w0(f0 + 32, f0 + 64), c0(160, 192), col("f", 0), A.is_ge, 2.0, A.mult)
        turn(w0(tt0, tt0 + 64), w0(f0, f0 + 64))
        scan(osl(0, 33), w0(tt0 + 32, tt0 + 65), v("Tat", 0, 33), -1.0, A.add, A.mult)
        scan(osl(1, 33), w0(tt0, tt0 + 33), c0(200, 233), 0.0, A.max, A.mult)
        ts(w0(nc + 32, nc + 64), msk, -1.0, A.mult, oc(0, 32), A.add)
        ts(w0(nc, nc + 32), msk, oc(0, 32), A.add)
        ts(w0(tm, tm + 99), c0(600, 699), oc(1, 31), A.mult)
        ts(c0(266), tau, -1.0, A.mult)
        step(2, v("P0"), oc(1, 32), tau, w0(nc + 32, nc + 64), A.is_lt, -HUGE)
        for j, s in enumerate((2, 9, 10)):
            scan(w0(520 + 34 * s + 33, 520 + 34 * s + 1, -1), w0(65, 33, -1), w0(tm + 33 * j + 31, tm + 33 * j - 1, -1), w0(tm + 33 * j + 32), A.add, A.max)
        w = oc(10, 2)
        ts(w0(dt0 + 33, dt0 + 170, 34), c0(8, 13), w, A.mult)
        ts(w0(1430), c0(13), w, A.mult)
        for s in range(3, 8):
            bias, base = (oc(2, 2), oc(9, 2)) if s == 3 else (oc(s - 1, 33), oc(s - 1, 31))
            step(s, v("P0"), bias, tau, w0(nc, nc + 32), A.is_ge, bias)
            scan(osl(s, 34), w0(34 * (s - 1), 34 * s), w0(dt0 + 34 * (s - 3), dt0 + 34 * (s - 2)), base, A.max, A.add)
            if s == 3:
                ts(w0(dt0 + 4 * 34 + 32), oc(3, 31), -1.0, A.mult)
                affine(v("D", 0, C), v("P1"), tau, oc(3, 31))
        ts(v("z"), v("D", 0, C), oc(7, 32), A.add, tau, A.mult)
        step(8, v("D", 0, C), oc(7, 33), 1.0, w0(nc, nc + 32), A.is_ge, w0(1430))
        scan(osl(8, 33), w0(34 * 7, 34 * 7 + 33), c0(234, 267), 0.0, A.max, A.mult)

    hs = [(HALF * h, HALF * h + HALF, 8 * h, 8 * h + 8) for h in range(2)]
    for t in range(R):
        Xn, Qn, Sn = "X%d" % (t + 1), "Q%d" % (t + 1), T["S%d" % (t + 1)]
        if t:
            select(t, K + HALF)
        else:
            select0()
        thr = col("o", 1000 + 600 + 33) if t else col("w0", 520 + 34 * 8 + 32)
        named("%dn" % t)
        ts(v("gtb", 0, C), v("z"), thr, A.is_gt, -UNIT, A.mult)
        ts(v("geb"), v("z"), thr, A.is_ge, UNIT, A.mult)
        scan(v("bnd", C - 1, -1, -1), v("gtb", C, 0, -1), v("zer"), UNIT * K, A.add, A.add)
        m = K if t == 0 else C
        scan(v("cnt", CO + 1, CO + 1 + m), v("geb", 0, m), v("bnd", 0, m), 0.0, A.add, A.min)
        if m < C:
            named("%dm" % t)
            scan(v("cnt", CO + 1 + m), v("geb", m), v("bnd", m), col("cnt", CO + m), A.add, A.min)
        w = C if t == 0 else K
        B, m = 2 ** KB, ROW * (KB - 1)
        pieces = [(h * w // NQ[t], (h + 1) * w // NQ[t]) for h in range(NQ[t])]
        named("%dv" % t)
        for a, b in pieces:
            scan(v("al", a, b), v("cnt", CO + a + 1, CO + b + 1), v("cnt", CO + a, CO + b), 0.0, A.max, A.subtract)
            scan(v("M", PAD + b - 1, PAD + a - 1, -1), v("Pl", b - 1, a - 1, -1), v("al", b - 1, a - 1, -1), BIG, A.min, A.add)
            if TWICE[t]:
                scan(v("Md", b - 1, a - 1, -1), v("Pl", b - 1, a - 1, -1), v("al", b - 1, a - 1, -1), BIG, A.min, A.add)
        for j in range(KB - 1):
            for a, b in pieces:
                named("%dd" % t)
                if j or not TWICE[t]:
                    cp(v("Md", C * j + a, C * j + b), v("M", ROW * j + PAD + a, ROW * j + PAD + b), "vsg")
                named("%da" % t)
                tt(v("M", ROW * (j + 1) + PAD + a, ROW * (j + 1) + PAD + b), ind(v("M", ROW * j, ROW * j + PAD + b), lst(j + 1, a, b)), v("Md", C * j + a, C * j + b), A.max)
        named("%db" % t)
        for a in range(B, w, B):
            tt(v("M", m + PAD + a, m + PAD + a + B), ind(v("M", m, m + PAD + a), lst(KB, a, a + B)), v("M", m + PAD + a, m + PAD + a + B), A.max)
        named("%dc" % t)
        scan(v("yy", K - 1, -1, -1), v("cnt", CO + C - 1, CO, -2), v("cnt", CO + C, CO, -2), BIG, A.min, A.add)
        for i in range(16):
            act(v("jk", WIN * i, WIN * i + WIN), v("yy", 8 * i, 8 * i + WIN), AF.Sign, col("nb", i), -1.0, col("ec", i))
        for h in range(2):
            a, b, c, d = hs[h]
            named("%de" % t)
            tt(v("e2", c, d), v("ec", c, d), v("et", c, d), A.add)
            ts(v("el", c, d), v("e2", c, d), off, A.add)
            named("%dp" % t)
            cp(v("Gr", a, b), ind(v("Ng"), v("el", c, d)), "sv")
            for j in range(2):
                src = (("rows" if t == 0 else "prow", 0), ("rows", ROW))[j]
                cp(v("pe", K * j + a, K * j + b), ind(v(src[0], src[1] + PAD, src[1] + ROW), v("el", c, d)), "sv")
                to_list(v("pel", 16 * j + c, 16 * j + d), v("pe", K * j + a, K * j + b), a, b, "scP", K * j)
            named("%dg" % t)
            for e in range(4):
                cp(v("V", K * e + a, K * e + b), ind(v("Xh", XW * e + CO, XW * e + XW), v("el", c, d)), "sv")
            named("%dq" % t)
            for j in range(2):
                tt(v("Br", a, b), ind(v("M", m, m + PAD + w), v("pel", 16 * j + c, 16 * j + d)), v("Br" if j else "Gr", a, b), A.max)
            to_list(None, v("Br", a, b), a, b, "scB", 0)
            ts(v("La", c, d), v("scB", a + 15, b, 16), off1, A.add)
            named("%dx" % t)
            for e in range(4):
                tt(v(Xn, 4 * a + e, 4 * b, 4), ind(v("Xh", XW * e, XW * e + XW), v("La", c, d)), v("V", K * e + a, K * e + b), A.add)
            named("%dw" % t)
            quant(v(Qn, a, b), v(Xn, 4 * a, 4 * b))
            send(v("LQ%d" % t, a, b), v(Qn, a, b), "arr%d%d" % (t, h), True)
            send(v("LS%d" % t, a, b), planes(v(Qn, a, b)), "arr%d%d" % (t, h), False)
        named("%dr" % t)
        ts(v("Lb"), v("scB", 15, K, 16), off2, A.add)
        if t < R - 1:
            act(v("prow", PAD, PAD + K), ind(v("cnt"), v("Lb")), AF.Relu, PAD - 1.0, 1 / UNIT)
            cp(v("rows", ROW + PAD + K, 2 * ROW), v("prow", PAD, PAD + K), "svg")
            to_list(lst(0, 0, K), v("prow", PAD, PAD + K), 0, K, "scJ", 0)
            jumps(t + 1, K, ("prow", 0))
            halve(t + 1, 0, K)
            early(t + 1)
        else:
            act(v("pe", 0, K), ind(v("cnt"), v("Lb")), AF.Abs, -1.0, 1 / UNIT)
            tt(v("pout", 0, K), v("pe", 0, K), v("iot", 0, K), A.min)
            named("o")
            store(T.oc[:, 0:1024], T[Qn][:, 0:K].bitcast(u8), v(Qn, 0, K))
            for k in range(4):
                store(T.osc[4 * k:4 * k + 4, 0:K], Sn[32 * k:32 * k + 4, 0:K], planes(v(Qn, 0, K)))
            mm("P0", v("QU"), v(Qn, 0, K))
            cp(v("ysb", 0, K), v("P0", 0, K), "vs")
            store(T.pl[:], T.pout[0:128:16, :], v("pout"))
            store(T.y[:, 0:K], T.ysb[:, 0:K], v("ysb", 0, K))

        def stage(kind, h):
            a, b = hs[h][0:2]
            banks = (("P6", "P7", "P0", "P1"), ("P2", "P3", "P4", "P5"))[h]
            named("%d%s" % (t, kind))
            if kind == "L":
                arr = "arr%d%d" % (t, h)
                for e in range(4):
                    mm("P%d" % (2 + e), v("WQ", 128 * e, 128 * e + 128), v("LQ%d" % t, a, b), (("warr", 2 * n_in), (arr, 2 * n_in)))
                    ops[-1][3].extend([(arr, -2), ("warr", -2)])
            elif kind == "R":
                for e in range(4):
                    out, src = v("H", 4 * a + e, 4 * b, 4), v("P%d" % (2 + e), 0, HALF)
                    op("vs", lambda q, out=out, src=src: S.activation(ap(out), ap(src), AF.Relu, scale=0.03125) if q == "s" else
                       V.tensor_scalar(ap(out), ap(src), 0.0, 0.03125, A.max, A.mult), [src], [out])
            elif kind == "H":
                quant(v("QH", a, b), v("H", 4 * a, 4 * b))
            elif kind == "D":
                for e in range(4):
                    mm(banks[e], v("QE", 128 * e, 128 * e + 128), v("QH", a, b))
            elif kind == "C":
                for e in range(4):
                    cp(v(Xn, 4 * (K + a) + e, 4 * (K + b), 4), v(banks[e], 0, HALF), "vs")
            elif kind == "X":
                quant(v(Qn, K + a, K + b), v(Xn, 4 * (K + a), 4 * (K + b)))
            elif t < R - 1:
                if h == 1:
                    halve(t + 1, K, C)
                else:
                    early(t + 1, 1)
            else:
                mm("P%d" % (6 + h), v("QU"), v(Qn, K + a, K + b))
                store(T.oc[:, 4 * (K + a):4 * (K + b)], T[Qn][:, K + a:K + b].bitcast(u8), v(Qn, K + a, K + b))
                if h == 1:
                    for k in range(4):
                        store(T.osc[4 * k:4 * k + 4, K:C], Sn[32 * k:32 * k + 4, K:C], planes(v(Qn, K, C)))
                cp(v("ysb", K + a, K + b), v("P%d" % (6 + h), 0, HALF), "vs")
                store(T.y[:, K + a:K + b], T.ysb[:, K + a:K + b], v("ysb", K + a, K + b))

        for name in "L0 R0 H0 L1 D0 R1 C0 H1 D1 X0 Y0 C1 X1 Y1".split():
            stage(name[0], int(name[1]))

    named("z")
    op("g", lambda q: None, [], [], (("sent", sent[0]),))
    ops[-1][3].extend([("out", -2)] + [(s, -2) for s in SEMAPHORES[-7:]])
    return ops


def rank_program(g, core, T, topo):
    if T.rank_of(core) is not None:
        _emit(g, T, program(g, core, T, topo))
